import numpy as np
import ml_dtypes


def mxq(x, axis, fmt="e4m3"):
    dtype, down = {"e4m3": (ml_dtypes.float8_e4m3fn, 7), "e5m2": (ml_dtypes.float8_e5m2, 14)}[fmt]
    v = np.moveaxis(np.asarray(x, np.float32).astype(ml_dtypes.bfloat16).astype(np.float64), axis, -1)
    blocks = v.reshape(v.shape[:-1] + (-1, 32))
    amax = np.abs(blocks).max(-1, keepdims=True)
    byte = np.maximum(np.where(amax > 0, np.frexp(amax)[1] - 1 + 127, 0) - down, 1)
    scale = np.exp2(byte - 127.0)
    codes = (blocks / scale).astype(np.float32).astype(dtype).astype(np.float64)
    return np.moveaxis((codes * scale).reshape(v.shape), -1, axis)


WIDE = False


def mx_kscale(k):
    if not WIDE:
        return np.ones(k)
    levels = np.array([10, -10, 5, -5, 0])
    if k % 512:
        return np.exp2(np.random.permutation(np.resize(levels, k // 32))).repeat(32)
    a = np.empty((k // 512, 16))
    for p in range(k // 512):
        a[p, :8] = np.random.permutation(np.resize(levels, 8))
        for g in range(8):
            far = levels[np.abs(levels - a[p, g]) >= 10]
            a[p, g + 8] = far[np.random.randint(len(far))]
    return np.exp2(a.ravel()).repeat(32)


def f64(x):
    return np.asarray(x).astype(np.float64)


def striped(idx):
    return np.tile(np.asarray(idx).reshape(-1, 16).T, (8, 1)).astype(np.uint16)


def unstriped(offs):
    return offs[:16].T.reshape(-1).astype(np.int64)


E2M1 = np.array([0.0, 0.5, 1.0, 1.5, 2.0, 3.0, 4.0, 6.0, -0.0, -0.5, -1.0, -1.5, -2.0, -3.0, -4.0, -6.0])


def pack_weight(w, fmt):
    k, n = w.shape
    w = f64(np.asarray(w, np.float32).astype(ml_dtypes.bfloat16)).reshape(k // 32, 32, n)
    amax = np.abs(w).max(1)
    if fmt == "e4m3":
        byte = np.frexp(amax)[1] - 1 + 127 - 7
    else:
        mant, ex = np.frexp(amax / 6.0)
        byte = np.where(mant > 0.5, ex, ex - 1) + 127
    byte = np.clip(np.where(amax > 0, byte, 1), 1, 254)
    scaled = (w * np.exp2(127.0 - byte)[:, None, :]).reshape(k, n).astype(np.float32)
    by_word = np.ascontiguousarray(scaled.reshape(k // 512, 128, 4, n).transpose(0, 1, 3, 2))
    if fmt == "e4m3":
        words = by_word.astype(ml_dtypes.float8_e4m3fn).view(np.uint8)
    else:
        c = by_word.astype(ml_dtypes.float4_e2m1fn).view(np.uint8) & 0xF
        words = (c[..., 0::2] | (c[..., 1::2] << 4)).reshape(k // 512, 128, 2 * n)
    return np.ascontiguousarray(words), np.ascontiguousarray(byte.astype(np.uint8).reshape(k // 512, 16, n))


def unpack_weight(words, scales, fmt):
    g, _, n = scales.shape
    words = np.ascontiguousarray(words).reshape(g, 128, n, -1)
    if fmt == "e4m3":
        vals = words.view(ml_dtypes.float8_e4m3fn).astype(np.float64)
    else:
        nib = np.empty((g, 128, n, 4), np.uint8)
        nib[..., 0::2] = words & 0xF
        nib[..., 1::2] = words >> 4
        vals = E2M1[nib]
    vals = vals * np.repeat(np.exp2(scales.astype(np.float64) - 127.0), 8, axis=1)[..., None]
    return vals.transpose(0, 1, 3, 2).reshape(g * 512, n)


B, N, T, D, DV, NQ = 2, 512, 2048, 1024, 256, 128


def setup_inputs():
    n = np.random.standard_normal
    seg = T // B
    idx = np.concatenate([b * seg + np.random.permutation(seg)[:N] for b in range(B)])
    s = mx_kscale(D)[:, None]
    u = np.ones(T)
    u[idx] = mx_kscale(B * N)
    r = np.random.uniform(0.5, 2.0, T)
    qp = [pack_weight(x, "e4m3") for x in n((B, D, NQ)) * s * (0.80 / np.sqrt(D))]
    k = n((D, T)) / s
    v = n((DV, T)) / (u * r)
    kp = pack_weight(k, "e2m1")
    return {
        "q_words": np.stack([x[0] for x in qp]),
        "q_scales": np.stack([x[1] for x in qp]),
        "k_words": np.ascontiguousarray(kp[0].reshape(D // 1024, 2, 128, T, 2).transpose(0, 2, 3, 1, 4)).reshape(D // 1024, 128, T, 4),
        "k_scales": kp[1],
        "vT": v.astype(np.float32),
        "vs": np.tile(u * r, (128, 1)).astype(np.float32),
        "kb": np.tile(n(T), (128, 1)).astype(np.float32),
        "offs": striped(idx),
    }


def reference(q_words, q_scales, k_words, k_scales, vT, vs, kb, offs):
    idx = unstriped(offs)
    k = unpack_weight(k_words.reshape(D // 1024, 128, T, 2, 2).transpose(0, 3, 1, 2, 4).reshape(D // 512, 128, 2 * T), k_scales, "e2m1")
    v = f64(vT)
    pick = lambda x: x[:, idx].reshape(x.shape[0], B, N).transpose(1, 0, 2)
    q = np.stack([unpack_weight(q_words[b], q_scales[b], "e4m3") for b in range(B)])
    score = q.transpose(0, 2, 1) @ pick(k)
    score = score + pick(f64(kb))[:, :1, :]
    p = 1.0 / (1.0 + np.exp(-score))
    w = p * pick(f64(vs))[:, :1, :]
    y = mxq(w, 2, "e4m3") @ mxq(pick(v).transpose(0, 2, 1), 1, "e4m3")
    y = y / 16.0
    return y

@@ -1,0 +1,234 @@
+from contextlib import ExitStack
+
+import concourse.mybir as mybir
+from concourse.masks import make_identity
+
+B, N, T, D, DV, NQ = 2, 512, 2048, 1024, 256, 128
+FLOPS = 2 * B * NQ * N * (D + DV)
+
+F32 = mybir.dt.float32
+BF16 = mybir.dt.bfloat16
+I32 = mybir.dt.int32
+U32 = mybir.dt.uint32
+U16 = mybir.dt.uint16
+U8 = mybir.dt.uint8
+FP8X4 = mybir.dt.float8_e4m3fn_x4
+FP4X4 = mybir.dt.float4_e2m1fn_x4
+ACT = mybir.ActivationFunctionType
+MULT = mybir.AluOpType.mult
+
+P = 128
+SEG = T // B
+COLS = N // 16
+PASSES = D // 512
+HALVES = DV // P
+
+
+def tile_attend_sigm_kb_segb2q128n512t2048_kernel(tc, q_words, q_scales, k_words, k_scales, vT, vs, kb, offs, out):
+    nc = tc.nc
+    with ExitStack() as ctx:
+        keep = ctx.enter_context(tc.tile_pool(name="keep", bufs=1))
+        stage = ctx.enter_context(tc.tile_pool(name="stage", bufs=2))
+        psum = ctx.enter_context(tc.psum_pool(name="psum", bufs=1))
+
+        offsets = keep.tile([P, B * COLS], U16, name="offsets")
+        nc.sync.dma_start(offsets[:], offs)
+
+        def listed(window, b):
+            return window[:, 0 : SEG * (b + 1)].indirect(offsets[:, b * COLS : (b + 1) * COLS])
+
+        def by_place(ap):
+            return ap.rearrange("p (u a m) -> p m a u", u=2, a=2)
+
+        warm = keep.tile([P, 8], F32, name="warm")
+        nc.vector.memset(warm[:], 0.0)
+        warm2 = keep.tile([P, 8], F32, name="warm2")
+        nc.scalar.activation(warm2[:], warm[:], ACT.Sigmoid)
+
+        ks_pool = keep.tile([P, T], U8, name="ks_pool", align_bytes=64)
+        nc.vector.memset(ks_pool[:].bitcast(I32), 0)
+        ks_rows = k_scales.rearrange("o f t -> (o f) t").bitcast(I32)
+        nc.sync.dma_start(ks_pool[0:32, :].bitcast(I32), ks_rows)
+        for quad in range(1, 4):
+            queue = nc.sync if quad == 1 else nc.scalar
+            queue.dma_start(ks_pool[32 * quad : 32 * quad + 4, :].bitcast(I32), ks_rows[4 * quad : 4 * quad + 4, :])
+
+        kw_pool = keep.tile([P, T], U32, name="kw_pool", align_bytes=64)
+        kw_dram = k_words[0].rearrange("p t c -> p (t c)")
+
+        def load_kw(b):
+            nc.sync.dma_start(
+                kw_pool[:, SEG * b : SEG * (b + 1)].bitcast(I32),
+                kw_dram[:, 4 * SEG * b : 4 * SEG * (b + 1)].bitcast(I32),
+            )
+
+        v_pool = [keep.tile([P, T], BF16, name="v_pool%d" % h, align_bytes=64) for h in range(HALVES)]
+
+        def load_v(b, h):
+            raw = stage.tile([P, SEG], F32, name="v_raw")
+            nc.sync.dma_start(raw[:], vT[P * h : P * (h + 1), SEG * b : SEG * (b + 1)])
+            nc.scalar.activation(v_pool[h][:, SEG * b : SEG * (b + 1)], raw[:], ACT.Copy)
+
+        qs = keep.tile([P, B * PASSES, NQ], U8, name="qs", align_bytes=64)
+        nc.vector.memset(qs[:].rearrange("p g q -> p (g q)").bitcast(I32), 0)
+        ks_second = keep.tile([P, B * N], U8, name="ks_second", align_bytes=64)
+        nc.vector.memset(ks_second[:].bitcast(I32), 0)
+        kb_pool = keep.tile([P, T], F32, name="kb_pool", align_bytes=64)
+        nc.vector.memset(kb_pool[:], 0.0)
+        vs_pool = keep.tile([P, T], F32, name="vs_pool", align_bytes=64)
+        nc.gpsimd.memset(vs_pool[:], 0.0)
+        ident = keep.tile([P, P], F32, name="ident", align_bytes=64)
+        make_identity(nc, ident[:])
+
+        load_v(0, 0)
+        load_kw(0)
+        load_v(0, 1)
+        nc.gpsimd.dma_start(kb_pool[0:1, :], kb[0:1, :])
+        qw = keep.tile([P, B * PASSES, NQ], U32, name="qw", align_bytes=64)
+        nc.sync.dma_start(qw[:].bitcast(I32), q_words.rearrange("b o p q c -> p (b o) (q c)").bitcast(I32))
+        qs_dram = q_scales.rearrange("b o f q -> f (b o) q")
+        for quad in range(4):
+            nc.scalar.dma_start(
+                qs[32 * quad : 32 * quad + 4, :, :].bitcast(I32),
+                qs_dram[4 * quad : 4 * quad + 4, :, :].bitcast(I32),
+            )
+        nc.gpsimd.dma_start(vs_pool[0:1, :], vs[0:1, :])
+        load_kw(1)
+
+        ks_first = keep.tile([P, B * N], U8, name="ks_first", align_bytes=64)
+        ks_listed = keep.tile([P, B * N], U8, name="ks_listed", align_bytes=64)
+        nc.vector.tensor_copy(ks_listed[:], ks_pool[:].indirect(offsets[:]))
+        ks_planes = [ks_first, ks_second]
+
+        def order_key_scales():
+            nc.vector.tensor_copy(
+                ks_first[:].rearrange("p (u a m) -> p u a m", u=2, a=2),
+                ks_listed[:].rearrange("p (m a u) -> p u a m", u=2, a=2),
+            )
+            for quad in range(4):
+                nc.sync.dma_start(
+                    ks_second[32 * quad : 32 * quad + 4, :].bitcast(I32),
+                    ks_first[16 + 4 * quad : 20 + 4 * quad, :].bitcast(I32),
+                )
+
+        def gather_keys(b):
+            kg = keep.tile([P, N], U32, name="kg%d" % b, align_bytes=64)
+            nc.vector.tensor_copy(by_place(kg[:]), listed(kw_pool, b))
+            return kg
+
+        def part_keys(b, kg):
+            kp = keep.tile([P, PASSES, N], U16, name="kp%d" % b, align_bytes=64)
+            nc.vector.tensor_copy(kp[:], kg[:].bitcast(U16).rearrange("p (n o) -> p o n", o=PASSES))
+            return kp
+
+        def scores(b, kp):
+            acc = psum.tile([P, 4, NQ], F32, name="score%d" % b)
+            for t in range(4):
+                for o in range(PASSES):
+                    lo = t * B * P + b * P
+                    nc.tensor.matmul_mx(
+                        out=acc[:, t, :],
+                        lhsT=kp[:, o, P * t : P * (t + 1)].bitcast(FP4X4),
+                        lhsT_scale=ks_planes[o][:, lo : lo + P],
+                        rhs=qw[:, PASSES * b + o, :].bitcast(FP8X4),
+                        rhs_scale=qs[:, PASSES * b + o, :],
+                        start=(o == 0),
+                        stop=(o == PASSES - 1),
+                    )
+            return acc
+
+        def token_columns(pool, b, label, tag):
+            g = keep.tile([P, N], F32, name="%s_g%d" % (label, b), align_bytes=64)
+            nc.vector.tensor_copy(g[:], listed(pool, b))
+            turned = psum.tile([P, 4, P], F32, name="%s_t%d" % (label, b), tag=tag)
+            for t in range(4):
+                first = 2 * (t % 2) + t // 2
+                nc.tensor.transpose(turned[:, t, :], g[:, first:N:4], ident[:])
+            return turned
+
+        def sigmoid(b, acc, kb_t):
+            bias = keep.tile([P, 8], F32, name="bias%d" % b)
+            nc.scalar.activation(bias[:, 0:4], kb_t[:, :, 0], ACT.Copy)
+            prob = keep.tile([P, 4, NQ], F32, name="prob%d" % b, align_bytes=64)
+            for t in range(4):
+                nc.scalar.activation(prob[:, t, :], acc[:, t, :], ACT.Sigmoid, bias=bias[:, t : t + 1])
+            return prob
+
+        def weigh(b, prob, vs_t):
+            w = keep.tile([P, NQ, 4], BF16, name="w%d" % b, align_bytes=64)
+            nc.vector.tensor_tensor(
+                w[:],
+                prob[:].rearrange("p t q -> p q t"),
+                vs_t[:, :, 0].unsqueeze(1).to_broadcast([P, NQ, 4]),
+                MULT,
+            )
+            return w
+
+        def quantize(src, width, label):
+            codes = keep.tile([P, width], U32, name=label + "_codes", align_bytes=64)
+            scales = keep.tile([P, width], U8, name=label + "_scales", align_bytes=64)
+            nc.vector.quantize_mx(out=codes[:].bitcast(FP8X4), scales=scales[:], in_=src)
+            return codes, scales
+
+        def gather_values(b):
+            turned = psum.tile([P, HALVES, 2, P], F32, name="v_t%d" % b)
+            for h in range(HALVES):
+                vg = keep.tile([P, N], BF16, name="vg%d%d" % (b, h), align_bytes=64)
+                nc.scalar.activation(
+                    vg[:].rearrange("p (u m a) -> p m a u", u=2, a=2), listed(v_pool[h], b), ACT.Copy
+                )
+                words = vg[:].bitcast(F32)
+                for u in range(2):
+                    nc.tensor.transpose(turned[:, h, u, :], words[:, P * u : P * (u + 1)], ident[:])
+            return turned
+
+        def group_values(b, turned):
+            grouped = keep.tile([P, DV * 4], BF16, name="v_grouped%d" % b, align_bytes=64)
+            nc.scalar.copy(
+                grouped[:].bitcast(F32).rearrange("p (h f u) -> p h f u", h=HALVES, u=2),
+                turned[:].rearrange("p h u f -> p h f u"),
+            )
+            return grouped
+
+        def finish(b, wq, vq):
+            acc = psum.tile([P, DV], F32, name="y%d" % b, tag="y")
+            nc.tensor.matmul_mx(
+                out=acc[:],
+                lhsT=wq[0][:].bitcast(FP8X4),
+                lhsT_scale=wq[1][:],
+                rhs=vq[0][:].bitcast(FP8X4),
+                rhs_scale=vq[1][:],
+                start=True,
+                stop=True,
+            )
+            y = keep.tile([P, DV], F32, name="y_sb%d" % b, align_bytes=64)
+            nc.scalar.activation(y[:], acc[:], ACT.Copy, scale=1.0 / 16.0)
+            nc.sync.dma_start(out[b], y[:])
+
+        kg0 = gather_keys(0)
+        order_key_scales()
+        kb_t0 = token_columns(kb_pool, 0, "kb", "kb_t")
+        kp0 = part_keys(0, kg0)
+        vt0 = gather_values(0)
+        load_v(1, 0)
+        load_v(1, 1)
+        acc0 = scores(0, kp0)
+        prob0 = sigmoid(0, acc0, kb_t0)
+        vs_t0 = token_columns(vs_pool, 0, "vs", "vs_t0")
+        kg1 = gather_keys(1)
+        kb_t1 = token_columns(kb_pool, 1, "kb", "kb_t")
+        kp1 = part_keys(1, kg1)
+        grouped0 = group_values(0, vt0)
+        w0 = weigh(0, prob0, vs_t0)
+        acc1 = scores(1, kp1)
+        vt1 = gather_values(1)
+        prob1 = sigmoid(1, acc1, kb_t1)
+        vs_t1 = token_columns(vs_pool, 1, "vs", "vs_t1")
+        wq0 = quantize(w0[:].rearrange("p q t -> p (q t)"), NQ, "w0")
+        vq0 = quantize(grouped0[:], DV, "v0")
+        grouped1 = group_values(1, vt1)
+        finish(0, wq0, vq0)
+        w1 = weigh(1, prob1, vs_t1)
+        vq1 = quantize(grouped1[:], DV, "v1")
+        wq1 = quantize(w1[:].rearrange("p q t -> p (q t)"), NQ, "w1")
+        finish(1, wq1, vq1)

@@ -24,12 +24,22 @@ PASSES = D // 512
 HALVES = DV // P
 
 
+ORDER = "Lv.0.1 Lkw.1 Lkb Lkw.0 Lv.0.0 Gkw.0 Gkb.0 Lqs Lv.1.1 Cast.1.1 Gkw.1 Gks Split.1 Cast.0.1 Perm Lv.1.0 Gv.0.1 Cast.0.0 Lvs.0 Cast.1.0 Bias.0 Gv.0.0 Lqw Score.1 Split.0 Gkb.1 Gv.1.0 Bias.1 Gv.1.1 Lvs.1 Score.0 Sig.0 Grp.0 Gvs.0 Gvs.1 Sig.1 Grp.1 Qv.1 Qv.0 W.0 W.1 Qw.0 Fin.0 Qw.1 Fin.1".split()
+OPT = dict(stage=3, ksq='ssaa', kbq='s', qsq='aaaa', shq='g', vsq='s', qwq='a', late=0, biasdep=1, biasv=1, onv=[], sc0='H', sc1='F', kb0='G', kb1='D', vs0='E', vs1='D', vt0='A', vt1='B', y0='D', y1='A')
+
+
 def tile_attend_sigm_kb_segb2q128n512t2048_kernel(tc, q_words, q_scales, k_words, k_scales, vT, vs, kb, offs, out):
     nc = tc.nc
+    queues = {"s": nc.sync, "a": nc.scalar, "g": nc.gpsimd}
     with ExitStack() as ctx:
         keep = ctx.enter_context(tc.tile_pool(name="keep", bufs=1))
-        stage = ctx.enter_context(tc.tile_pool(name="stage", bufs=2))
+        stage = ctx.enter_context(tc.tile_pool(name="stage", bufs=OPT["stage"]))
         psum = ctx.enter_context(tc.psum_pool(name="psum", bufs=1))
+        made = {}
+
+        def sb(name, shape, dtype, tag=None):
+            made[name] = keep.tile(shape, dtype, name=name, tag=tag or name, align_bytes=64)
+            return made[name]
 
         offsets = keep.tile([P, B * COLS], U16, name="offsets")
         nc.sync.dma_start(offsets[:], offs)
@@ -37,92 +47,83 @@ def tile_attend_sigm_kb_segb2q128n512t2048_kernel(tc, q_words, q_scales, k_words
         def listed(window, b):
             return window[:, 0 : SEG * (b + 1)].indirect(offsets[:, b * COLS : (b + 1) * COLS])
 
-        def by_place(ap):
-            return ap.rearrange("p (u a m) -> p m a u", u=2, a=2)
-
-        warm = keep.tile([P, 8], F32, name="warm")
+        ks_pool = sb("ks_pool", [P, T], U8)
+        nc.vector.memset(ks_pool[:].bitcast(I32), 0)
+        ks_rows = k_scales.bitcast(I32).rearrange("o (g r) t -> r g o t", r=4)
+        for r in range(4):
+            queues[OPT["ksq"][r]].dma_start(ks_pool[r:P:16, :].bitcast(I32), ks_rows[r])
+        warm = sb("warm", [P, 8], F32)
         nc.vector.memset(warm[:], 0.0)
-        warm2 = keep.tile([P, 8], F32, name="warm2")
+        warm2 = sb("warm2", [P, 8], F32)
         nc.scalar.activation(warm2[:], warm[:], ACT.Sigmoid)
 
-        ks_pool = keep.tile([P, T], U8, name="ks_pool", align_bytes=64)
-        nc.vector.memset(ks_pool[:].bitcast(I32), 0)
-        ks_rows = k_scales.rearrange("o f t -> (o f) t").bitcast(I32)
-        nc.sync.dma_start(ks_pool[0:32, :].bitcast(I32), ks_rows)
-        for quad in range(1, 4):
-            queue = nc.sync if quad == 1 else nc.scalar
-            queue.dma_start(ks_pool[32 * quad : 32 * quad + 4, :].bitcast(I32), ks_rows[4 * quad : 4 * quad + 4, :])
-
-        kw_pool = keep.tile([P, T], U32, name="kw_pool", align_bytes=64)
-        kw_dram = k_words[0].rearrange("p t c -> p (t c)")
-
-        def load_kw(b):
-            nc.sync.dma_start(
-                kw_pool[:, SEG * b : SEG * (b + 1)].bitcast(I32),
-                kw_dram[:, 4 * SEG * b : 4 * SEG * (b + 1)].bitcast(I32),
-            )
-
-        v_pool = [keep.tile([P, T], BF16, name="v_pool%d" % h, align_bytes=64) for h in range(HALVES)]
-
-        def load_v(b, h):
-            raw = stage.tile([P, SEG], F32, name="v_raw")
-            nc.sync.dma_start(raw[:], vT[P * h : P * (h + 1), SEG * b : SEG * (b + 1)])
-            nc.scalar.activation(v_pool[h][:, SEG * b : SEG * (b + 1)], raw[:], ACT.Copy)
-
-        qs = keep.tile([P, B * PASSES, NQ], U8, name="qs", align_bytes=64)
+        kb_pool = sb("kb_pool", [P, T], F32)
+        nc.vector.memset(kb_pool[:].bitcast(I32), 0)
+        qs = sb("qs", [P, B * PASSES, NQ], U8)
         nc.vector.memset(qs[:].rearrange("p g q -> p (g q)").bitcast(I32), 0)
-        ks_second = keep.tile([P, B * N], U8, name="ks_second", align_bytes=64)
+        ks_second = sb("ks_second", [P, B * N], U8)
         nc.vector.memset(ks_second[:].bitcast(I32), 0)
-        kb_pool = keep.tile([P, T], F32, name="kb_pool", align_bytes=64)
-        nc.vector.memset(kb_pool[:], 0.0)
-        vs_pool = keep.tile([P, T], F32, name="vs_pool", align_bytes=64)
-        nc.gpsimd.memset(vs_pool[:], 0.0)
-        ident = keep.tile([P, P], F32, name="ident", align_bytes=64)
+        vs_pool = sb("vs_pool", [P, T], F32)
+        ident = sb("ident", [P, P], F32)
         make_identity(nc, ident[:])
-
-        load_v(0, 0)
-        load_kw(0)
-        load_v(0, 1)
-        nc.gpsimd.dma_start(kb_pool[0:1, :], kb[0:1, :])
-        qw = keep.tile([P, B * PASSES, NQ], U32, name="qw", align_bytes=64)
-        nc.sync.dma_start(qw[:].bitcast(I32), q_words.rearrange("b o p q c -> p (b o) (q c)").bitcast(I32))
-        qs_dram = q_scales.rearrange("b o f q -> f (b o) q")
-        for quad in range(4):
-            nc.scalar.dma_start(
-                qs[32 * quad : 32 * quad + 4, :, :].bitcast(I32),
-                qs_dram[4 * quad : 4 * quad + 4, :, :].bitcast(I32),
-            )
-        nc.gpsimd.dma_start(vs_pool[0:1, :], vs[0:1, :])
-        load_kw(1)
-
-        ks_first = keep.tile([P, B * N], U8, name="ks_first", align_bytes=64)
-        ks_listed = keep.tile([P, B * N], U8, name="ks_listed", align_bytes=64)
-        nc.vector.tensor_copy(ks_listed[:], ks_pool[:].indirect(offsets[:]))
+        kw_pool = sb("kw_pool", [P, T], U32)
+        kw_dram = k_words[0].rearrange("p t c -> p (t c)")
+        v_pool = [sb("v_pool%d" % h, [P, T], BF16) for h in range(HALVES)]
+        qw = sb("qw", [P, B * PASSES, NQ], U32)
+        ks_first = sb("ks_first", [P, B * N], U8)
+        ks_listed = sb("ks_listed", [P, B * N], U8)
         ks_planes = [ks_first, ks_second]
 
-        def order_key_scales():
+        def seg(b):
+            return slice(SEG * b, SEG * (b + 1))
+
+        def Lkw(b):
+            nc.sync.dma_start(kw_pool[:, seg(b)].bitcast(I32), kw_dram[:, 4 * SEG * b : 4 * SEG * (b + 1)].bitcast(I32))
+
+        def Lv(b, h):
+            raw = stage.tile([P, SEG], F32, name="v_raw", align_bytes=64)
+            made["raw%d%d" % (b, h)] = raw
+            nc.sync.dma_start(raw[:], vT[P * h : P * (h + 1), seg(b)])
+
+        def Lkb():
+            queues[OPT["kbq"]].dma_start(kb_pool[0:1, :], kb[0:1, :])
+
+        def Lvs(b):
+            queues[OPT["vsq"]].dma_start(vs_pool[:, seg(b)], vs[:, seg(b)])
+
+        def Lqw():
+            queues[OPT["qwq"]].dma_start(qw[:].bitcast(I32), q_words.rearrange("b o p q c -> p (b o) (q c)").bitcast(I32))
+
+        def Lqs():
+            qs_dram = q_scales.rearrange("b o f q -> f (b o) q")
+            for quad in range(4):
+                queues[OPT["qsq"][quad]].dma_start(
+                    qs[32 * quad : 32 * quad + 4, :, :].bitcast(I32),
+                    qs_dram[4 * quad : 4 * quad + 4, :, :].bitcast(I32),
+                )
+
+        def Gks():
+            nc.vector.tensor_copy(ks_listed[:], ks_pool[:].indirect(offsets[:]))
+
+        def Perm():
             nc.vector.tensor_copy(
                 ks_first[:].rearrange("p (u a m) -> p u a m", u=2, a=2),
                 ks_listed[:].rearrange("p (m a u) -> p u a m", u=2, a=2),
             )
-            for quad in range(4):
-                nc.sync.dma_start(
-                    ks_second[32 * quad : 32 * quad + 4, :].bitcast(I32),
-                    ks_first[16 + 4 * quad : 20 + 4 * quad, :].bitcast(I32),
-                )
+            queues[OPT["shq"]].dma_start(ks_second[0 : P - 16, :].bitcast(I32), ks_first[16:P, :].bitcast(I32))
 
-        def gather_keys(b):
-            kg = keep.tile([P, N], U32, name="kg%d" % b, align_bytes=64)
-            nc.vector.tensor_copy(by_place(kg[:]), listed(kw_pool, b))
-            return kg
+        def Gkw(b):
+            kg = sb("kg%d" % b, [P, N], U32)
+            nc.vector.tensor_copy(kg[:].rearrange("p (u a m) -> p m a u", u=2, a=2), listed(kw_pool, b))
 
-        def part_keys(b, kg):
-            kp = keep.tile([P, PASSES, N], U16, name="kp%d" % b, align_bytes=64)
-            nc.vector.tensor_copy(kp[:], kg[:].bitcast(U16).rearrange("p (n o) -> p o n", o=PASSES))
-            return kp
+        def Split(b):
+            kp = sb("kp%d" % b, [P, PASSES, N], U16, tag="late%d" % b)
+            nc.vector.tensor_copy(kp[:], made["kg%d" % b][:].bitcast(U16).rearrange("p (n o) -> p o n", o=PASSES))
 
-        def scores(b, kp):
-            acc = psum.tile([P, 4, NQ], F32, name="score%d" % b)
+        def Score(b):
+            acc = psum.tile([P, 4, NQ], F32, name="score%d" % b, tag=OPT["sc%d" % b])
+            made["acc%d" % b] = acc
+            kp = made["kp%d" % b]
             for t in range(4):
                 for o in range(PASSES):
                     lo = t * B * P + b * P
@@ -135,100 +136,104 @@ def tile_attend_sigm_kb_segb2q128n512t2048_kernel(tc, q_words, q_scales, k_words
                         start=(o == 0),
                         stop=(o == PASSES - 1),
                     )
-            return acc
 
-        def token_columns(pool, b, label, tag):
-            g = keep.tile([P, N], F32, name="%s_g%d" % (label, b), align_bytes=64)
+        def columns(pool, b, label, bank, slot):
+            g = sb("%s_g%d" % (label, b), [P, N], F32, tag=slot)
             nc.vector.tensor_copy(g[:], listed(pool, b))
-            turned = psum.tile([P, 4, P], F32, name="%s_t%d" % (label, b), tag=tag)
+            turned = psum.tile([P, 4, P], F32, name="%s_t%d" % (label, b), tag=bank)
+            made["%s_t%d" % (label, b)] = turned
             for t in range(4):
                 first = 2 * (t % 2) + t // 2
                 nc.tensor.transpose(turned[:, t, :], g[:, first:N:4], ident[:])
-            return turned
 
-        def sigmoid(b, acc, kb_t):
-            bias = keep.tile([P, 8], F32, name="bias%d" % b)
-            nc.scalar.activation(bias[:, 0:4], kb_t[:, :, 0], ACT.Copy)
-            prob = keep.tile([P, 4, NQ], F32, name="prob%d" % b, align_bytes=64)
+        def Gkb(b):
+            columns(kb_pool, b, "kb", OPT["kb%d" % b], None)
+
+        def Gvs(b):
+            columns(vs_pool, b, "vs", OPT["vs%d" % b], "late%d" % b if OPT["late"] else None)
+
+        def Bias(b):
+            if OPT["biasdep"]:
+                bias = stage.tile([P, 16], F32, name="v_raw", align_bytes=64)
+                made["bias%d" % b] = bias
+            else:
+                bias = sb("bias%d" % b, [P, 16], F32)
+            if OPT["biasv"]:
+                nc.vector.tensor_copy(bias[:, 0:4], made["kb_t%d" % b][:, :, 0])
+            else:
+                nc.scalar.activation(bias[:, 0:4], made["kb_t%d" % b][:, :, 0], ACT.Copy)
+
+        def Sig(b):
+            prob = sb("prob%d" % b, [P, 4, NQ], F32)
             for t in range(4):
-                nc.scalar.activation(prob[:, t, :], acc[:, t, :], ACT.Sigmoid, bias=bias[:, t : t + 1])
-            return prob
+                nc.scalar.activation(
+                    prob[:, t, :], made["acc%d" % b][:, t, :], ACT.Sigmoid, bias=made["bias%d" % b][:, t : t + 1]
+                )
 
-        def weigh(b, prob, vs_t):
-            w = keep.tile([P, NQ, 4], BF16, name="w%d" % b, align_bytes=64)
+        def W(b):
+            w = sb("w%d" % b, [P, NQ, 4], BF16)
             nc.vector.tensor_tensor(
                 w[:],
-                prob[:].rearrange("p t q -> p q t"),
-                vs_t[:, :, 0].unsqueeze(1).to_broadcast([P, NQ, 4]),
+                made["prob%d" % b][:].rearrange("p t q -> p q t"),
+                made["vs_t%d" % b][:, :, 0].unsqueeze(1).to_broadcast([P, NQ, 4]),
                 MULT,
             )
-            return w
 
         def quantize(src, width, label):
-            codes = keep.tile([P, width], U32, name=label + "_codes", align_bytes=64)
-            scales = keep.tile([P, width], U8, name=label + "_scales", align_bytes=64)
+            codes = sb(label + "_codes", [P, width], U32)
+            scales = sb(label + "_scales", [P, width], U8)
             nc.vector.quantize_mx(out=codes[:].bitcast(FP8X4), scales=scales[:], in_=src)
-            return codes, scales
 
-        def gather_values(b):
-            turned = psum.tile([P, HALVES, 2, P], F32, name="v_t%d" % b)
-            for h in range(HALVES):
-                vg = keep.tile([P, N], BF16, name="vg%d%d" % (b, h), align_bytes=64)
-                nc.scalar.activation(
-                    vg[:].rearrange("p (u m a) -> p m a u", u=2, a=2), listed(v_pool[h], b), ACT.Copy
-                )
-                words = vg[:].bitcast(F32)
-                for u in range(2):
-                    nc.tensor.transpose(turned[:, h, u, :], words[:, P * u : P * (u + 1)], ident[:])
-            return turned
+        def Qw(b):
+            quantize(made["w%d" % b][:].rearrange("p q t -> p (q t)"), NQ, "w%d" % b)
 
-        def group_values(b, turned):
-            grouped = keep.tile([P, DV * 4], BF16, name="v_grouped%d" % b, align_bytes=64)
+        def Qv(b):
+            quantize(made["vgr%d" % b][:], DV, "v%d" % b)
+
+        def Cast(b, h):
+            if "%d%d" % (b, h) not in OPT["onv"]:
+                nc.scalar.activation(v_pool[h][:, seg(b)], made["raw%d%d" % (b, h)][:], ACT.Copy)
+
+        def Gv(b, h):
+            if "v_t%d" % b not in made:
+                made["v_t%d" % b] = psum.tile([P, HALVES, 2, P], F32, name="v_t%d" % b, tag=OPT["vt%d" % b])
+            vg = sb("vg%d%d" % (b, h), [P, N], BF16)
+            placed = vg[:].rearrange("p (u m a) -> p m a u", u=2, a=2)
+            if "%d%d" % (b, h) in OPT["onv"]:
+                nc.vector.tensor_copy(placed, listed(made["raw%d%d" % (b, h)], b))
+            else:
+                nc.scalar.activation(placed, listed(v_pool[h], b), ACT.Copy)
+            words = vg[:].bitcast(F32)
+            for u in range(2):
+                nc.tensor.transpose(made["v_t%d" % b][:, h, u, :], words[:, P * u : P * (u + 1)], ident[:])
+
+        def Grp(b):
+            grouped = sb("vgr%d" % b, [P, DV * 4], BF16)
             nc.scalar.copy(
                 grouped[:].bitcast(F32).rearrange("p (h f u) -> p h f u", h=HALVES, u=2),
-                turned[:].rearrange("p h u f -> p h f u"),
+                made["v_t%d" % b][:].rearrange("p h u f -> p h f u"),
             )
-            return grouped
 
-        def finish(b, wq, vq):
-            acc = psum.tile([P, DV], F32, name="y%d" % b, tag="y")
+        def Fin(b):
+            acc = psum.tile([P, DV], F32, name="y%d" % b, tag=OPT["y%d" % b])
             nc.tensor.matmul_mx(
                 out=acc[:],
-                lhsT=wq[0][:].bitcast(FP8X4),
-                lhsT_scale=wq[1][:],
-                rhs=vq[0][:].bitcast(FP8X4),
-                rhs_scale=vq[1][:],
+                lhsT=made["w%d_codes" % b][:].bitcast(FP8X4),
+                lhsT_scale=made["w%d_scales" % b][:],
+                rhs=made["v%d_codes" % b][:].bitcast(FP8X4),
+                rhs_scale=made["v%d_scales" % b][:],
                 start=True,
                 stop=True,
             )
-            y = keep.tile([P, DV], F32, name="y_sb%d" % b, align_bytes=64)
+            y = sb("y_sb%d" % b, [P, DV], F32)
             nc.scalar.activation(y[:], acc[:], ACT.Copy, scale=1.0 / 16.0)
             nc.sync.dma_start(out[b], y[:])
 
-        kg0 = gather_keys(0)
-        order_key_scales()
-        kb_t0 = token_columns(kb_pool, 0, "kb", "kb_t")
-        kp0 = part_keys(0, kg0)
-        vt0 = gather_values(0)
-        load_v(1, 0)
-        load_v(1, 1)
-        acc0 = scores(0, kp0)
-        prob0 = sigmoid(0, acc0, kb_t0)
-        vs_t0 = token_columns(vs_pool, 0, "vs", "vs_t0")
-        kg1 = gather_keys(1)
-        kb_t1 = token_columns(kb_pool, 1, "kb", "kb_t")
-        kp1 = part_keys(1, kg1)
-        grouped0 = group_values(0, vt0)
-        w0 = weigh(0, prob0, vs_t0)
-        acc1 = scores(1, kp1)
-        vt1 = gather_values(1)
-        prob1 = sigmoid(1, acc1, kb_t1)
-        vs_t1 = token_columns(vs_pool, 1, "vs", "vs_t1")
-        wq0 = quantize(w0[:].rearrange("p q t -> p (q t)"), NQ, "w0")
-        vq0 = quantize(grouped0[:], DV, "v0")
-        grouped1 = group_values(1, vt1)
-        finish(0, wq0, vq0)
-        w1 = weigh(1, prob1, vs_t1)
-        vq1 = quantize(grouped1[:], DV, "v1")
-        wq1 = quantize(w1[:].rearrange("p q t -> p (q t)"), NQ, "w1")
-        finish(1, wq1, vq1)
+        steps = {
+            "Lkw": Lkw, "Lv": Lv, "Lkb": Lkb, "Lvs": Lvs, "Lqw": Lqw, "Lqs": Lqs, "Gks": Gks, "Perm": Perm,
+            "Gkw": Gkw, "Split": Split, "Score": Score, "Gkb": Gkb, "Gvs": Gvs, "Bias": Bias, "Sig": Sig, "W": W,
+            "Qw": Qw, "Qv": Qv, "Cast": Cast, "Gv": Gv, "Grp": Grp, "Fin": Fin,
+        }
+        for step in ORDER:
+            parts = step.split(".")
+            steps[parts[0]](*[int(c) for c in parts[1:]])

@@ -24,8 +24,8 @@ PASSES = D // 512
 HALVES = DV // P
 
 
-ORDER = "Lv.0.1 Lkw.1 Lkb Lkw.0 Lv.0.0 Gkw.0 Gkb.0 Lqs Lv.1.1 Cast.1.1 Gkw.1 Gks Split.1 Cast.0.1 Perm Lv.1.0 Gv.0.1 Cast.0.0 Lvs.0 Cast.1.0 Bias.0 Gv.0.0 Lqw Score.1 Split.0 Gkb.1 Gv.1.0 Bias.1 Gv.1.1 Lvs.1 Score.0 Sig.0 Grp.0 Gvs.0 Gvs.1 Sig.1 Grp.1 Qv.1 Qv.0 W.0 W.1 Qw.0 Fin.0 Qw.1 Fin.1".split()
-OPT = dict(stage=3, ksq='ssaa', kbq='s', qsq='aaaa', shq='g', vsq='s', qwq='a', late=0, biasdep=1, biasv=1, onv=[], sc0='H', sc1='F', kb0='G', kb1='D', vs0='E', vs1='D', vt0='A', vt1='B', y0='D', y1='A')
+ORDER = "Lvs.0 Lv.0.0 Lks.1 Lks.0 Lkw.1 Cast.0.0 Lks.2 Lks.3 Gv.0.0 Lv.1.0 Lkw.0 Gkw.0 Gks Cast.1.0 Warm Perm Lqs Lqw Lv.1.1 Lkb Gkw.1 Gkb.0 Split.0 Lv.0.1 Cast.0.1 Split.1 Gv.0.1 Cast.1.1 Score.0 Gv.1.0 Gkb.1 Sig.0 Score.1 Gv.1.1 Gvs.0 Grp.1 Grp.0 Qv.0 W.0 Lvs.1 Qw.0 Gvs.1 Sig.1 W.1 Qw.1 Qv.1 Fin.0 Fin.1".split()
+OPT = dict(ksq='aaaa', kbq='s', qsq='ssss', shq='g', vsq='s', qwq='s', onv=[], cut=['00'], grpv='va', yv='aa', kbr='ss', vsr='ss', vsrow=0, sc0='A', sc1='B', vt0='C', vt1='D', y0='E', y1='F', t_vs_g1='kg1', t_prob1='vg10', t_prob0='', t_vs_g0='')
 
 
 def tile_attend_sigm_kb_segb2q128n512t2048_kernel(tc, q_words, q_scales, k_words, k_scales, vT, vs, kb, offs, out):
@@ -33,12 +33,11 @@ def tile_attend_sigm_kb_segb2q128n512t2048_kernel(tc, q_words, q_scales, k_words
     queues = {"s": nc.sync, "a": nc.scalar, "g": nc.gpsimd}
     with ExitStack() as ctx:
         keep = ctx.enter_context(tc.tile_pool(name="keep", bufs=1))
-        stage = ctx.enter_context(tc.tile_pool(name="stage", bufs=OPT["stage"]))
         psum = ctx.enter_context(tc.psum_pool(name="psum", bufs=1))
         made = {}
 
-        def sb(name, shape, dtype, tag=None):
-            made[name] = keep.tile(shape, dtype, name=name, tag=tag or name, align_bytes=64)
+        def sb(name, shape, dtype):
+            made[name] = keep.tile(shape, dtype, name=name, tag=OPT.get("t_" + name) or name, align_bytes=64)
             return made[name]
 
         offsets = keep.tile([P, B * COLS], U16, name="offsets")
@@ -50,12 +49,15 @@ def tile_attend_sigm_kb_segb2q128n512t2048_kernel(tc, q_words, q_scales, k_words
         ks_pool = sb("ks_pool", [P, T], U8)
         nc.vector.memset(ks_pool[:].bitcast(I32), 0)
         ks_rows = k_scales.bitcast(I32).rearrange("o (g r) t -> r g o t", r=4)
-        for r in range(4):
-            queues[OPT["ksq"][r]].dma_start(ks_pool[r:P:16, :].bitcast(I32), ks_rows[r])
         warm = sb("warm", [P, 8], F32)
         nc.vector.memset(warm[:], 0.0)
-        warm2 = sb("warm2", [P, 8], F32)
-        nc.scalar.activation(warm2[:], warm[:], ACT.Sigmoid)
+
+        def Lks(r):
+            queues[OPT["ksq"][r]].dma_start(ks_pool[r:P:16, :].bitcast(I32), ks_rows[r])
+
+        def Warm():
+            warm2 = sb("warm2", [P, 8], F32)
+            nc.scalar.activation(warm2[:], warm[:], ACT.Sigmoid)
 
         kb_pool = sb("kb_pool", [P, T], F32)
         nc.vector.memset(kb_pool[:].bitcast(I32), 0)
@@ -64,11 +66,14 @@ def tile_attend_sigm_kb_segb2q128n512t2048_kernel(tc, q_words, q_scales, k_words
         ks_second = sb("ks_second", [P, B * N], U8)
         nc.vector.memset(ks_second[:].bitcast(I32), 0)
         vs_pool = sb("vs_pool", [P, T], F32)
+        if OPT["vsrow"]:
+            nc.vector.memset(vs_pool[:].bitcast(I32), 0)
         ident = sb("ident", [P, P], F32)
         make_identity(nc, ident[:])
         kw_pool = sb("kw_pool", [P, T], U32)
         kw_dram = k_words[0].rearrange("p t c -> p (t c)")
         v_pool = [sb("v_pool%d" % h, [P, T], BF16) for h in range(HALVES)]
+        v_raw = [sb("v_raw%d" % h, [P, T], F32) for h in range(HALVES)]
         qw = sb("qw", [P, B * PASSES, NQ], U32)
         ks_first = sb("ks_first", [P, B * N], U8)
         ks_listed = sb("ks_listed", [P, B * N], U8)
@@ -77,19 +82,24 @@ def tile_attend_sigm_kb_segb2q128n512t2048_kernel(tc, q_words, q_scales, k_words
         def seg(b):
             return slice(SEG * b, SEG * (b + 1))
 
+        def pieces(b, h):
+            if "%d%d" % (b, h) in OPT["cut"]:
+                return [slice(SEG * b, SEG * b + SEG // 2), slice(SEG * b + SEG // 2, SEG * (b + 1))]
+            return [seg(b)]
+
         def Lkw(b):
             nc.sync.dma_start(kw_pool[:, seg(b)].bitcast(I32), kw_dram[:, 4 * SEG * b : 4 * SEG * (b + 1)].bitcast(I32))
 
         def Lv(b, h):
-            raw = stage.tile([P, SEG], F32, name="v_raw", align_bytes=64)
-            made["raw%d%d" % (b, h)] = raw
-            nc.sync.dma_start(raw[:], vT[P * h : P * (h + 1), seg(b)])
+            for cols in pieces(b, h):
+                nc.sync.dma_start(v_raw[h][:, cols], vT[P * h : P * (h + 1), cols])
 
         def Lkb():
             queues[OPT["kbq"]].dma_start(kb_pool[0:1, :], kb[0:1, :])
 
         def Lvs(b):
-            queues[OPT["vsq"]].dma_start(vs_pool[:, seg(b)], vs[:, seg(b)])
+            rows = 1 if OPT["vsrow"] else P
+            queues[OPT["vsq"]].dma_start(vs_pool[0:rows, seg(b)], vs[0:rows, seg(b)])
 
         def Lqw():
             queues[OPT["qwq"]].dma_start(qw[:].bitcast(I32), q_words.rearrange("b o p q c -> p (b o) (q c)").bitcast(I32))
@@ -114,11 +124,14 @@ def tile_attend_sigm_kb_segb2q128n512t2048_kernel(tc, q_words, q_scales, k_words
 
         def Gkw(b):
             kg = sb("kg%d" % b, [P, N], U32)
-            nc.vector.tensor_copy(kg[:].rearrange("p (u a m) -> p m a u", u=2, a=2), listed(kw_pool, b))
+            nc.vector.tensor_copy(kg[:], listed(kw_pool, b))
 
         def Split(b):
-            kp = sb("kp%d" % b, [P, PASSES, N], U16, tag="late%d" % b)
-            nc.vector.tensor_copy(kp[:], made["kg%d" % b][:].bitcast(U16).rearrange("p (n o) -> p o n", o=PASSES))
+            kp = sb("kp%d" % b, [P, PASSES, N], U16)
+            nc.vector.tensor_copy(
+                kp[:].rearrange("p o (u a m) -> p o m a u", u=2, a=2),
+                made["kg%d" % b][:].bitcast(U16).rearrange("p (m a u o) -> p o m a u", u=2, a=2, o=PASSES),
+            )
 
         def Score(b):
             acc = psum.tile([P, 4, NQ], F32, name="score%d" % b, tag=OPT["sc%d" % b])
@@ -137,45 +150,32 @@ def tile_attend_sigm_kb_segb2q128n512t2048_kernel(tc, q_words, q_scales, k_words
                         stop=(o == PASSES - 1),
                     )
 
-        def columns(pool, b, label, bank, slot):
-            g = sb("%s_g%d" % (label, b), [P, N], F32, tag=slot)
+        def columns(pool, b, label):
+            g = sb("%s_g%d" % (label, b), [P, N], F32)
             nc.vector.tensor_copy(g[:], listed(pool, b))
-            turned = psum.tile([P, 4, P], F32, name="%s_t%d" % (label, b), tag=bank)
-            made["%s_t%d" % (label, b)] = turned
-            for t in range(4):
-                first = 2 * (t % 2) + t // 2
-                nc.tensor.transpose(turned[:, t, :], g[:, first:N:4], ident[:])
+            col = sb("%s_c%d" % (label, b), [P, 4], F32)
+            queues[OPT[label + "r"][b]].dma_start(col[:], g[0:1, :].rearrange("o (p t) -> o p t", t=4))
 
         def Gkb(b):
-            columns(kb_pool, b, "kb", OPT["kb%d" % b], None)
+            columns(kb_pool, b, "kb")
 
         def Gvs(b):
-            columns(vs_pool, b, "vs", OPT["vs%d" % b], "late%d" % b if OPT["late"] else None)
-
-        def Bias(b):
-            if OPT["biasdep"]:
-                bias = stage.tile([P, 16], F32, name="v_raw", align_bytes=64)
-                made["bias%d" % b] = bias
-            else:
-                bias = sb("bias%d" % b, [P, 16], F32)
-            if OPT["biasv"]:
-                nc.vector.tensor_copy(bias[:, 0:4], made["kb_t%d" % b][:, :, 0])
-            else:
-                nc.scalar.activation(bias[:, 0:4], made["kb_t%d" % b][:, :, 0], ACT.Copy)
+            columns(vs_pool, b, "vs")
 
         def Sig(b):
             prob = sb("prob%d" % b, [P, 4, NQ], F32)
             for t in range(4):
+                step = 2 * (t % 2) + t // 2
                 nc.scalar.activation(
-                    prob[:, t, :], made["acc%d" % b][:, t, :], ACT.Sigmoid, bias=made["bias%d" % b][:, t : t + 1]
+                    prob[:, t, :], made["acc%d" % b][:, t, :], ACT.Sigmoid, bias=made["kb_c%d" % b][:, step : step + 1]
                 )
 
         def W(b):
             w = sb("w%d" % b, [P, NQ, 4], BF16)
             nc.vector.tensor_tensor(
-                w[:],
-                made["prob%d" % b][:].rearrange("p t q -> p q t"),
-                made["vs_t%d" % b][:, :, 0].unsqueeze(1).to_broadcast([P, NQ, 4]),
+                w[:].rearrange("p q (u a) -> p q u a", u=2),
+                made["prob%d" % b][:].rearrange("p (u a) q -> p q u a", u=2),
+                made["vs_c%d" % b][:].rearrange("p (a u) -> p u a", u=2).unsqueeze(1).to_broadcast([P, NQ, 2, 2]),
                 MULT,
             )
 
@@ -192,7 +192,8 @@ def tile_attend_sigm_kb_segb2q128n512t2048_kernel(tc, q_words, q_scales, k_words
 
         def Cast(b, h):
             if "%d%d" % (b, h) not in OPT["onv"]:
-                nc.scalar.activation(v_pool[h][:, seg(b)], made["raw%d%d" % (b, h)][:], ACT.Copy)
+                for cols in pieces(b, h):
+                    nc.scalar.activation(v_pool[h][:, cols], v_raw[h][:, cols], ACT.Copy)
 
         def Gv(b, h):
             if "v_t%d" % b not in made:
@@ -200,7 +201,7 @@ def tile_attend_sigm_kb_segb2q128n512t2048_kernel(tc, q_words, q_scales, k_words
             vg = sb("vg%d%d" % (b, h), [P, N], BF16)
             placed = vg[:].rearrange("p (u m a) -> p m a u", u=2, a=2)
             if "%d%d" % (b, h) in OPT["onv"]:
-                nc.vector.tensor_copy(placed, listed(made["raw%d%d" % (b, h)], b))
+                nc.vector.tensor_copy(placed, listed(v_raw[h], b))
             else:
                 nc.scalar.activation(placed, listed(v_pool[h], b), ACT.Copy)
             words = vg[:].bitcast(F32)
@@ -209,7 +210,8 @@ def tile_attend_sigm_kb_segb2q128n512t2048_kernel(tc, q_words, q_scales, k_words
 
         def Grp(b):
             grouped = sb("vgr%d" % b, [P, DV * 4], BF16)
-            nc.scalar.copy(
+            mover = nc.vector.tensor_copy if OPT["grpv"][b] == "v" else nc.scalar.copy
+            mover(
                 grouped[:].bitcast(F32).rearrange("p (h f u) -> p h f u", h=HALVES, u=2),
                 made["v_t%d" % b][:].rearrange("p h u f -> p h f u"),
             )
@@ -226,12 +228,15 @@ def tile_attend_sigm_kb_segb2q128n512t2048_kernel(tc, q_words, q_scales, k_words
                 stop=True,
             )
             y = sb("y_sb%d" % b, [P, DV], F32)
-            nc.scalar.activation(y[:], acc[:], ACT.Copy, scale=1.0 / 16.0)
+            if OPT["yv"][b] == "v":
+                nc.vector.tensor_scalar(y[:], acc[:], 1.0 / 16.0, None, MULT)
+            else:
+                nc.scalar.activation(y[:], acc[:], ACT.Copy, scale=1.0 / 16.0)
             nc.sync.dma_start(out[b], y[:])
 
         steps = {
-            "Lkw": Lkw, "Lv": Lv, "Lkb": Lkb, "Lvs": Lvs, "Lqw": Lqw, "Lqs": Lqs, "Gks": Gks, "Perm": Perm,
-            "Gkw": Gkw, "Split": Split, "Score": Score, "Gkb": Gkb, "Gvs": Gvs, "Bias": Bias, "Sig": Sig, "W": W,
+            "Lks": Lks, "Warm": Warm, "Lkw": Lkw, "Lv": Lv, "Lkb": Lkb, "Lvs": Lvs, "Lqw": Lqw, "Lqs": Lqs, "Gks": Gks, "Perm": Perm,
+            "Gkw": Gkw, "Split": Split, "Score": Score, "Gkb": Gkb, "Gvs": Gvs, "Sig": Sig, "W": W,
             "Qw": Qw, "Qv": Qv, "Cast": Cast, "Gv": Gv, "Grp": Grp, "Fin": Fin,
         }
         for step in ORDER:

@@ -15,230 +15,219 @@ U8 = mybir.dt.uint8
 FP8X4 = mybir.dt.float8_e4m3fn_x4
 FP4X4 = mybir.dt.float4_e2m1fn_x4
 ACT = mybir.ActivationFunctionType
-MULT = mybir.AluOpType.mult
 
 P = 128
+PLACES = 4
 SEG = T // B
-COLS = N // 16
-PASSES = D // 512
+LIST_COLS = N // 16
+PASSES = D // (P * PLACES)
 HALVES = DV // P
-
-
-ORDER = "Lvs.0 Lv.0.0 Lks.1 Lks.0 Lkw.1 Cast.0.0 Lks.2 Lks.3 Gv.0.0 Lv.1.0 Lkw.0 Gkw.0 Gks Cast.1.0 Warm Perm Lqs Lqw Lv.1.1 Lkb Gkw.1 Gkb.0 Split.0 Lv.0.1 Cast.0.1 Split.1 Gv.0.1 Cast.1.1 Score.0 Gv.1.0 Gkb.1 Sig.0 Score.1 Gv.1.1 Gvs.0 Grp.1 Grp.0 Qv.0 W.0 Lvs.1 Qw.0 Gvs.1 Sig.1 W.1 Qw.1 Qv.1 Fin.0 Fin.1".split()
-OPT = dict(ksq='aaaa', kbq='s', qsq='ssss', shq='g', vsq='s', qwq='s', onv=[], cut=['00'], grpv='va', yv='aa', kbr='ss', vsr='ss', vsrow=0, sc0='A', sc1='B', vt0='C', vt1='D', y0='E', y1='F', t_vs_g1='kg1', t_prob1='vg10', t_prob0='', t_vs_g0='')
+SECOND_PASS_SHIFT = 16
 
 
 def tile_attend_sigm_kb_segb2q128n512t2048_kernel(tc, q_words, q_scales, k_words, k_scales, vT, vs, kb, offs, out):
     nc = tc.nc
-    queues = {"s": nc.sync, "a": nc.scalar, "g": nc.gpsimd}
     with ExitStack() as ctx:
-        keep = ctx.enter_context(tc.tile_pool(name="keep", bufs=1))
+        sbuf = ctx.enter_context(tc.tile_pool(name="sbuf", bufs=1))
         psum = ctx.enter_context(tc.psum_pool(name="psum", bufs=1))
-        made = {}
 
-        def sb(name, shape, dtype):
-            made[name] = keep.tile(shape, dtype, name=name, tag=OPT.get("t_" + name) or name, align_bytes=64)
-            return made[name]
+        def new_tile(name, shape, dtype, takes_over=None):
+            return sbuf.tile(shape, dtype, name=name, tag=takes_over or name, align_bytes=64)
 
-        offsets = keep.tile([P, B * COLS], U16, name="offsets")
-        nc.sync.dma_start(offsets[:], offs)
-
-        def listed(window, b):
-            return window[:, 0 : SEG * (b + 1)].indirect(offsets[:, b * COLS : (b + 1) * COLS])
-
-        ks_pool = sb("ks_pool", [P, T], U8)
-        nc.vector.memset(ks_pool[:].bitcast(I32), 0)
-        ks_rows = k_scales.bitcast(I32).rearrange("o (g r) t -> r g o t", r=4)
-        warm = sb("warm", [P, 8], F32)
-        nc.vector.memset(warm[:], 0.0)
-
-        def Lks(r):
-            queues[OPT["ksq"][r]].dma_start(ks_pool[r:P:16, :].bitcast(I32), ks_rows[r])
-
-        def Warm():
-            warm2 = sb("warm2", [P, 8], F32)
-            nc.scalar.activation(warm2[:], warm[:], ACT.Sigmoid)
-
-        kb_pool = sb("kb_pool", [P, T], F32)
-        nc.vector.memset(kb_pool[:].bitcast(I32), 0)
-        qs = sb("qs", [P, B * PASSES, NQ], U8)
-        nc.vector.memset(qs[:].rearrange("p g q -> p (g q)").bitcast(I32), 0)
-        ks_second = sb("ks_second", [P, B * N], U8)
-        nc.vector.memset(ks_second[:].bitcast(I32), 0)
-        vs_pool = sb("vs_pool", [P, T], F32)
-        if OPT["vsrow"]:
-            nc.vector.memset(vs_pool[:].bitcast(I32), 0)
-        ident = sb("ident", [P, P], F32)
-        make_identity(nc, ident[:])
-        kw_pool = sb("kw_pool", [P, T], U32)
-        kw_dram = k_words[0].rearrange("p t c -> p (t c)")
-        v_pool = [sb("v_pool%d" % h, [P, T], BF16) for h in range(HALVES)]
-        v_raw = [sb("v_raw%d" % h, [P, T], F32) for h in range(HALVES)]
-        qw = sb("qw", [P, B * PASSES, NQ], U32)
-        ks_first = sb("ks_first", [P, B * N], U8)
-        ks_listed = sb("ks_listed", [P, B * N], U8)
-        ks_planes = [ks_first, ks_second]
-
-        def seg(b):
+        def stretch(b):
             return slice(SEG * b, SEG * (b + 1))
 
-        def pieces(b, h):
-            if "%d%d" % (b, h) in OPT["cut"]:
-                return [slice(SEG * b, SEG * b + SEG // 2), slice(SEG * b + SEG // 2, SEG * (b + 1))]
-            return [seg(b)]
+        offsets = sbuf.tile([P, B * LIST_COLS], U16, name="offsets")
+        nc.sync.dma_start(offsets[:], offs)
 
-        def Lkw(b):
-            nc.sync.dma_start(kw_pool[:, seg(b)].bitcast(I32), kw_dram[:, 4 * SEG * b : 4 * SEG * (b + 1)].bitcast(I32))
+        def listed_for_all(pool):
+            return pool[:].indirect(offsets[:])
 
-        def Lv(b, h):
-            for cols in pieces(b, h):
-                nc.sync.dma_start(v_raw[h][:, cols], vT[P * h : P * (h + 1), cols])
+        def listed_for(pool, b):
+            return pool[:, 0 : SEG * (b + 1)].indirect(offsets[:, b * LIST_COLS : (b + 1) * LIST_COLS])
 
-        def Lkb():
-            queues[OPT["kbq"]].dma_start(kb_pool[0:1, :], kb[0:1, :])
+        ks_pool = new_tile("ks_pool", [P, T], U8)
+        nc.vector.memset(ks_pool[:].bitcast(I32), 0)
+        warm_in = new_tile("warm_in", [P, 8], F32)
+        nc.vector.memset(warm_in[:], 0.0)
+        identity = new_tile("identity", [P, P], F32)
+        make_identity(nc, identity[:])
+        kb_pool = new_tile("kb_pool", [P, T], F32)
+        nc.vector.memset(kb_pool[:].bitcast(I32), 0)
+        q_planes = new_tile("q_planes", [P, B * PASSES, NQ], U8)
+        nc.gpsimd.memset(q_planes[:].rearrange("p g q -> p (g q)").bitcast(I32), 0)
+        ks_pass1 = new_tile("ks_pass1", [P, B * N], U8)
+        nc.gpsimd.memset(ks_pass1[:].bitcast(I32), 0)
+        vs_pool = new_tile("vs_pool", [P, T], F32)
+        nc.gpsimd.memset(vs_pool[:].bitcast(I32), 0)
 
-        def Lvs(b):
-            rows = 1 if OPT["vsrow"] else P
-            queues[OPT["vsq"]].dma_start(vs_pool[0:rows, seg(b)], vs[0:rows, seg(b)])
+        v_raw = [new_tile("v_raw%d" % h, [P, T], F32) for h in range(HALVES)]
+        v_pool = [new_tile("v_pool%d" % h, [P, T], BF16) for h in range(HALVES)]
 
-        def Lqw():
-            queues[OPT["qwq"]].dma_start(qw[:].bitcast(I32), q_words.rearrange("b o p q c -> p (b o) (q c)").bitcast(I32))
+        def load_values(h, cols):
+            nc.sync.dma_start(v_raw[h][:, cols], vT[P * h : P * (h + 1), cols])
 
-        def Lqs():
-            qs_dram = q_scales.rearrange("b o f q -> f (b o) q")
-            for quad in range(4):
-                queues[OPT["qsq"][quad]].dma_start(
-                    qs[32 * quad : 32 * quad + 4, :, :].bitcast(I32),
-                    qs_dram[4 * quad : 4 * quad + 4, :, :].bitcast(I32),
-                )
+        first_cols = [slice(0, SEG // 2), slice(SEG // 2, SEG)]
+        load_values(0, first_cols[0])
 
-        def Gks():
-            nc.vector.tensor_copy(ks_listed[:], ks_pool[:].indirect(offsets[:]))
+        ks_rows = k_scales.bitcast(I32).rearrange("o (c r) t -> r c o t", r=4)
+        for r, queue in enumerate((nc.sync, nc.sync, nc.scalar, nc.scalar)):
+            queue.dma_start(ks_pool[r:P:SECOND_PASS_SHIFT, :].bitcast(I32), ks_rows[r])
 
-        def Perm():
-            nc.vector.tensor_copy(
-                ks_first[:].rearrange("p (u a m) -> p u a m", u=2, a=2),
-                ks_listed[:].rearrange("p (m a u) -> p u a m", u=2, a=2),
+        warm_out = new_tile("warm_out", [P, 8], F32)
+        nc.scalar.activation(warm_out[:], warm_in[:], ACT.Sigmoid)
+
+        load_values(0, first_cols[1])
+        load_values(1, stretch(0))
+        nc.sync.dma_start(kb_pool[0:1, :], kb[0:1, :])
+        load_values(0, stretch(1))
+        kw_pool = new_tile("kw_pool", [P, T], U32)
+        kw_bytes = k_words[0].rearrange("p t c -> p (t c)")
+        for b in range(B):
+            nc.sync.dma_start(
+                kw_pool[:, stretch(b)].bitcast(I32), kw_bytes[:, 4 * SEG * b : 4 * SEG * (b + 1)].bitcast(I32)
             )
-            queues[OPT["shq"]].dma_start(ks_second[0 : P - 16, :].bitcast(I32), ks_first[16:P, :].bitcast(I32))
 
-        def Gkw(b):
-            kg = sb("kg%d" % b, [P, N], U32)
-            nc.vector.tensor_copy(kg[:], listed(kw_pool, b))
+        ks_listed = new_tile("ks_listed", [P, B * N], U8)
+        nc.vector.tensor_copy(ks_listed[:], listed_for_all(ks_pool))
+        ks_pass0 = new_tile("ks_pass0", [P, B * N], U8)
+        nc.vector.tensor_copy(
+            ks_pass0[:].rearrange("p (u a m) -> p u a m", u=2, a=2),
+            ks_listed[:].rearrange("p (m a u) -> p u a m", u=2, a=2),
+        )
+        nc.sync.dma_start(
+            ks_pass1[0 : P - SECOND_PASS_SHIFT, :].bitcast(I32), ks_pass0[SECOND_PASS_SHIFT:P, :].bitcast(I32)
+        )
+        k_planes = [ks_pass0, ks_pass1]
 
-        def Split(b):
-            kp = sb("kp%d" % b, [P, PASSES, N], U16)
-            nc.vector.tensor_copy(
-                kp[:].rearrange("p o (u a m) -> p o m a u", u=2, a=2),
-                made["kg%d" % b][:].bitcast(U16).rearrange("p (m a u o) -> p o m a u", u=2, a=2, o=PASSES),
+        q_codes = new_tile("q_codes", [P, B * PASSES, NQ], U32)
+        nc.sync.dma_start(q_codes[:].bitcast(I32), q_words.rearrange("b o p q c -> p (b o) (q c)").bitcast(I32))
+        qs_rows = q_scales.rearrange("b o f q -> f (b o) q")
+        for c in range(4):
+            nc.sync.dma_start(
+                q_planes[32 * c : 32 * c + 4, :, :].bitcast(I32), qs_rows[4 * c : 4 * c + 4, :, :].bitcast(I32)
             )
+        load_values(1, stretch(1))
+        for b in range(B):
+            nc.sync.dma_start(vs_pool[0:1, stretch(b)], vs[0:1, stretch(b)])
 
-        def Score(b):
-            acc = psum.tile([P, 4, NQ], F32, name="score%d" % b, tag=OPT["sc%d" % b])
-            made["acc%d" % b] = acc
-            kp = made["kp%d" % b]
-            for t in range(4):
+        def deal_out(name, row):
+            cols = new_tile(name, [P, PLACES], F32)
+            nc.sync.dma_start(cols[:], row.rearrange("r (m t) -> r m t", t=PLACES))
+            return cols
+
+        kb_listed = new_tile("kb_listed", [P, B * N], F32)
+        nc.vector.tensor_copy(kb_listed[:], listed_for_all(kb_pool))
+        kb_cols = [deal_out("kb_cols%d" % b, kb_listed[0:1, N * b : N * (b + 1)]) for b in range(B)]
+
+        kw_listed = new_tile("kw_listed", [P, B * N], U32)
+        nc.vector.tensor_copy(kw_listed[:], listed_for_all(kw_pool))
+        k_codes = new_tile("k_codes", [P, PASSES, B * N], U16)
+        nc.vector.tensor_copy(
+            k_codes[:].rearrange("p o (u a m) -> p o m a u", u=2, a=2),
+            kw_listed[:].bitcast(U16).rearrange("p (m a u o) -> p o m a u", u=2, a=2, o=PASSES),
+        )
+
+        def round_values(h, cols):
+            nc.scalar.activation(v_pool[h][:, cols], v_raw[h][:, cols], ACT.Copy)
+
+        v_turned = [psum.tile([P, HALVES, 2, P], F32, name="v_turned%d" % b) for b in range(B)]
+
+        def gather_values(b, h):
+            v_listed = new_tile("v_listed%d%d" % (b, h), [P, N], BF16)
+            nc.scalar.activation(
+                v_listed[:].rearrange("p (u m a) -> p m a u", u=2, a=2), listed_for(v_pool[h], b), ACT.Copy
+            )
+            words = v_listed[:].bitcast(F32)
+            for u in range(2):
+                nc.tensor.transpose(v_turned[b][:, h, u, :], words[:, P * u : P * (u + 1)], identity[:])
+
+        def group_values(b, takes_over):
+            grouped = new_tile("v_grouped%d" % b, [P, DV * PLACES], BF16, takes_over)
+            nc.scalar.copy(
+                grouped[:].bitcast(F32).rearrange("p (h f u) -> p h f u", h=HALVES, u=2),
+                v_turned[b][:].rearrange("p h u f -> p h f u"),
+            )
+            return grouped
+
+        def gather_token_scales(b):
+            vs_listed = new_tile("vs_listed%d" % b, [P, N], F32)
+            nc.vector.tensor_copy(vs_listed[:], listed_for(vs_pool, b))
+            return deal_out("vs_cols%d" % b, vs_listed[0:1, :])
+
+        def scores(b):
+            acc = psum.tile([P, PLACES, NQ], F32, name="scores%d" % b)
+            for place in range(PLACES):
+                cols = slice(place * B * P + b * P, place * B * P + (b + 1) * P)
                 for o in range(PASSES):
-                    lo = t * B * P + b * P
                     nc.tensor.matmul_mx(
-                        out=acc[:, t, :],
-                        lhsT=kp[:, o, P * t : P * (t + 1)].bitcast(FP4X4),
-                        lhsT_scale=ks_planes[o][:, lo : lo + P],
-                        rhs=qw[:, PASSES * b + o, :].bitcast(FP8X4),
-                        rhs_scale=qs[:, PASSES * b + o, :],
+                        out=acc[:, place, :],
+                        lhsT=k_codes[:, o, cols].bitcast(FP4X4),
+                        lhsT_scale=k_planes[o][:, cols],
+                        rhs=q_codes[:, PASSES * b + o, :].bitcast(FP8X4),
+                        rhs_scale=q_planes[:, PASSES * b + o, :],
                         start=(o == 0),
                         stop=(o == PASSES - 1),
                     )
+            return acc
 
-        def columns(pool, b, label):
-            g = sb("%s_g%d" % (label, b), [P, N], F32)
-            nc.vector.tensor_copy(g[:], listed(pool, b))
-            col = sb("%s_c%d" % (label, b), [P, 4], F32)
-            queues[OPT[label + "r"][b]].dma_start(col[:], g[0:1, :].rearrange("o (p t) -> o p t", t=4))
+        def sigmoid(b, acc):
+            prob = new_tile("prob%d" % b, [P, PLACES, NQ], F32)
+            for place in range(PLACES):
+                u, a = divmod(place, 2)
+                bias = kb_cols[b][:, 2 * a + u : 2 * a + u + 1]
+                nc.scalar.activation(prob[:, place, :], acc[:, place, :], ACT.Sigmoid, bias=bias)
+            return prob
 
-        def Gkb(b):
-            columns(kb_pool, b, "kb")
-
-        def Gvs(b):
-            columns(vs_pool, b, "vs")
-
-        def Sig(b):
-            prob = sb("prob%d" % b, [P, 4, NQ], F32)
-            for t in range(4):
-                step = 2 * (t % 2) + t // 2
-                nc.scalar.activation(
-                    prob[:, t, :], made["acc%d" % b][:, t, :], ACT.Sigmoid, bias=made["kb_c%d" % b][:, step : step + 1]
-                )
-
-        def W(b):
-            w = sb("w%d" % b, [P, NQ, 4], BF16)
+        def weigh(b, prob, token_scales):
+            w = new_tile("w%d" % b, [P, NQ * PLACES], BF16)
             nc.vector.tensor_tensor(
-                w[:].rearrange("p q (u a) -> p q u a", u=2),
-                made["prob%d" % b][:].rearrange("p (u a) q -> p q u a", u=2),
-                made["vs_c%d" % b][:].rearrange("p (a u) -> p u a", u=2).unsqueeze(1).to_broadcast([P, NQ, 2, 2]),
-                MULT,
+                w[:].rearrange("p (q u a) -> p q u a", u=2, a=2),
+                prob[:].rearrange("p (u a) q -> p q u a", u=2),
+                token_scales[:].rearrange("p (a u) -> p u a", u=2).unsqueeze(1).to_broadcast([P, NQ, 2, 2]),
+                mybir.AluOpType.mult,
             )
+            return w
 
-        def quantize(src, width, label):
-            codes = sb(label + "_codes", [P, width], U32)
-            scales = sb(label + "_scales", [P, width], U8)
-            nc.vector.quantize_mx(out=codes[:].bitcast(FP8X4), scales=scales[:], in_=src)
+        def quantize(name, grouped, width, takes_over=None):
+            codes = new_tile(name + "_codes", [P, width], U32, takes_over)
+            scales = new_tile(name + "_scales", [P, width], U8)
+            nc.vector.quantize_mx(out=codes[:].bitcast(FP8X4), scales=scales[:], in_=grouped[:])
+            return codes, scales
 
-        def Qw(b):
-            quantize(made["w%d" % b][:].rearrange("p q t -> p (q t)"), NQ, "w%d" % b)
-
-        def Qv(b):
-            quantize(made["vgr%d" % b][:], DV, "v%d" % b)
-
-        def Cast(b, h):
-            if "%d%d" % (b, h) not in OPT["onv"]:
-                for cols in pieces(b, h):
-                    nc.scalar.activation(v_pool[h][:, cols], v_raw[h][:, cols], ACT.Copy)
-
-        def Gv(b, h):
-            if "v_t%d" % b not in made:
-                made["v_t%d" % b] = psum.tile([P, HALVES, 2, P], F32, name="v_t%d" % b, tag=OPT["vt%d" % b])
-            vg = sb("vg%d%d" % (b, h), [P, N], BF16)
-            placed = vg[:].rearrange("p (u m a) -> p m a u", u=2, a=2)
-            if "%d%d" % (b, h) in OPT["onv"]:
-                nc.vector.tensor_copy(placed, listed(v_raw[h], b))
-            else:
-                nc.scalar.activation(placed, listed(v_pool[h], b), ACT.Copy)
-            words = vg[:].bitcast(F32)
-            for u in range(2):
-                nc.tensor.transpose(made["v_t%d" % b][:, h, u, :], words[:, P * u : P * (u + 1)], ident[:])
-
-        def Grp(b):
-            grouped = sb("vgr%d" % b, [P, DV * 4], BF16)
-            mover = nc.vector.tensor_copy if OPT["grpv"][b] == "v" else nc.scalar.copy
-            mover(
-                grouped[:].bitcast(F32).rearrange("p (h f u) -> p h f u", h=HALVES, u=2),
-                made["v_t%d" % b][:].rearrange("p h u f -> p h f u"),
-            )
-
-        def Fin(b):
-            acc = psum.tile([P, DV], F32, name="y%d" % b, tag=OPT["y%d" % b])
+        def finish(b, w_mx, v_mx):
+            acc = psum.tile([P, DV], F32, name="y_acc%d" % b)
             nc.tensor.matmul_mx(
                 out=acc[:],
-                lhsT=made["w%d_codes" % b][:].bitcast(FP8X4),
-                lhsT_scale=made["w%d_scales" % b][:],
-                rhs=made["v%d_codes" % b][:].bitcast(FP8X4),
-                rhs_scale=made["v%d_scales" % b][:],
+                lhsT=w_mx[0][:].bitcast(FP8X4),
+                lhsT_scale=w_mx[1][:],
+                rhs=v_mx[0][:].bitcast(FP8X4),
+                rhs_scale=v_mx[1][:],
                 start=True,
                 stop=True,
             )
-            y = sb("y_sb%d" % b, [P, DV], F32)
-            if OPT["yv"][b] == "v":
-                nc.vector.tensor_scalar(y[:], acc[:], 1.0 / 16.0, None, MULT)
-            else:
-                nc.scalar.activation(y[:], acc[:], ACT.Copy, scale=1.0 / 16.0)
+            y = new_tile("y%d" % b, [P, DV], F32)
+            nc.scalar.activation(y[:], acc[:], ACT.Copy, scale=1.0 / 16.0)
             nc.sync.dma_start(out[b], y[:])
 
-        steps = {
-            "Lks": Lks, "Warm": Warm, "Lkw": Lkw, "Lv": Lv, "Lkb": Lkb, "Lvs": Lvs, "Lqw": Lqw, "Lqs": Lqs, "Gks": Gks, "Perm": Perm,
-            "Gkw": Gkw, "Split": Split, "Score": Score, "Gkb": Gkb, "Gvs": Gvs, "Sig": Sig, "W": W,
-            "Qw": Qw, "Qv": Qv, "Cast": Cast, "Gv": Gv, "Grp": Grp, "Fin": Fin,
-        }
-        for step in ORDER:
-            parts = step.split(".")
-            steps[parts[0]](*[int(c) for c in parts[1:]])
+        round_values(0, first_cols[0])
+        round_values(0, first_cols[1])
+        round_values(1, stretch(0))
+        gather_values(0, 0)
+        gather_values(0, 1)
+        round_values(0, stretch(1))
+        gather_values(1, 0)
+        v_grouped0 = group_values(0, "v_raw0")
+        round_values(1, stretch(1))
+        gather_values(1, 1)
+        vs_cols = [gather_token_scales(b) for b in range(B)]
+        accs = [scores(b) for b in range(B)]
+        probs = [sigmoid(b, accs[b]) for b in range(B)]
+        v_grouped1 = group_values(1, "kb_cols1")
+        v_mx0 = quantize("v0", v_grouped0, DV, "kb_listed")
+        w_mx0 = quantize("w0", weigh(0, probs[0], vs_cols[0]), NQ)
+        w1 = weigh(1, probs[1], vs_cols[1])
+        v_mx1 = quantize("v1", v_grouped1, DV, "vs_listed1")
+        w_mx1 = quantize("w1", w1, NQ)
+        finish(0, w_mx0, v_mx0)
+        finish(1, w_mx1, v_mx1)

@@ -18,11 +18,13 @@ ACT = mybir.ActivationFunctionType
 
 P = 128
 PLACES = 4
+RUN = 4
 SEG = T // B
 LIST_COLS = N // 16
 PASSES = D // (P * PLACES)
 HALVES = DV // P
 SECOND_PASS_SHIFT = 16
+COL_STEP = 8
 
 
 def tile_attend_sigm_kb_segb2q128n512t2048_kernel(tc, q_words, q_scales, k_words, k_scales, vT, vs, kb, offs, out):
@@ -34,41 +36,44 @@ def tile_attend_sigm_kb_segb2q128n512t2048_kernel(tc, q_words, q_scales, k_words
         def new_tile(name, shape, dtype, takes_over=None):
             return sbuf.tile(shape, dtype, name=name, tag=takes_over or name, align_bytes=64)
 
+        def new_bank(name, shape, takes_over=None):
+            return psum.tile(shape, F32, name=name, tag=takes_over or name)
+
         def stretch(b):
             return slice(SEG * b, SEG * (b + 1))
 
         offsets = sbuf.tile([P, B * LIST_COLS], U16, name="offsets")
         nc.sync.dma_start(offsets[:], offs)
 
-        def listed_for_all(pool):
-            return pool[:].indirect(offsets[:])
+        def listed_for_all(window):
+            return window.indirect(offsets[:])
 
-        def listed_for(pool, b):
-            return pool[:, 0 : SEG * (b + 1)].indirect(offsets[:, b * LIST_COLS : (b + 1) * LIST_COLS])
+        def listed_for(window, b):
+            return window[:, 0 : SEG * (b + 1)].indirect(offsets[:, b * LIST_COLS : (b + 1) * LIST_COLS])
 
         ks_pool = new_tile("ks_pool", [P, T], U8)
         nc.vector.memset(ks_pool[:].bitcast(I32), 0)
         warm_in = new_tile("warm_in", [P, 8], F32)
         nc.vector.memset(warm_in[:], 0.0)
-        identity = new_tile("identity", [P, P], F32)
-        make_identity(nc, identity[:])
-        kb_pool = new_tile("kb_pool", [P, T], F32)
-        nc.vector.memset(kb_pool[:].bitcast(I32), 0)
+        kb_pool = new_tile("kb_pool", [P, T], I32)
+        nc.vector.memset(kb_pool[:], 0)
         q_planes = new_tile("q_planes", [P, B * PASSES, NQ], U8)
         nc.gpsimd.memset(q_planes[:].rearrange("p g q -> p (g q)").bitcast(I32), 0)
         ks_pass1 = new_tile("ks_pass1", [P, B * N], U8)
         nc.gpsimd.memset(ks_pass1[:].bitcast(I32), 0)
-        vs_pool = new_tile("vs_pool", [P, T], F32)
-        nc.gpsimd.memset(vs_pool[:].bitcast(I32), 0)
+        identity = new_tile("identity", [P, P], F32)
+        make_identity(nc, identity[:])
+        vs_pool = new_tile("vs_pool", [P, T], I32)
+        nc.gpsimd.memset(vs_pool[:], 0)
 
-        v_raw = [new_tile("v_raw%d" % h, [P, T], F32) for h in range(HALVES)]
+        v_raw = [[new_tile("v_raw%d%d" % (b, h), [P, SEG], F32) for h in range(HALVES)] for b in range(B)]
         v_pool = [new_tile("v_pool%d" % h, [P, T], BF16) for h in range(HALVES)]
 
-        def load_values(h, cols):
-            nc.sync.dma_start(v_raw[h][:, cols], vT[P * h : P * (h + 1), cols])
+        def load_values(b, h, cols=slice(0, SEG)):
+            nc.sync.dma_start(v_raw[b][h][:, cols], vT[P * h : P * (h + 1), SEG * b + cols.start : SEG * b + cols.stop])
 
         first_cols = [slice(0, SEG // 2), slice(SEG // 2, SEG)]
-        load_values(0, first_cols[0])
+        load_values(0, 0, first_cols[0])
 
         ks_rows = k_scales.bitcast(I32).rearrange("o (c r) t -> r c o t", r=4)
         for r, queue in enumerate((nc.sync, nc.sync, nc.scalar, nc.scalar)):
@@ -77,29 +82,20 @@ def tile_attend_sigm_kb_segb2q128n512t2048_kernel(tc, q_words, q_scales, k_words
         warm_out = new_tile("warm_out", [P, 8], F32)
         nc.scalar.activation(warm_out[:], warm_in[:], ACT.Sigmoid)
 
-        load_values(0, first_cols[1])
-        load_values(1, stretch(0))
-        nc.sync.dma_start(kb_pool[0:1, :], kb[0:1, :])
-        load_values(0, stretch(1))
         kw_pool = new_tile("kw_pool", [P, T], U32)
         kw_bytes = k_words[0].rearrange("p t c -> p (t c)")
-        for b in range(B):
+
+        def load_keys(b):
             nc.sync.dma_start(
                 kw_pool[:, stretch(b)].bitcast(I32), kw_bytes[:, 4 * SEG * b : 4 * SEG * (b + 1)].bitcast(I32)
             )
 
-        ks_listed = new_tile("ks_listed", [P, B * N], U8)
-        nc.vector.tensor_copy(ks_listed[:], listed_for_all(ks_pool))
-        ks_pass0 = new_tile("ks_pass0", [P, B * N], U8)
-        nc.vector.tensor_copy(
-            ks_pass0[:].rearrange("p (u a m) -> p u a m", u=2, a=2),
-            ks_listed[:].rearrange("p (m a u) -> p u a m", u=2, a=2),
-        )
-        nc.sync.dma_start(
-            ks_pass1[0 : P - SECOND_PASS_SHIFT, :].bitcast(I32), ks_pass0[SECOND_PASS_SHIFT:P, :].bitcast(I32)
-        )
-        k_planes = [ks_pass0, ks_pass1]
-
+        load_values(0, 0, first_cols[1])
+        load_values(0, 1)
+        load_keys(0)
+        load_values(1, 0)
+        nc.sync.dma_start(kb_pool[0:1, :], kb[0:1, :].bitcast(I32))
+        load_keys(1)
         q_codes = new_tile("q_codes", [P, B * PASSES, NQ], U32)
         nc.sync.dma_start(q_codes[:].bitcast(I32), q_words.rearrange("b o p q c -> p (b o) (q c)").bitcast(I32))
         qs_rows = q_scales.rearrange("b o f q -> f (b o) q")
@@ -107,42 +103,68 @@ def tile_attend_sigm_kb_segb2q128n512t2048_kernel(tc, q_words, q_scales, k_words
             nc.sync.dma_start(
                 q_planes[32 * c : 32 * c + 4, :, :].bitcast(I32), qs_rows[4 * c : 4 * c + 4, :, :].bitcast(I32)
             )
-        load_values(1, stretch(1))
-        for b in range(B):
-            nc.sync.dma_start(vs_pool[0:1, stretch(b)], vs[0:1, stretch(b)])
 
-        def deal_out(name, row):
-            cols = new_tile(name, [P, PLACES], F32)
-            nc.sync.dma_start(cols[:], row.rearrange("r (m t) -> r m t", t=PLACES))
-            return cols
+        ks_listed = new_tile("ks_listed", [P, B * N], U8)
+        nc.vector.tensor_copy(ks_listed[:], listed_for_all(ks_pool[:]))
 
-        kb_listed = new_tile("kb_listed", [P, B * N], F32)
-        nc.vector.tensor_copy(kb_listed[:], listed_for_all(kb_pool))
-        kb_cols = [deal_out("kb_cols%d" % b, kb_listed[0:1, N * b : N * (b + 1)]) for b in range(B)]
+        kw_listed = [new_tile("kw_listed%d" % b, [P, N], U32) for b in range(B)]
+        k_codes = [new_tile("k_codes%d" % b, [P, PASSES, N], U16) for b in range(B)]
 
-        kw_listed = new_tile("kw_listed", [P, B * N], U32)
-        nc.vector.tensor_copy(kw_listed[:], listed_for_all(kw_pool))
-        k_codes = new_tile("k_codes", [P, PASSES, B * N], U16)
+        def gather_keys(b):
+            nc.vector.tensor_copy(kw_listed[b][:], listed_for(kw_pool, b))
+
+        def part_keys(b):
+            nc.vector.tensor_copy(
+                k_codes[b][:].rearrange("p o (t g r) -> p o t g r", t=PLACES, r=RUN),
+                kw_listed[b][:].bitcast(U16).rearrange("p (g t r o) -> p o t g r", t=PLACES, r=RUN, o=PASSES),
+            )
+
+        gather_keys(0)
+
+        ks_pass0 = new_tile("ks_pass0", [P, B * N], U8)
         nc.vector.tensor_copy(
-            k_codes[:].rearrange("p o (u a m) -> p o m a u", u=2, a=2),
-            kw_listed[:].bitcast(U16).rearrange("p (m a u o) -> p o m a u", u=2, a=2, o=PASSES),
+            ks_pass0[:].bitcast(I32).rearrange("p (b t x y) -> p b x t y", b=B, t=PLACES, y=4),
+            ks_listed[:].bitcast(I32).rearrange("p (b x y t) -> p b x t y", b=B, t=PLACES, y=4),
         )
+        nc.sync.dma_start(
+            ks_pass1[0 : P - SECOND_PASS_SHIFT, :].bitcast(I32), ks_pass0[SECOND_PASS_SHIFT:P, :].bitcast(I32)
+        )
+        k_planes = [ks_pass0, ks_pass1]
+        load_values(1, 1)
+        nc.sync.dma_start(vs_pool[0:1, :], vs[0:1, :].bitcast(I32))
 
-        def round_values(h, cols):
-            nc.scalar.activation(v_pool[h][:, cols], v_raw[h][:, cols], ACT.Copy)
+        def turn_rows(name, listed, count):
+            bank = new_bank(name, [P, COL_STEP * (count - 1) + P])
+            for k in range(count):
+                nc.tensor.transpose(
+                    bank[:, COL_STEP * k : COL_STEP * k + P], listed[:, P * k : P * (k + 1)].bitcast(F32), identity[:]
+                )
+            return bank[:, 0 : COL_STEP * count : COL_STEP]
 
-        v_turned = [psum.tile([P, HALVES, 2, P], F32, name="v_turned%d" % b) for b in range(B)]
+        kb_listed = new_tile("kb_listed", [P, B * N], U32)
+        nc.vector.tensor_copy(
+            kb_listed[:].rearrange("p (b t g r) -> p b g t r", b=B, t=PLACES, r=RUN),
+            listed_for_all(kb_pool[:].bitcast(U32)),
+        )
+        part_keys(0)
+
+        def round_values(b, h, cols=slice(0, SEG)):
+            nc.scalar.activation(
+                v_pool[h][:, SEG * b + cols.start : SEG * b + cols.stop], v_raw[b][h][:, cols], ACT.Copy
+            )
+
+        v_turned = [new_bank("v_turned%d" % b, [P, HALVES, 2, P]) for b in range(B)]
 
         def gather_values(b, h):
             v_listed = new_tile("v_listed%d%d" % (b, h), [P, N], BF16)
             nc.scalar.activation(
-                v_listed[:].rearrange("p (u m a) -> p m a u", u=2, a=2), listed_for(v_pool[h], b), ACT.Copy
+                v_listed[:].rearrange("p (g r t) -> p g t r", t=PLACES, r=RUN), listed_for(v_pool[h], b), ACT.Copy
             )
             words = v_listed[:].bitcast(F32)
             for u in range(2):
-                nc.tensor.transpose(v_turned[b][:, h, u, :], words[:, P * u : P * (u + 1)], identity[:])
+                nc.tensor.transpose(v_turned[b][:, h, u, :], words[:, u : N // 2 : 2], identity[:])
 
-        def group_values(b, takes_over):
+        def group_values(b, takes_over=None):
             grouped = new_tile("v_grouped%d" % b, [P, DV * PLACES], BF16, takes_over)
             nc.scalar.copy(
                 grouped[:].bitcast(F32).rearrange("p (h f u) -> p h f u", h=HALVES, u=2),
@@ -151,19 +173,23 @@ def tile_attend_sigm_kb_segb2q128n512t2048_kernel(tc, q_words, q_scales, k_words
             return grouped
 
         def gather_token_scales(b):
-            vs_listed = new_tile("vs_listed%d" % b, [P, N], F32)
-            nc.vector.tensor_copy(vs_listed[:], listed_for(vs_pool, b))
-            return deal_out("vs_cols%d" % b, vs_listed[0:1, :])
+            vs_listed = new_tile("vs_listed%d" % b, [P, N], U32)
+            nc.vector.tensor_copy(
+                vs_listed[:].rearrange("p (t g r) -> p g t r", t=PLACES, r=RUN),
+                listed_for(vs_pool[:].bitcast(U32), b),
+            )
+            return turn_rows("vs_turned%d" % b, vs_listed, PLACES)
 
         def scores(b):
-            acc = psum.tile([P, PLACES, NQ], F32, name="scores%d" % b)
+            acc = new_bank("scores%d" % b, [P, PLACES, NQ])
             for place in range(PLACES):
-                cols = slice(place * B * P + b * P, place * B * P + (b + 1) * P)
+                cols = slice(place * P, (place + 1) * P)
+                plane_cols = slice(b * N + place * P, b * N + (place + 1) * P)
                 for o in range(PASSES):
                     nc.tensor.matmul_mx(
                         out=acc[:, place, :],
-                        lhsT=k_codes[:, o, cols].bitcast(FP4X4),
-                        lhsT_scale=k_planes[o][:, cols],
+                        lhsT=k_codes[b][:, o, cols].bitcast(FP4X4),
+                        lhsT_scale=k_planes[o][:, plane_cols],
                         rhs=q_codes[:, PASSES * b + o, :].bitcast(FP8X4),
                         rhs_scale=q_planes[:, PASSES * b + o, :],
                         start=(o == 0),
@@ -171,20 +197,19 @@ def tile_attend_sigm_kb_segb2q128n512t2048_kernel(tc, q_words, q_scales, k_words
                     )
             return acc
 
-        def sigmoid(b, acc):
-            prob = new_tile("prob%d" % b, [P, PLACES, NQ], F32)
+        def sigmoid(b, acc, kb_cols, takes_over=None):
+            prob = new_tile("prob%d" % b, [P, PLACES, NQ], F32, takes_over)
             for place in range(PLACES):
-                u, a = divmod(place, 2)
-                bias = kb_cols[b][:, 2 * a + u : 2 * a + u + 1]
-                nc.scalar.activation(prob[:, place, :], acc[:, place, :], ACT.Sigmoid, bias=bias)
+                col = PLACES * b + place
+                nc.scalar.activation(prob[:, place, :], acc[:, place, :], ACT.Sigmoid, bias=kb_cols[:, col : col + 1])
             return prob
 
         def weigh(b, prob, token_scales):
             w = new_tile("w%d" % b, [P, NQ * PLACES], BF16)
             nc.vector.tensor_tensor(
-                w[:].rearrange("p (q u a) -> p q u a", u=2, a=2),
-                prob[:].rearrange("p (u a) q -> p q u a", u=2),
-                token_scales[:].rearrange("p (a u) -> p u a", u=2).unsqueeze(1).to_broadcast([P, NQ, 2, 2]),
+                w[:].rearrange("p (c i t) -> p c t i", i=4, t=PLACES),
+                prob[:].rearrange("p t (c i) -> p c t i", i=4),
+                token_scales.unsqueeze(1).unsqueeze(3).to_broadcast([P, NQ // 4, PLACES, 4]),
                 mybir.AluOpType.mult,
             )
             return w
@@ -195,8 +220,8 @@ def tile_attend_sigm_kb_segb2q128n512t2048_kernel(tc, q_words, q_scales, k_words
             nc.vector.quantize_mx(out=codes[:].bitcast(FP8X4), scales=scales[:], in_=grouped[:])
             return codes, scales
 
-        def finish(b, w_mx, v_mx):
-            acc = psum.tile([P, DV], F32, name="y_acc%d" % b)
+        def finish(b, w_mx, v_mx, takes_over):
+            acc = new_bank("y_acc%d" % b, [P, DV], takes_over)
             nc.tensor.matmul_mx(
                 out=acc[:],
                 lhsT=w_mx[0][:].bitcast(FP8X4),
@@ -210,24 +235,33 @@ def tile_attend_sigm_kb_segb2q128n512t2048_kernel(tc, q_words, q_scales, k_words
             nc.scalar.activation(y[:], acc[:], ACT.Copy, scale=1.0 / 16.0)
             nc.sync.dma_start(out[b], y[:])
 
-        round_values(0, first_cols[0])
-        round_values(0, first_cols[1])
-        round_values(1, stretch(0))
+        round_values(0, 0, first_cols[0])
+        round_values(0, 0, first_cols[1])
         gather_values(0, 0)
+        round_values(0, 1)
         gather_values(0, 1)
-        round_values(0, stretch(1))
+        kb_turned = turn_rows("kb_turned", kb_listed, B * PLACES)
+        round_values(1, 0)
+        v_grouped0 = group_values(0, "v_raw10")
         gather_values(1, 0)
-        v_grouped0 = group_values(0, "v_raw0")
-        round_values(1, stretch(1))
+        round_values(1, 1)
         gather_values(1, 1)
-        vs_cols = [gather_token_scales(b) for b in range(B)]
-        accs = [scores(b) for b in range(B)]
-        probs = [sigmoid(b, accs[b]) for b in range(B)]
-        v_grouped1 = group_values(1, "kb_cols1")
-        v_mx0 = quantize("v0", v_grouped0, DV, "kb_listed")
-        w_mx0 = quantize("w0", weigh(0, probs[0], vs_cols[0]), NQ)
-        w1 = weigh(1, probs[1], vs_cols[1])
+        kb_cols = new_tile("kb_cols", [P, B * PLACES], F32, "v_raw11")
+        nc.scalar.copy(kb_cols[:], kb_turned)
+        acc0 = scores(0)
+        gather_keys(1)
+        vs_cols0 = gather_token_scales(0)
+        part_keys(1)
+        prob0 = sigmoid(0, acc0, kb_cols, "v_pool1")
+        acc1 = scores(1)
+        vs_cols1 = gather_token_scales(1)
+        v_grouped1 = group_values(1)
+        prob1 = sigmoid(1, acc1, kb_cols, "v_listed11")
+        v_mx0 = quantize("v0", v_grouped0, DV, "kw_listed1")
+        w0 = weigh(0, prob0, vs_cols0)
         v_mx1 = quantize("v1", v_grouped1, DV, "vs_listed1")
+        w_mx0 = quantize("w0", w0, NQ)
+        w1 = weigh(1, prob1, vs_cols1)
         w_mx1 = quantize("w1", w1, NQ)
-        finish(0, w_mx0, v_mx0)
-        finish(1, w_mx1, v_mx1)
+        finish(0, w_mx0, v_mx0, None)
+        finish(1, w_mx1, v_mx1, "kb_turned")

@@ -18,13 +18,11 @@ ACT = mybir.ActivationFunctionType
 
 P = 128
 PLACES = 4
-RUN = 4
 SEG = T // B
 LIST_COLS = N // 16
 PASSES = D // (P * PLACES)
 HALVES = DV // P
-SECOND_PASS_SHIFT = 16
-COL_STEP = 8
+ROW_STEP = 4
 
 
 def tile_attend_sigm_kb_segb2q128n512t2048_kernel(tc, q_words, q_scales, k_words, k_scales, vT, vs, kb, offs, out):
@@ -49,22 +47,22 @@ def tile_attend_sigm_kb_segb2q128n512t2048_kernel(tc, q_words, q_scales, k_words
             return window.indirect(offsets[:])
 
         def listed_for(window, b):
-            return window[:, 0 : SEG * (b + 1)].indirect(offsets[:, b * LIST_COLS : (b + 1) * LIST_COLS])
+            return window.indirect(offsets[:, b * LIST_COLS : (b + 1) * LIST_COLS])
 
         ks_pool = new_tile("ks_pool", [P, T], U8)
         nc.vector.memset(ks_pool[:].bitcast(I32), 0)
         warm_in = new_tile("warm_in", [P, 8], F32)
         nc.vector.memset(warm_in[:], 0.0)
-        kb_pool = new_tile("kb_pool", [P, T], I32)
-        nc.vector.memset(kb_pool[:], 0)
+        kb_pool = new_tile("kb_pool", [P, T], F32)
+        nc.vector.memset(kb_pool[:].bitcast(I32), 0)
+        vs_pool = new_tile("vs_pool", [P, T], F32)
+        nc.vector.memset(vs_pool[:].bitcast(I32), 0)
         q_planes = new_tile("q_planes", [P, B * PASSES, NQ], U8)
         nc.gpsimd.memset(q_planes[:].rearrange("p g q -> p (g q)").bitcast(I32), 0)
-        ks_pass1 = new_tile("ks_pass1", [P, B * N], U8)
-        nc.gpsimd.memset(ks_pass1[:].bitcast(I32), 0)
+        k_planes = new_tile("k_planes", [P, PASSES, B * N], U8)
+        nc.gpsimd.memset(k_planes[:].rearrange("p o n -> p (o n)").bitcast(I32), 0)
         identity = new_tile("identity", [P, P], F32)
         make_identity(nc, identity[:])
-        vs_pool = new_tile("vs_pool", [P, T], I32)
-        nc.gpsimd.memset(vs_pool[:], 0)
 
         v_raw = [[new_tile("v_raw%d%d" % (b, h), [P, SEG], F32) for h in range(HALVES)] for b in range(B)]
         v_pool = [new_tile("v_pool%d" % h, [P, T], BF16) for h in range(HALVES)]
@@ -73,11 +71,8 @@ def tile_attend_sigm_kb_segb2q128n512t2048_kernel(tc, q_words, q_scales, k_words
             nc.sync.dma_start(v_raw[b][h][:, cols], vT[P * h : P * (h + 1), SEG * b + cols.start : SEG * b + cols.stop])
 
         first_cols = [slice(0, SEG // 2), slice(SEG // 2, SEG)]
+        nc.sync.dma_start(ks_pool[0:P:ROW_STEP, :].bitcast(I32), k_scales.rearrange("o f t -> (o f) t").bitcast(I32))
         load_values(0, 0, first_cols[0])
-
-        ks_rows = k_scales.bitcast(I32).rearrange("o (c r) t -> r c o t", r=4)
-        for r, queue in enumerate((nc.sync, nc.sync, nc.scalar, nc.scalar)):
-            queue.dma_start(ks_pool[r:P:SECOND_PASS_SHIFT, :].bitcast(I32), ks_rows[r])
 
         warm_out = new_tile("warm_out", [P, 8], F32)
         nc.scalar.activation(warm_out[:], warm_in[:], ACT.Sigmoid)
@@ -91,11 +86,13 @@ def tile_attend_sigm_kb_segb2q128n512t2048_kernel(tc, q_words, q_scales, k_words
             )
 
         load_values(0, 0, first_cols[1])
+        nc.sync.dma_start(kb_pool[0:1, :], kb[0:1, :])
         load_values(0, 1)
         load_keys(0)
         load_values(1, 0)
-        nc.sync.dma_start(kb_pool[0:1, :], kb[0:1, :].bitcast(I32))
+        nc.sync.dma_start(vs_pool[0:1, :], vs[0:1, :])
         load_keys(1)
+        load_values(1, 1)
         q_codes = new_tile("q_codes", [P, B * PASSES, NQ], U32)
         nc.sync.dma_start(q_codes[:].bitcast(I32), q_words.rearrange("b o p q c -> p (b o) (q c)").bitcast(I32))
         qs_rows = q_scales.rearrange("b o f q -> f (b o) q")
@@ -106,90 +103,82 @@ def tile_attend_sigm_kb_segb2q128n512t2048_kernel(tc, q_words, q_scales, k_words
 
         ks_listed = new_tile("ks_listed", [P, B * N], U8)
         nc.vector.tensor_copy(ks_listed[:], listed_for_all(ks_pool[:]))
+        ks_placed = new_tile("ks_placed", [P, B * N], U8)
+        nc.vector.tensor_copy(
+            ks_placed[:].rearrange("p (t m) -> p t m", t=PLACES), ks_listed[:].rearrange("p (m t) -> p t m", t=PLACES)
+        )
+        for o in reversed(range(PASSES)):
+            for r in range(4):
+                first = ROW_STEP * (16 * o + r)
+                nc.sync.dma_start(
+                    k_planes[r:P:32, o, :].bitcast(I32),
+                    ks_placed[first : first + 3 * 4 * ROW_STEP + 1 : 4 * ROW_STEP, :].bitcast(I32),
+                )
+
+        def deal_out(name, listed):
+            cols = [new_tile("%s%d" % (name, b), [P, PLACES], F32) for b in range(B)]
+            for b in range(B):
+                nc.sync.dma_start(cols[b][:], listed[0:1, N * b : N * (b + 1)].rearrange("r (m t) -> r m t", t=PLACES))
+            return cols
+
+        kb_listed = new_tile("kb_listed", [P, B * N], F32)
+        nc.vector.tensor_copy(kb_listed[:], listed_for_all(kb_pool[:]))
+        kb_cols = deal_out("kb_cols", kb_listed)
 
         kw_listed = [new_tile("kw_listed%d" % b, [P, N], U32) for b in range(B)]
         k_codes = [new_tile("k_codes%d" % b, [P, PASSES, N], U16) for b in range(B)]
 
         def gather_keys(b):
-            nc.vector.tensor_copy(kw_listed[b][:], listed_for(kw_pool, b))
+            nc.vector.tensor_copy(kw_listed[b][:], listed_for(kw_pool[:, 0 : SEG * (b + 1)], b))
 
         def part_keys(b):
             nc.vector.tensor_copy(
-                k_codes[b][:].rearrange("p o (t g r) -> p o t g r", t=PLACES, r=RUN),
-                kw_listed[b][:].bitcast(U16).rearrange("p (g t r o) -> p o t g r", t=PLACES, r=RUN, o=PASSES),
+                k_codes[b][:].rearrange("p o (t x y) -> p o x t y", t=PLACES, y=4),
+                kw_listed[b][:].bitcast(U16).rearrange("p (x y t o) -> p o x t y", t=PLACES, y=4, o=PASSES),
             )
 
         gather_keys(0)
-
-        ks_pass0 = new_tile("ks_pass0", [P, B * N], U8)
-        nc.vector.tensor_copy(
-            ks_pass0[:].bitcast(I32).rearrange("p (b t x y) -> p b x t y", b=B, t=PLACES, y=4),
-            ks_listed[:].bitcast(I32).rearrange("p (b x y t) -> p b x t y", b=B, t=PLACES, y=4),
-        )
-        nc.sync.dma_start(
-            ks_pass1[0 : P - SECOND_PASS_SHIFT, :].bitcast(I32), ks_pass0[SECOND_PASS_SHIFT:P, :].bitcast(I32)
-        )
-        k_planes = [ks_pass0, ks_pass1]
-        load_values(1, 1)
-        nc.sync.dma_start(vs_pool[0:1, :], vs[0:1, :].bitcast(I32))
-
-        def turn_rows(name, listed, count):
-            bank = new_bank(name, [P, COL_STEP * (count - 1) + P])
-            for k in range(count):
-                nc.tensor.transpose(
-                    bank[:, COL_STEP * k : COL_STEP * k + P], listed[:, P * k : P * (k + 1)].bitcast(F32), identity[:]
-                )
-            return bank[:, 0 : COL_STEP * count : COL_STEP]
-
-        kb_listed = new_tile("kb_listed", [P, B * N], U32)
-        nc.vector.tensor_copy(
-            kb_listed[:].rearrange("p (b t g r) -> p b g t r", b=B, t=PLACES, r=RUN),
-            listed_for_all(kb_pool[:].bitcast(U32)),
-        )
+        vs_listed = new_tile("vs_listed", [P, B * N], F32)
+        nc.vector.tensor_copy(vs_listed[:], listed_for_all(vs_pool[:]))
+        vs_cols = deal_out("vs_cols", vs_listed)
         part_keys(0)
+        gather_keys(1)
+        part_keys(1)
 
         def round_values(b, h, cols=slice(0, SEG)):
             nc.scalar.activation(
                 v_pool[h][:, SEG * b + cols.start : SEG * b + cols.stop], v_raw[b][h][:, cols], ACT.Copy
             )
 
-        v_turned = [new_bank("v_turned%d" % b, [P, HALVES, 2, P]) for b in range(B)]
-
         def gather_values(b, h):
             v_listed = new_tile("v_listed%d%d" % (b, h), [P, N], BF16)
             nc.scalar.activation(
-                v_listed[:].rearrange("p (g r t) -> p g t r", t=PLACES, r=RUN), listed_for(v_pool[h], b), ACT.Copy
+                v_listed[:].rearrange("p (u m a) -> p m u a", u=2, a=2),
+                listed_for(v_pool[h][:, 0 : SEG * (b + 1)], b),
+                ACT.Copy,
             )
+            return v_listed
+
+        def turn_values(bank, v_listed):
             words = v_listed[:].bitcast(F32)
             for u in range(2):
-                nc.tensor.transpose(v_turned[b][:, h, u, :], words[:, u : N // 2 : 2], identity[:])
+                nc.tensor.transpose(bank[:, u, :], words[:, P * u : P * (u + 1)], identity[:])
 
-        def group_values(b, takes_over=None):
-            grouped = new_tile("v_grouped%d" % b, [P, DV * PLACES], BF16, takes_over)
+        def group_values(grouped, bank):
             nc.scalar.copy(
-                grouped[:].bitcast(F32).rearrange("p (h f u) -> p h f u", h=HALVES, u=2),
-                v_turned[b][:].rearrange("p h u f -> p h f u"),
+                grouped.bitcast(F32).rearrange("p (h f u) -> p h f u", f=P, u=2), bank.rearrange("p h u f -> p h f u")
             )
-            return grouped
-
-        def gather_token_scales(b):
-            vs_listed = new_tile("vs_listed%d" % b, [P, N], U32)
-            nc.vector.tensor_copy(
-                vs_listed[:].rearrange("p (t g r) -> p g t r", t=PLACES, r=RUN),
-                listed_for(vs_pool[:].bitcast(U32), b),
-            )
-            return turn_rows("vs_turned%d" % b, vs_listed, PLACES)
 
         def scores(b):
             acc = new_bank("scores%d" % b, [P, PLACES, NQ])
             for place in range(PLACES):
                 cols = slice(place * P, (place + 1) * P)
-                plane_cols = slice(b * N + place * P, b * N + (place + 1) * P)
+                plane_cols = slice((place * B + b) * P, (place * B + b + 1) * P)
                 for o in range(PASSES):
                     nc.tensor.matmul_mx(
                         out=acc[:, place, :],
                         lhsT=k_codes[b][:, o, cols].bitcast(FP4X4),
-                        lhsT_scale=k_planes[o][:, plane_cols],
+                        lhsT_scale=k_planes[:, o, plane_cols],
                         rhs=q_codes[:, PASSES * b + o, :].bitcast(FP8X4),
                         rhs_scale=q_planes[:, PASSES * b + o, :],
                         start=(o == 0),
@@ -197,11 +186,11 @@ def tile_attend_sigm_kb_segb2q128n512t2048_kernel(tc, q_words, q_scales, k_words
                     )
             return acc
 
-        def sigmoid(b, acc, kb_cols, takes_over=None):
+        def sigmoid(b, acc, takes_over=None):
             prob = new_tile("prob%d" % b, [P, PLACES, NQ], F32, takes_over)
             for place in range(PLACES):
-                col = PLACES * b + place
-                nc.scalar.activation(prob[:, place, :], acc[:, place, :], ACT.Sigmoid, bias=kb_cols[:, col : col + 1])
+                bias = kb_cols[b][:, place : place + 1]
+                nc.scalar.activation(prob[:, place, :], acc[:, place, :], ACT.Sigmoid, bias=bias)
             return prob
 
         def weigh(b, prob, token_scales):
@@ -209,7 +198,7 @@ def tile_attend_sigm_kb_segb2q128n512t2048_kernel(tc, q_words, q_scales, k_words
             nc.vector.tensor_tensor(
                 w[:].rearrange("p (c i t) -> p c t i", i=4, t=PLACES),
                 prob[:].rearrange("p t (c i) -> p c t i", i=4),
-                token_scales.unsqueeze(1).unsqueeze(3).to_broadcast([P, NQ // 4, PLACES, 4]),
+                token_scales[:].unsqueeze(1).unsqueeze(3).to_broadcast([P, NQ // 4, PLACES, 4]),
                 mybir.AluOpType.mult,
             )
             return w
@@ -235,33 +224,32 @@ def tile_attend_sigm_kb_segb2q128n512t2048_kernel(tc, q_words, q_scales, k_words
             nc.scalar.activation(y[:], acc[:], ACT.Copy, scale=1.0 / 16.0)
             nc.sync.dma_start(out[b], y[:])
 
+        v_turned0 = new_bank("v_turned0", [P, HALVES, 2, P])
+        v_turned10 = new_bank("v_turned10", [P, 1, 2, P])
         round_values(0, 0, first_cols[0])
         round_values(0, 0, first_cols[1])
-        gather_values(0, 0)
+        turn_values(v_turned0[:, 0], gather_values(0, 0))
         round_values(0, 1)
-        gather_values(0, 1)
-        kb_turned = turn_rows("kb_turned", kb_listed, B * PLACES)
+        turn_values(v_turned0[:, 1], gather_values(0, 1))
         round_values(1, 0)
-        v_grouped0 = group_values(0, "v_raw10")
-        gather_values(1, 0)
+        v_grouped0 = new_tile("v_grouped0", [P, DV * PLACES], BF16, "v_raw10")
+        group_values(v_grouped0[:], v_turned0[:])
+        turn_values(v_turned10[:, 0], gather_values(1, 0))
         round_values(1, 1)
-        gather_values(1, 1)
-        kb_cols = new_tile("kb_cols", [P, B * PLACES], F32, "v_raw11")
-        nc.scalar.copy(kb_cols[:], kb_turned)
-        acc0 = scores(0)
-        gather_keys(1)
-        vs_cols0 = gather_token_scales(0)
-        part_keys(1)
-        prob0 = sigmoid(0, acc0, kb_cols, "v_pool1")
-        acc1 = scores(1)
-        vs_cols1 = gather_token_scales(1)
-        v_grouped1 = group_values(1)
-        prob1 = sigmoid(1, acc1, kb_cols, "v_listed11")
+        v_grouped1 = new_tile("v_grouped1", [P, DV * PLACES], BF16, "v_raw11")
+        group_values(v_grouped1[:, 0 : P * PLACES], v_turned10[:])
+        v_listed11 = gather_values(1, 1)
+        accs = [scores(b) for b in range(B)]
+        prob0 = sigmoid(0, accs[0], "v_pool1")
+        v_turned11 = new_bank("v_turned11", [P, 1, 2, P], "scores0")
+        turn_values(v_turned11[:, 0], v_listed11)
+        prob1 = sigmoid(1, accs[1])
+        group_values(v_grouped1[:, P * PLACES : 2 * P * PLACES], v_turned11[:])
         v_mx0 = quantize("v0", v_grouped0, DV, "kw_listed1")
-        w0 = weigh(0, prob0, vs_cols0)
-        v_mx1 = quantize("v1", v_grouped1, DV, "vs_listed1")
+        w0 = weigh(0, prob0, vs_cols[0])
         w_mx0 = quantize("w0", w0, NQ)
-        w1 = weigh(1, prob1, vs_cols1)
+        w1 = weigh(1, prob1, vs_cols[1])
+        v_mx1 = quantize("v1", v_grouped1, DV)
         w_mx1 = quantize("w1", w1, NQ)
         finish(0, w_mx0, v_mx0, None)
-        finish(1, w_mx1, v_mx1, "kb_turned")
+        finish(1, w_mx1, v_mx1, None)

@@ -49,32 +49,36 @@ def tile_attend_sigm_kb_segb2q128n512t2048_kernel(tc, q_words, q_scales, k_words
         def listed_for(window, b):
             return window.indirect(offsets[:, b * LIST_COLS : (b + 1) * LIST_COLS])
 
-        ks_pool = new_tile("ks_pool", [P, T], U8)
+        ks_pool = new_tile("ks_pool", [P, T + 4], U8)
         nc.vector.memset(ks_pool[:].bitcast(I32), 0)
-        warm_in = new_tile("warm_in", [P, 8], F32)
+        warm_in = new_tile("warm_in", [P, 1], F32)
         nc.vector.memset(warm_in[:], 0.0)
-        kb_pool = new_tile("kb_pool", [P, T], F32)
+        kb_pool = new_tile("kb_pool", [P, T + 1], F32)
         nc.vector.memset(kb_pool[:].bitcast(I32), 0)
         vs_pool = new_tile("vs_pool", [P, T], F32)
-        nc.vector.memset(vs_pool[:].bitcast(I32), 0)
+        nc.gpsimd.memset(vs_pool[:].bitcast(I32), 0)
+        identity = new_tile("identity", [P, P], F32)
+        make_identity(nc, identity[:])
         q_planes = new_tile("q_planes", [P, B * PASSES, NQ], U8)
         nc.gpsimd.memset(q_planes[:].rearrange("p g q -> p (g q)").bitcast(I32), 0)
         k_planes = new_tile("k_planes", [P, PASSES, B * N], U8)
         nc.gpsimd.memset(k_planes[:].rearrange("p o n -> p (o n)").bitcast(I32), 0)
-        identity = new_tile("identity", [P, P], F32)
-        make_identity(nc, identity[:])
 
         v_raw = [[new_tile("v_raw%d%d" % (b, h), [P, SEG], F32) for h in range(HALVES)] for b in range(B)]
-        v_pool = [new_tile("v_pool%d" % h, [P, T], BF16) for h in range(HALVES)]
+        v_pool_first = new_tile("v_pool_first", [P, SEG], BF16)
+        v_pool_mid = new_tile("v_pool_mid", [P, T], BF16)
+        v_pool_last = new_tile("v_pool_last", [P, T], BF16)
+        nc.gpsimd.memset(v_pool_last[:, stretch(0)].bitcast(I32), 0)
+        v_pool = [[v_pool_first, v_pool_mid], [v_pool_mid, v_pool_last]]
 
         def load_values(b, h, cols=slice(0, SEG)):
             nc.sync.dma_start(v_raw[b][h][:, cols], vT[P * h : P * (h + 1), SEG * b + cols.start : SEG * b + cols.stop])
 
         first_cols = [slice(0, SEG // 2), slice(SEG // 2, SEG)]
-        nc.sync.dma_start(ks_pool[0:P:ROW_STEP, :].bitcast(I32), k_scales.rearrange("o f t -> (o f) t").bitcast(I32))
+        nc.sync.dma_start(ks_pool[0:P:ROW_STEP, 0:T].bitcast(I32), k_scales.rearrange("o f t -> (o f) t").bitcast(I32))
         load_values(0, 0, first_cols[0])
 
-        warm_out = new_tile("warm_out", [P, 8], F32)
+        warm_out = new_tile("warm_out", [P, 1], F32)
         nc.scalar.activation(warm_out[:], warm_in[:], ACT.Sigmoid)
 
         kw_pool = new_tile("kw_pool", [P, T], U32)
@@ -86,7 +90,7 @@ def tile_attend_sigm_kb_segb2q128n512t2048_kernel(tc, q_words, q_scales, k_words
             )
 
         load_values(0, 0, first_cols[1])
-        nc.sync.dma_start(kb_pool[0:1, :], kb[0:1, :])
+        nc.sync.dma_start(kb_pool[0:1, 0:T], kb[0:1, :])
         load_values(0, 1)
         load_keys(0)
         load_values(1, 0)
@@ -102,7 +106,7 @@ def tile_attend_sigm_kb_segb2q128n512t2048_kernel(tc, q_words, q_scales, k_words
             )
 
         ks_listed = new_tile("ks_listed", [P, B * N], U8)
-        nc.vector.tensor_copy(ks_listed[:], listed_for_all(ks_pool[:]))
+        nc.vector.tensor_copy(ks_listed[:], listed_for_all(ks_pool[:, 0:T]))
         ks_placed = new_tile("ks_placed", [P, B * N], U8)
         nc.vector.tensor_copy(
             ks_placed[:].rearrange("p (t m) -> p t m", t=PLACES), ks_listed[:].rearrange("p (m t) -> p t m", t=PLACES)
@@ -122,7 +126,7 @@ def tile_attend_sigm_kb_segb2q128n512t2048_kernel(tc, q_words, q_scales, k_words
             return cols
 
         kb_listed = new_tile("kb_listed", [P, B * N], F32)
-        nc.vector.tensor_copy(kb_listed[:], listed_for_all(kb_pool[:]))
+        nc.vector.tensor_copy(kb_listed[:], listed_for_all(kb_pool[:, 0:T]))
         kb_cols = deal_out("kb_cols", kb_listed)
 
         kw_listed = [new_tile("kw_listed%d" % b, [P, N], U32) for b in range(B)]
@@ -147,22 +151,18 @@ def tile_attend_sigm_kb_segb2q128n512t2048_kernel(tc, q_words, q_scales, k_words
 
         def round_values(b, h, cols=slice(0, SEG)):
             nc.scalar.activation(
-                v_pool[h][:, SEG * b + cols.start : SEG * b + cols.stop], v_raw[b][h][:, cols], ACT.Copy
+                v_pool[b][h][:, SEG * b + cols.start : SEG * b + cols.stop], v_raw[b][h][:, cols], ACT.Copy
             )
 
-        def gather_values(b, h):
-            v_listed = new_tile("v_listed%d%d" % (b, h), [P, N], BF16)
-            nc.scalar.activation(
-                v_listed[:].rearrange("p (u m a) -> p m u a", u=2, a=2),
-                listed_for(v_pool[h][:, 0 : SEG * (b + 1)], b),
-                ACT.Copy,
-            )
+        def gather_values(name, listed, count):
+            v_listed = new_tile(name, [P, count], BF16)
+            nc.scalar.activation(v_listed[:], listed, ACT.Copy)
             return v_listed
 
         def turn_values(bank, v_listed):
-            words = v_listed[:].bitcast(F32)
+            words = v_listed.bitcast(F32)
             for u in range(2):
-                nc.tensor.transpose(bank[:, u, :], words[:, P * u : P * (u + 1)], identity[:])
+                nc.tensor.transpose(bank[:, u, :], words[:, u : N // 2 : 2], identity[:])
 
         def group_values(grouped, bank):
             nc.scalar.copy(
@@ -228,21 +228,23 @@ def tile_attend_sigm_kb_segb2q128n512t2048_kernel(tc, q_words, q_scales, k_words
         v_turned10 = new_bank("v_turned10", [P, 1, 2, P])
         round_values(0, 0, first_cols[0])
         round_values(0, 0, first_cols[1])
-        turn_values(v_turned0[:, 0], gather_values(0, 0))
+        v_listed00 = gather_values("v_listed00", listed_for(v_pool_first[:], 0), N)
+        turn_values(v_turned0[:, 0], v_listed00[:])
         round_values(0, 1)
-        turn_values(v_turned0[:, 1], gather_values(0, 1))
         round_values(1, 0)
-        v_grouped0 = new_tile("v_grouped0", [P, DV * PLACES], BF16, "v_raw10")
-        group_values(v_grouped0[:], v_turned0[:])
-        turn_values(v_turned10[:, 0], gather_values(1, 0))
+        v_listed_mid = gather_values("v_listed_mid", listed_for_all(v_pool_mid[:]), B * N)
+        turn_values(v_turned0[:, 1], v_listed_mid[:, 0:N])
+        turn_values(v_turned10[:, 0], v_listed_mid[:, N : 2 * N])
         round_values(1, 1)
-        v_grouped1 = new_tile("v_grouped1", [P, DV * PLACES], BF16, "v_raw11")
-        group_values(v_grouped1[:, 0 : P * PLACES], v_turned10[:])
-        v_listed11 = gather_values(1, 1)
+        v_grouped0 = new_tile("v_grouped0", [P, DV * PLACES], BF16, "v_raw11")
+        group_values(v_grouped0[:], v_turned0[:])
+        v_listed11 = gather_values("v_listed11", listed_for(v_pool_last[:], 1), N)
+        v_grouped1 = new_tile("v_grouped1", [P, DV * PLACES], BF16, "v_pool_last")
         accs = [scores(b) for b in range(B)]
-        prob0 = sigmoid(0, accs[0], "v_pool1")
+        prob0 = sigmoid(0, accs[0])
+        group_values(v_grouped1[:, 0 : P * PLACES], v_turned10[:])
         v_turned11 = new_bank("v_turned11", [P, 1, 2, P], "scores0")
-        turn_values(v_turned11[:, 0], v_listed11)
+        turn_values(v_turned11[:, 0], v_listed11[:])
         prob1 = sigmoid(1, accs[1])
         group_values(v_grouped1[:, P * PLACES : 2 * P * PLACES], v_turned11[:])
         v_mx0 = quantize("v0", v_grouped0, DV, "kw_listed1")

@@ -65,11 +65,7 @@ def tile_attend_sigm_kb_segb2q128n512t2048_kernel(tc, q_words, q_scales, k_words
         nc.gpsimd.memset(k_planes[:].rearrange("p o n -> p (o n)").bitcast(I32), 0)
 
         v_raw = [[new_tile("v_raw%d%d" % (b, h), [P, SEG], F32) for h in range(HALVES)] for b in range(B)]
-        v_pool_first = new_tile("v_pool_first", [P, SEG], BF16)
-        v_pool_mid = new_tile("v_pool_mid", [P, T], BF16)
-        v_pool_last = new_tile("v_pool_last", [P, T], BF16)
-        nc.gpsimd.memset(v_pool_last[:, stretch(0)].bitcast(I32), 0)
-        v_pool = [[v_pool_first, v_pool_mid], [v_pool_mid, v_pool_last]]
+        v_pool = [new_tile("v_pool%d" % h, [P, T], BF16) for h in range(HALVES)]
 
         def load_values(b, h, cols=slice(0, SEG)):
             nc.sync.dma_start(v_raw[b][h][:, cols], vT[P * h : P * (h + 1), SEG * b + cols.start : SEG * b + cols.stop])
@@ -90,13 +86,13 @@ def tile_attend_sigm_kb_segb2q128n512t2048_kernel(tc, q_words, q_scales, k_words
             )
 
         load_values(0, 0, first_cols[1])
-        nc.sync.dma_start(kb_pool[0:1, 0:T], kb[0:1, :])
-        load_values(0, 1)
-        load_keys(0)
         load_values(1, 0)
+        nc.sync.dma_start(kb_pool[0:1, 0:T], kb[0:1, :])
+        load_keys(0)
+        load_values(0, 1)
         nc.sync.dma_start(vs_pool[0:1, :], vs[0:1, :])
-        load_keys(1)
         load_values(1, 1)
+        load_keys(1)
         q_codes = new_tile("q_codes", [P, B * PASSES, NQ], U32)
         nc.sync.dma_start(q_codes[:].bitcast(I32), q_words.rearrange("b o p q c -> p (b o) (q c)").bitcast(I32))
         qs_rows = q_scales.rearrange("b o f q -> f (b o) q")
@@ -151,7 +147,7 @@ def tile_attend_sigm_kb_segb2q128n512t2048_kernel(tc, q_words, q_scales, k_words
 
         def round_values(b, h, cols=slice(0, SEG)):
             nc.scalar.activation(
-                v_pool[b][h][:, SEG * b + cols.start : SEG * b + cols.stop], v_raw[b][h][:, cols], ACT.Copy
+                v_pool[h][:, SEG * b + cols.start : SEG * b + cols.stop], v_raw[b][h][:, cols], ACT.Copy
             )
 
         def gather_values(name, listed, count):
@@ -164,19 +160,23 @@ def tile_attend_sigm_kb_segb2q128n512t2048_kernel(tc, q_words, q_scales, k_words
             for u in range(2):
                 nc.tensor.transpose(bank[:, u, :], words[:, u : N // 2 : 2], identity[:])
 
-        def group_values(grouped, bank):
-            nc.scalar.copy(
+        def group_values(grouped, bank, copy=nc.scalar.copy):
+            copy(
                 grouped.bitcast(F32).rearrange("p (h f u) -> p h f u", f=P, u=2), bank.rearrange("p h u f -> p h f u")
             )
 
         def scores(b):
-            acc = new_bank("scores%d" % b, [P, PLACES, NQ])
+            if b == 0:
+                bank = new_bank("scores0", [P, PLACES, NQ])
+                acc = [bank[:, place, :] for place in range(PLACES)]
+            else:
+                acc = [new_bank("scores1%d" % place, [P, NQ])[:] for place in range(PLACES)]
             for place in range(PLACES):
                 cols = slice(place * P, (place + 1) * P)
                 plane_cols = slice((place * B + b) * P, (place * B + b + 1) * P)
                 for o in range(PASSES):
                     nc.tensor.matmul_mx(
-                        out=acc[:, place, :],
+                        out=acc[place],
                         lhsT=k_codes[b][:, o, cols].bitcast(FP4X4),
                         lhsT_scale=k_planes[:, o, plane_cols],
                         rhs=q_codes[:, PASSES * b + o, :].bitcast(FP8X4),
@@ -190,7 +190,7 @@ def tile_attend_sigm_kb_segb2q128n512t2048_kernel(tc, q_words, q_scales, k_words
             prob = new_tile("prob%d" % b, [P, PLACES, NQ], F32, takes_over)
             for place in range(PLACES):
                 bias = kb_cols[b][:, place : place + 1]
-                nc.scalar.activation(prob[:, place, :], acc[:, place, :], ACT.Sigmoid, bias=bias)
+                nc.scalar.activation(prob[:, place, :], acc[place], ACT.Sigmoid, bias=bias)
             return prob
 
         def weigh(b, prob, token_scales):
@@ -209,49 +209,55 @@ def tile_attend_sigm_kb_segb2q128n512t2048_kernel(tc, q_words, q_scales, k_words
             nc.vector.quantize_mx(out=codes[:].bitcast(FP8X4), scales=scales[:], in_=grouped[:])
             return codes, scales
 
-        def finish(b, w_mx, v_mx, takes_over):
-            acc = new_bank("y_acc%d" % b, [P, DV], takes_over)
+        def finish(b, w_mx, v_mx, cols, bank, on_vector=False):
+            width = cols.stop - cols.start
+            acc = new_bank("y_acc%d_%d" % (b, cols.start), [P, width], bank)
             nc.tensor.matmul_mx(
                 out=acc[:],
                 lhsT=w_mx[0][:].bitcast(FP8X4),
                 lhsT_scale=w_mx[1][:],
-                rhs=v_mx[0][:].bitcast(FP8X4),
-                rhs_scale=v_mx[1][:],
+                rhs=v_mx[0][:, cols].bitcast(FP8X4),
+                rhs_scale=v_mx[1][:, cols],
                 start=True,
                 stop=True,
             )
-            y = new_tile("y%d" % b, [P, DV], F32)
-            nc.scalar.activation(y[:], acc[:], ACT.Copy, scale=1.0 / 16.0)
-            nc.sync.dma_start(out[b], y[:])
+            y = new_tile("y%d_%d" % (b, cols.start), [P, width], F32)
+            if on_vector:
+                nc.vector.tensor_scalar_mul(y[:], acc[:], 1.0 / 16.0)
+                nc.sync.dma_start(out[b][:, cols], y[:])
+            else:
+                nc.scalar.activation(y[:], acc[:], ACT.Copy, scale=1.0 / 16.0)
+                (nc.scalar if b else nc.sync).dma_start(out[b][:, cols], y[:])
 
         v_turned0 = new_bank("v_turned0", [P, HALVES, 2, P])
         v_turned10 = new_bank("v_turned10", [P, 1, 2, P])
         round_values(0, 0, first_cols[0])
         round_values(0, 0, first_cols[1])
-        v_listed00 = gather_values("v_listed00", listed_for(v_pool_first[:], 0), N)
-        turn_values(v_turned0[:, 0], v_listed00[:])
-        round_values(0, 1)
         round_values(1, 0)
-        v_listed_mid = gather_values("v_listed_mid", listed_for_all(v_pool_mid[:]), B * N)
-        turn_values(v_turned0[:, 1], v_listed_mid[:, 0:N])
-        turn_values(v_turned10[:, 0], v_listed_mid[:, N : 2 * N])
+        v_listed0 = gather_values("v_listed0", listed_for_all(v_pool[0][:]), B * N)
+        turn_values(v_turned0[:, 0], v_listed0[:, 0:N])
+        turn_values(v_turned10[:, 0], v_listed0[:, N : 2 * N])
+        round_values(0, 1)
         round_values(1, 1)
-        v_grouped0 = new_tile("v_grouped0", [P, DV * PLACES], BF16, "v_raw11")
+        v_listed01 = gather_values("v_listed01", listed_for(v_pool[1][:], 0), N)
+        turn_values(v_turned0[:, 1], v_listed01[:])
+        v_listed11 = gather_values("v_listed11", listed_for(v_pool[1][:], 1), N)
+        v_grouped0 = new_tile("v_grouped0", [P, DV * PLACES], BF16, "v_pool1")
         group_values(v_grouped0[:], v_turned0[:])
-        v_listed11 = gather_values("v_listed11", listed_for(v_pool_last[:], 1), N)
-        v_grouped1 = new_tile("v_grouped1", [P, DV * PLACES], BF16, "v_pool_last")
+        v_grouped1 = new_tile("v_grouped1", [P, DV * PLACES], BF16, "kw_listed1")
         accs = [scores(b) for b in range(B)]
         prob0 = sigmoid(0, accs[0])
-        group_values(v_grouped1[:, 0 : P * PLACES], v_turned10[:])
         v_turned11 = new_bank("v_turned11", [P, 1, 2, P], "scores0")
         turn_values(v_turned11[:, 0], v_listed11[:])
         prob1 = sigmoid(1, accs[1])
         group_values(v_grouped1[:, P * PLACES : 2 * P * PLACES], v_turned11[:])
-        v_mx0 = quantize("v0", v_grouped0, DV, "kw_listed1")
+        v_mx0 = quantize("v0", v_grouped0, DV, "kw_pool")
+        group_values(v_grouped1[:, 0 : P * PLACES], v_turned10[:], nc.vector.tensor_copy)
         w0 = weigh(0, prob0, vs_cols[0])
         w_mx0 = quantize("w0", w0, NQ)
         w1 = weigh(1, prob1, vs_cols[1])
         v_mx1 = quantize("v1", v_grouped1, DV)
         w_mx1 = quantize("w1", w1, NQ)
-        finish(0, w_mx0, v_mx0, None)
-        finish(1, w_mx1, v_mx1, None)
+        finish(0, w_mx0, v_mx0, slice(0, DV), "v_turned0")
+        finish(1, w_mx1, v_mx1, slice(0, P), "v_turned10")
+        finish(1, w_mx1, v_mx1, slice(P, DV), None, True)

@@ -55,12 +55,12 @@ def tile_attend_sigm_kb_segb2q128n512t2048_kernel(tc, q_words, q_scales, k_words
         nc.vector.memset(warm_in[:], 0.0)
         kb_pool = new_tile("kb_pool", [P, T + 1], F32)
         nc.vector.memset(kb_pool[:].bitcast(I32), 0)
+        q_planes = new_tile("q_planes", [P, B * PASSES, NQ], U8)
+        nc.gpsimd.memset(q_planes[:].rearrange("p g q -> p (g q)").bitcast(I32), 0)
         vs_pool = new_tile("vs_pool", [P, T], F32)
         nc.gpsimd.memset(vs_pool[:].bitcast(I32), 0)
         identity = new_tile("identity", [P, P], F32)
         make_identity(nc, identity[:])
-        q_planes = new_tile("q_planes", [P, B * PASSES, NQ], U8)
-        nc.gpsimd.memset(q_planes[:].rearrange("p g q -> p (g q)").bitcast(I32), 0)
         k_planes = new_tile("k_planes", [P, PASSES, B * N], U8)
         nc.gpsimd.memset(k_planes[:].rearrange("p o n -> p (o n)").bitcast(I32), 0)
 
@@ -73,6 +73,12 @@ def tile_attend_sigm_kb_segb2q128n512t2048_kernel(tc, q_words, q_scales, k_words
         first_cols = [slice(0, SEG // 2), slice(SEG // 2, SEG)]
         nc.sync.dma_start(ks_pool[0:P:ROW_STEP, 0:T].bitcast(I32), k_scales.rearrange("o f t -> (o f) t").bitcast(I32))
         load_values(0, 0, first_cols[0])
+
+        qs_rows = q_scales.rearrange("b o f q -> f (b o) q")
+        for c in range(4):
+            nc.scalar.dma_start(
+                q_planes[32 * c : 32 * c + 4, :, :].bitcast(I32), qs_rows[4 * c : 4 * c + 4, :, :].bitcast(I32)
+            )
 
         warm_out = new_tile("warm_out", [P, 1], F32)
         nc.scalar.activation(warm_out[:], warm_in[:], ACT.Sigmoid)
@@ -92,14 +98,6 @@ def tile_attend_sigm_kb_segb2q128n512t2048_kernel(tc, q_words, q_scales, k_words
         load_values(0, 1)
         nc.sync.dma_start(vs_pool[0:1, :], vs[0:1, :])
         load_values(1, 1)
-        load_keys(1)
-        q_codes = new_tile("q_codes", [P, B * PASSES, NQ], U32)
-        nc.sync.dma_start(q_codes[:].bitcast(I32), q_words.rearrange("b o p q c -> p (b o) (q c)").bitcast(I32))
-        qs_rows = q_scales.rearrange("b o f q -> f (b o) q")
-        for c in range(4):
-            nc.sync.dma_start(
-                q_planes[32 * c : 32 * c + 4, :, :].bitcast(I32), qs_rows[4 * c : 4 * c + 4, :, :].bitcast(I32)
-            )
 
         ks_listed = new_tile("ks_listed", [P, B * N], U8)
         nc.vector.tensor_copy(ks_listed[:], listed_for_all(ks_pool[:, 0:T]))
@@ -114,6 +112,9 @@ def tile_attend_sigm_kb_segb2q128n512t2048_kernel(tc, q_words, q_scales, k_words
                     k_planes[r:P:32, o, :].bitcast(I32),
                     ks_placed[first : first + 3 * 4 * ROW_STEP + 1 : 4 * ROW_STEP, :].bitcast(I32),
                 )
+        load_keys(1)
+        q_codes = new_tile("q_codes", [P, B * PASSES, NQ], U32)
+        nc.sync.dma_start(q_codes[:].bitcast(I32), q_words.rearrange("b o p q c -> p (b o) (q c)").bitcast(I32))
 
         def deal_out(name, listed):
             cols = [new_tile("%s%d" % (name, b), [P, PLACES], F32) for b in range(B)]
@@ -246,7 +247,7 @@ def tile_attend_sigm_kb_segb2q128n512t2048_kernel(tc, q_words, q_scales, k_words
         group_values(v_grouped0[:], v_turned0[:])
         v_grouped1 = new_tile("v_grouped1", [P, DV * PLACES], BF16, "kw_listed1")
         accs = [scores(b) for b in range(B)]
-        prob0 = sigmoid(0, accs[0])
+        prob0 = sigmoid(0, accs[0], "v_listed01")
         v_turned11 = new_bank("v_turned11", [P, 1, 2, P], "scores0")
         turn_values(v_turned11[:, 0], v_listed11[:])
         prob1 = sigmoid(1, accs[1])

@@ -22,7 +22,8 @@ SEG = T // B
 LIST_COLS = N // 16
 PASSES = D // (P * PLACES)
 HALVES = DV // P
-ROW_STEP = 4
+KS_FIRST = P - PASSES * 16
+ROW = P - 1
 
 
 def tile_attend_sigm_kb_segb2q128n512t2048_kernel(tc, q_words, q_scales, k_words, k_scales, vT, vs, kb, offs, out):
@@ -49,16 +50,16 @@ def tile_attend_sigm_kb_segb2q128n512t2048_kernel(tc, q_words, q_scales, k_words
         def listed_for(window, b):
             return window.indirect(offsets[:, b * LIST_COLS : (b + 1) * LIST_COLS])
 
-        ks_pool = new_tile("ks_pool", [P, T + 4], U8)
-        nc.vector.memset(ks_pool[:].bitcast(I32), 0)
+        ks_pool = new_tile("ks_pool", [P, T], U8)
+        nc.gpsimd.memset(ks_pool[0:KS_FIRST, :].bitcast(I32), 0)
         warm_in = new_tile("warm_in", [P, 1], F32)
-        nc.vector.memset(warm_in[:], 0.0)
+        nc.gpsimd.memset(warm_in[:], 0.0)
         kb_pool = new_tile("kb_pool", [P, T + 1], F32)
-        nc.vector.memset(kb_pool[:].bitcast(I32), 0)
+        nc.vector.memset(kb_pool[0:ROW, :].bitcast(I32), 0)
         q_planes = new_tile("q_planes", [P, B * PASSES, NQ], U8)
         nc.gpsimd.memset(q_planes[:].rearrange("p g q -> p (g q)").bitcast(I32), 0)
         vs_pool = new_tile("vs_pool", [P, T], F32)
-        nc.gpsimd.memset(vs_pool[:].bitcast(I32), 0)
+        nc.gpsimd.memset(vs_pool[0:ROW, :].bitcast(I32), 0)
         identity = new_tile("identity", [P, P], F32)
         make_identity(nc, identity[:])
         k_planes = new_tile("k_planes", [P, PASSES, B * N], U8)
@@ -71,7 +72,7 @@ def tile_attend_sigm_kb_segb2q128n512t2048_kernel(tc, q_words, q_scales, k_words
             nc.sync.dma_start(v_raw[b][h][:, cols], vT[P * h : P * (h + 1), SEG * b + cols.start : SEG * b + cols.stop])
 
         first_cols = [slice(0, SEG // 2), slice(SEG // 2, SEG)]
-        nc.sync.dma_start(ks_pool[0:P:ROW_STEP, 0:T].bitcast(I32), k_scales.rearrange("o f t -> (o f) t").bitcast(I32))
+        nc.sync.dma_start(ks_pool[KS_FIRST:P, :].bitcast(I32), k_scales.rearrange("o f t -> (o f) t").bitcast(I32))
         load_values(0, 0, first_cols[0])
 
         qs_rows = q_scales.rearrange("b o f q -> f (b o) q")
@@ -92,25 +93,25 @@ def tile_attend_sigm_kb_segb2q128n512t2048_kernel(tc, q_words, q_scales, k_words
             )
 
         load_values(0, 0, first_cols[1])
-        load_values(1, 0)
-        nc.sync.dma_start(kb_pool[0:1, 0:T], kb[0:1, :])
+        load_values(1, 0, first_cols[0])
+        load_values(1, 0, first_cols[1])
+        nc.sync.dma_start(kb_pool[ROW:P, 0:T], kb[0:1, :])
         load_keys(0)
         load_values(0, 1)
-        nc.sync.dma_start(vs_pool[0:1, :], vs[0:1, :])
+        nc.sync.dma_start(vs_pool[ROW:P, :], vs[0:1, :])
         load_values(1, 1)
 
         ks_listed = new_tile("ks_listed", [P, B * N], U8)
-        nc.vector.tensor_copy(ks_listed[:], listed_for_all(ks_pool[:, 0:T]))
+        nc.vector.tensor_copy(ks_listed[:], listed_for_all(ks_pool[:]))
         ks_placed = new_tile("ks_placed", [P, B * N], U8)
         nc.vector.tensor_copy(
             ks_placed[:].rearrange("p (t m) -> p t m", t=PLACES), ks_listed[:].rearrange("p (m t) -> p t m", t=PLACES)
         )
         for o in reversed(range(PASSES)):
-            for r in range(4):
-                first = ROW_STEP * (16 * o + r)
+            for c in range(4):
+                first = KS_FIRST + 16 * o + 4 * c
                 nc.sync.dma_start(
-                    k_planes[r:P:32, o, :].bitcast(I32),
-                    ks_placed[first : first + 3 * 4 * ROW_STEP + 1 : 4 * ROW_STEP, :].bitcast(I32),
+                    k_planes[32 * c : 32 * c + 4, o, :].bitcast(I32), ks_placed[first : first + 4, :].bitcast(I32)
                 )
         load_keys(1)
         q_codes = new_tile("q_codes", [P, B * PASSES, NQ], U32)
@@ -119,7 +120,7 @@ def tile_attend_sigm_kb_segb2q128n512t2048_kernel(tc, q_words, q_scales, k_words
         def deal_out(name, listed):
             cols = [new_tile("%s%d" % (name, b), [P, PLACES], F32) for b in range(B)]
             for b in range(B):
-                nc.sync.dma_start(cols[b][:], listed[0:1, N * b : N * (b + 1)].rearrange("r (m t) -> r m t", t=PLACES))
+                nc.sync.dma_start(cols[b][:], listed[ROW:P, N * b : N * (b + 1)].rearrange("r (m t) -> r m t", t=PLACES))
             return cols
 
         kb_listed = new_tile("kb_listed", [P, B * N], F32)
@@ -234,7 +235,8 @@ def tile_attend_sigm_kb_segb2q128n512t2048_kernel(tc, q_words, q_scales, k_words
         v_turned10 = new_bank("v_turned10", [P, 1, 2, P])
         round_values(0, 0, first_cols[0])
         round_values(0, 0, first_cols[1])
-        round_values(1, 0)
+        round_values(1, 0, first_cols[0])
+        round_values(1, 0, first_cols[1])
         v_listed0 = gather_values("v_listed0", listed_for_all(v_pool[0][:]), B * N)
         turn_values(v_turned0[:, 0], v_listed0[:, 0:N])
         turn_values(v_turned10[:, 0], v_listed0[:, N : 2 * N])

@@ -73,13 +73,8 @@ def tile_attend_sigm_kb_segb2q128n512t2048_kernel(tc, q_words, q_scales, k_words
 
         first_cols = [slice(0, SEG // 2), slice(SEG // 2, SEG)]
         nc.sync.dma_start(ks_pool[KS_FIRST:P, :].bitcast(I32), k_scales.rearrange("o f t -> (o f) t").bitcast(I32))
+        nc.sync.dma_start(kb_pool[ROW:P, 0:T], kb[0:1, :])
         load_values(0, 0, first_cols[0])
-
-        qs_rows = q_scales.rearrange("b o f q -> f (b o) q")
-        for c in range(4):
-            nc.scalar.dma_start(
-                q_planes[32 * c : 32 * c + 4, :, :].bitcast(I32), qs_rows[4 * c : 4 * c + 4, :, :].bitcast(I32)
-            )
 
         warm_out = new_tile("warm_out", [P, 1], F32)
         nc.scalar.activation(warm_out[:], warm_in[:], ACT.Sigmoid)
@@ -95,45 +90,38 @@ def tile_attend_sigm_kb_segb2q128n512t2048_kernel(tc, q_words, q_scales, k_words
         load_values(0, 0, first_cols[1])
         load_values(1, 0, first_cols[0])
         load_values(1, 0, first_cols[1])
-        nc.sync.dma_start(kb_pool[ROW:P, 0:T], kb[0:1, :])
         load_keys(0)
-        load_values(0, 1)
         nc.sync.dma_start(vs_pool[ROW:P, :], vs[0:1, :])
+        load_values(0, 1)
         load_values(1, 1)
-
-        ks_listed = new_tile("ks_listed", [P, B * N], U8)
-        nc.vector.tensor_copy(ks_listed[:], listed_for_all(ks_pool[:]))
-        ks_placed = new_tile("ks_placed", [P, B * N], U8)
-        nc.vector.tensor_copy(
-            ks_placed[:].rearrange("p (t m) -> p t m", t=PLACES), ks_listed[:].rearrange("p (m t) -> p t m", t=PLACES)
-        )
-        for o in reversed(range(PASSES)):
-            for c in range(4):
-                first = KS_FIRST + 16 * o + 4 * c
-                nc.sync.dma_start(
-                    k_planes[32 * c : 32 * c + 4, o, :].bitcast(I32), ks_placed[first : first + 4, :].bitcast(I32)
-                )
         load_keys(1)
         q_codes = new_tile("q_codes", [P, B * PASSES, NQ], U32)
         nc.sync.dma_start(q_codes[:].bitcast(I32), q_words.rearrange("b o p q c -> p (b o) (q c)").bitcast(I32))
+        qs_rows = q_scales.rearrange("b o f q -> f (b o) q")
+        for c in range(4):
+            nc.sync.dma_start(
+                q_planes[32 * c : 32 * c + 4, :, :].bitcast(I32), qs_rows[4 * c : 4 * c + 4, :, :].bitcast(I32)
+            )
 
+        ks_listed = new_tile("ks_listed", [P, B * N], U8)
+        nc.vector.tensor_copy(ks_listed[:], listed_for_all(ks_pool[:]))
+        kb_listed = new_tile("kb_listed", [P, B * N], F32)
+        nc.vector.tensor_copy(kb_listed[:], listed_for_all(kb_pool[:, 0:T]))
         def deal_out(name, listed):
             cols = [new_tile("%s%d" % (name, b), [P, PLACES], F32) for b in range(B)]
             for b in range(B):
                 nc.sync.dma_start(cols[b][:], listed[ROW:P, N * b : N * (b + 1)].rearrange("r (m t) -> r m t", t=PLACES))
             return cols
 
-        kb_listed = new_tile("kb_listed", [P, B * N], F32)
-        nc.vector.tensor_copy(kb_listed[:], listed_for_all(kb_pool[:, 0:T]))
-        kb_cols = deal_out("kb_cols", kb_listed)
 
         kw_listed = [new_tile("kw_listed%d" % b, [P, N], U32) for b in range(B)]
-        k_codes = [new_tile("k_codes%d" % b, [P, PASSES, N], U16) for b in range(B)]
+        k_codes = [None, None]
 
         def gather_keys(b):
             nc.vector.tensor_copy(kw_listed[b][:], listed_for(kw_pool[:, 0 : SEG * (b + 1)], b))
 
-        def part_keys(b):
+        def part_keys(b, takes_over=None):
+            k_codes[b] = new_tile("k_codes%d" % b, [P, PASSES, N], U16, takes_over)
             nc.vector.tensor_copy(
                 k_codes[b][:].rearrange("p o (t x y) -> p o x t y", t=PLACES, y=4),
                 kw_listed[b][:].bitcast(U16).rearrange("p (x y t o) -> p o x t y", t=PLACES, y=4, o=PASSES),
@@ -142,10 +130,6 @@ def tile_attend_sigm_kb_segb2q128n512t2048_kernel(tc, q_words, q_scales, k_words
         gather_keys(0)
         vs_listed = new_tile("vs_listed", [P, B * N], F32)
         nc.vector.tensor_copy(vs_listed[:], listed_for_all(vs_pool[:]))
-        vs_cols = deal_out("vs_cols", vs_listed)
-        part_keys(0)
-        gather_keys(1)
-        part_keys(1)
 
         def round_values(b, h, cols=slice(0, SEG)):
             nc.scalar.activation(
@@ -242,21 +226,38 @@ def tile_attend_sigm_kb_segb2q128n512t2048_kernel(tc, q_words, q_scales, k_words
         turn_values(v_turned10[:, 0], v_listed0[:, N : 2 * N])
         round_values(0, 1)
         round_values(1, 1)
+        ks_placed = new_tile("ks_placed", [P, B * N], U8, "v_raw10")
+        nc.vector.tensor_copy(
+            ks_placed[:].rearrange("p (t m) -> p t m", t=PLACES), ks_listed[:].rearrange("p (m t) -> p t m", t=PLACES)
+        )
+        for o in reversed(range(PASSES)):
+            for c in range(4):
+                first = KS_FIRST + 16 * o + 4 * c
+                nc.sync.dma_start(
+                    k_planes[32 * c : 32 * c + 4, o, :].bitcast(I32), ks_placed[first : first + 4, :].bitcast(I32)
+                )
+
+        kb_cols = deal_out("kb_cols", kb_listed)
+        vs_cols = deal_out("vs_cols", vs_listed)
+        part_keys(0, "v_raw01")
+        gather_keys(1)
+        part_keys(1)
+
         v_listed01 = gather_values("v_listed01", listed_for(v_pool[1][:], 0), N)
         turn_values(v_turned0[:, 1], v_listed01[:])
         v_listed11 = gather_values("v_listed11", listed_for(v_pool[1][:], 1), N)
         v_grouped0 = new_tile("v_grouped0", [P, DV * PLACES], BF16, "v_pool1")
         group_values(v_grouped0[:], v_turned0[:])
-        v_grouped1 = new_tile("v_grouped1", [P, DV * PLACES], BF16, "kw_listed1")
+        v_grouped1 = new_tile("v_grouped1", [P, DV * PLACES], BF16, "kw_pool")
         accs = [scores(b) for b in range(B)]
         prob0 = sigmoid(0, accs[0], "v_listed01")
         v_turned11 = new_bank("v_turned11", [P, 1, 2, P], "scores0")
         turn_values(v_turned11[:, 0], v_listed11[:])
         prob1 = sigmoid(1, accs[1])
         group_values(v_grouped1[:, P * PLACES : 2 * P * PLACES], v_turned11[:])
-        v_mx0 = quantize("v0", v_grouped0, DV, "kw_pool")
         group_values(v_grouped1[:, 0 : P * PLACES], v_turned10[:], nc.vector.tensor_copy)
         w0 = weigh(0, prob0, vs_cols[0])
+        v_mx0 = quantize("v0", v_grouped0, DV, "vs_listed")
         w_mx0 = quantize("w0", w0, NQ)
         w1 = weigh(1, prob1, vs_cols[1])
         v_mx1 = quantize("v1", v_grouped1, DV)

@@ -56,24 +56,20 @@ def tile_attend_sigm_kb_segb2q128n512t2048_kernel(tc, q_words, q_scales, k_words
         nc.gpsimd.memset(warm_in[:], 0.0)
         kb_pool = new_tile("kb_pool", [P, T + 1], F32)
         nc.vector.memset(kb_pool[0:ROW, :].bitcast(I32), 0)
-        q_planes = new_tile("q_planes", [P, B * PASSES, NQ], U8)
-        nc.gpsimd.memset(q_planes[:].rearrange("p g q -> p (g q)").bitcast(I32), 0)
         vs_pool = new_tile("vs_pool", [P, T], F32)
         nc.gpsimd.memset(vs_pool[0:ROW, :].bitcast(I32), 0)
         identity = new_tile("identity", [P, P], F32)
         make_identity(nc, identity[:])
-        k_planes = new_tile("k_planes", [P, PASSES, B * N], U8)
-        nc.gpsimd.memset(k_planes[:].rearrange("p o n -> p (o n)").bitcast(I32), 0)
 
         v_raw = [[new_tile("v_raw%d%d" % (b, h), [P, SEG], F32) for h in range(HALVES)] for b in range(B)]
-        v_pool = [new_tile("v_pool%d" % h, [P, T], BF16) for h in range(HALVES)]
+        first_pool = new_tile("first_pool", [P, SEG], BF16)
+        v_pool = new_tile("v_pool", [P, T], BF16)
 
         def load_values(b, h, cols=slice(0, SEG)):
             nc.sync.dma_start(v_raw[b][h][:, cols], vT[P * h : P * (h + 1), SEG * b + cols.start : SEG * b + cols.stop])
 
         first_cols = [slice(0, SEG // 2), slice(SEG // 2, SEG)]
-        nc.sync.dma_start(ks_pool[KS_FIRST:P, :].bitcast(I32), k_scales.rearrange("o f t -> (o f) t").bitcast(I32))
-        nc.sync.dma_start(kb_pool[ROW:P, 0:T], kb[0:1, :])
+        nc.sync.dma_start(ks_pool[KS_FIRST:P, :].bitcast(I32), k_scales.rearrange("o f t -> f o t").bitcast(I32))
         load_values(0, 0, first_cols[0])
 
         warm_out = new_tile("warm_out", [P, 1], F32)
@@ -88,31 +84,39 @@ def tile_attend_sigm_kb_segb2q128n512t2048_kernel(tc, q_words, q_scales, k_words
             )
 
         load_values(0, 0, first_cols[1])
-        load_values(1, 0, first_cols[0])
-        load_values(1, 0, first_cols[1])
-        load_keys(0)
-        nc.sync.dma_start(vs_pool[ROW:P, :], vs[0:1, :])
-        load_values(0, 1)
-        load_values(1, 1)
-        load_keys(1)
-        q_codes = new_tile("q_codes", [P, B * PASSES, NQ], U32)
-        nc.sync.dma_start(q_codes[:].bitcast(I32), q_words.rearrange("b o p q c -> p (b o) (q c)").bitcast(I32))
-        qs_rows = q_scales.rearrange("b o f q -> f (b o) q")
-        for c in range(4):
+        nc.sync.dma_start(kb_pool[ROW:P, 0:T], kb[0:1, :])
+        scale_rows = new_tile("scale_rows", [P, B * (N + NQ)], U8)
+        for b in range(B):
             nc.sync.dma_start(
-                q_planes[32 * c : 32 * c + 4, :, :].bitcast(I32), qs_rows[4 * c : 4 * c + 4, :, :].bitcast(I32)
+                scale_rows[KS_FIRST:P, B * N + NQ * b : B * N + NQ * (b + 1)].bitcast(I32),
+                q_scales[b].rearrange("o f q -> f o q").bitcast(I32),
             )
+        load_values(0, 1)
+        nc.sync.dma_start(vs_pool[ROW:P, :], vs[0:1, :])
+        load_values(1, 0)
+        load_keys(0)
 
-        ks_listed = new_tile("ks_listed", [P, B * N], U8)
-        nc.vector.tensor_copy(ks_listed[:], listed_for_all(ks_pool[:]))
+        ks_listed = [new_tile("ks_listed%d" % b, [P, N], U8) for b in range(B)]
+        for b in range(B):
+            nc.vector.tensor_copy(ks_listed[b][:], listed_for(ks_pool[:], b))
+        for b in range(B):
+            nc.vector.tensor_copy(
+                scale_rows[:, N * b : N * (b + 1)].rearrange("p (t m) -> p t m", t=PLACES),
+                ks_listed[b][:].rearrange("p (m t) -> p t m", t=PLACES),
+            )
+        planes = new_tile("planes", [P, PASSES, B * (N + NQ)], U8)
+        for c in range(4):
+            first = KS_FIRST + 8 * c
+            nc.sync.dma_start(planes[32 * c : 32 * c + 4, :, :].bitcast(I32), scale_rows[first : first + 8, :].bitcast(I32))
+
+        load_values(1, 1)
         kb_listed = new_tile("kb_listed", [P, B * N], F32)
         nc.vector.tensor_copy(kb_listed[:], listed_for_all(kb_pool[:, 0:T]))
-        def deal_out(name, listed):
-            cols = [new_tile("%s%d" % (name, b), [P, PLACES], F32) for b in range(B)]
-            for b in range(B):
-                nc.sync.dma_start(cols[b][:], listed[ROW:P, N * b : N * (b + 1)].rearrange("r (m t) -> r m t", t=PLACES))
-            return cols
 
+        def deal_out(name, listed):
+            cols = new_tile(name, [P, PLACES], F32)
+            nc.sync.dma_start(cols[:], listed.rearrange("r (m t) -> r m t", t=PLACES))
+            return cols
 
         kw_listed = [new_tile("kw_listed%d" % b, [P, N], U32) for b in range(B)]
         k_codes = [None, None]
@@ -120,25 +124,23 @@ def tile_attend_sigm_kb_segb2q128n512t2048_kernel(tc, q_words, q_scales, k_words
         def gather_keys(b):
             nc.vector.tensor_copy(kw_listed[b][:], listed_for(kw_pool[:, 0 : SEG * (b + 1)], b))
 
-        def part_keys(b, takes_over=None):
-            k_codes[b] = new_tile("k_codes%d" % b, [P, PASSES, N], U16, takes_over)
-            nc.vector.tensor_copy(
-                k_codes[b][:].rearrange("p o (t x y) -> p o x t y", t=PLACES, y=4),
-                kw_listed[b][:].bitcast(U16).rearrange("p (x y t o) -> p o x t y", t=PLACES, y=4, o=PASSES),
-            )
+        def part_keys(b, pieces):
+            k_codes[b] = new_tile("k_codes%d" % b, [P, PLACES, PASSES, P], U16)
+            parted = k_codes[b][:].rearrange("p t o (x y) -> p o x t y", y=4)
+            paired = kw_listed[b][:].bitcast(U16).rearrange("p (x y t o) -> p o x t y", t=PLACES, y=4, o=PASSES)
+            for first in range(0, PLACES, PLACES // pieces):
+                places = slice(first, first + PLACES // pieces)
+                nc.vector.tensor_copy(parted[:, :, :, places, :], paired[:, :, :, places, :])
 
-        gather_keys(0)
-        vs_listed = new_tile("vs_listed", [P, B * N], F32)
-        nc.vector.tensor_copy(vs_listed[:], listed_for_all(vs_pool[:]))
+        def gather_token_scales(b):
+            nc.vector.tensor_copy(vs_listed[:, N * b : N * (b + 1)], listed_for(vs_pool[:], b))
 
-        def round_values(b, h, cols=slice(0, SEG)):
-            nc.scalar.activation(
-                v_pool[h][:, SEG * b + cols.start : SEG * b + cols.stop], v_raw[b][h][:, cols], ACT.Copy
-            )
+        def round_values(pool, b, h, cols=slice(0, SEG)):
+            nc.scalar.activation(pool[:, SEG * b + cols.start : SEG * b + cols.stop], v_raw[b][h][:, cols], ACT.Copy)
 
-        def gather_values(name, listed, count):
-            v_listed = new_tile(name, [P, count], BF16)
-            nc.scalar.activation(v_listed[:], listed, ACT.Copy)
+        def gather_values(pool, b, h, takes_over=None):
+            v_listed = new_tile("v_listed%d%d" % (b, h), [P, N], BF16, takes_over)
+            nc.scalar.activation(v_listed[:], listed_for(pool[:], b), ACT.Copy)
             return v_listed
 
         def turn_values(bank, v_listed):
@@ -153,20 +155,19 @@ def tile_attend_sigm_kb_segb2q128n512t2048_kernel(tc, q_words, q_scales, k_words
 
         def scores(b):
             if b == 0:
-                bank = new_bank("scores0", [P, PLACES, NQ])
-                acc = [bank[:, place, :] for place in range(PLACES)]
+                banks = [new_bank("scores0%d" % pair, [P, 2, NQ]) for pair in range(PLACES // 2)]
+                acc = [banks[place // 2][:, place % 2, :] for place in range(PLACES)]
             else:
                 acc = [new_bank("scores1%d" % place, [P, NQ])[:] for place in range(PLACES)]
             for place in range(PLACES):
-                cols = slice(place * P, (place + 1) * P)
-                plane_cols = slice((place * B + b) * P, (place * B + b + 1) * P)
+                plane_cols = slice(N * b + place * P, N * b + (place + 1) * P)
                 for o in range(PASSES):
                     nc.tensor.matmul_mx(
                         out=acc[place],
-                        lhsT=k_codes[b][:, o, cols].bitcast(FP4X4),
-                        lhsT_scale=k_planes[:, o, plane_cols],
+                        lhsT=k_codes[b][:, place, o, :].bitcast(FP4X4),
+                        lhsT_scale=planes[:, o, plane_cols],
                         rhs=q_codes[:, PASSES * b + o, :].bitcast(FP8X4),
-                        rhs_scale=q_planes[:, PASSES * b + o, :],
+                        rhs_scale=planes[:, o, B * N + NQ * b : B * N + NQ * (b + 1)],
                         start=(o == 0),
                         stop=(o == PASSES - 1),
                     )
@@ -179,8 +180,8 @@ def tile_attend_sigm_kb_segb2q128n512t2048_kernel(tc, q_words, q_scales, k_words
                 nc.scalar.activation(prob[:, place, :], acc[place], ACT.Sigmoid, bias=bias)
             return prob
 
-        def weigh(b, prob, token_scales):
-            w = new_tile("w%d" % b, [P, NQ * PLACES], BF16)
+        def weigh(b, prob, token_scales, takes_over=None):
+            w = new_tile("w%d" % b, [P, NQ * PLACES], BF16, takes_over)
             nc.vector.tensor_tensor(
                 w[:].rearrange("p (c i t) -> p c t i", i=4, t=PLACES),
                 prob[:].rearrange("p t (c i) -> p c t i", i=4),
@@ -202,8 +203,8 @@ def tile_attend_sigm_kb_segb2q128n512t2048_kernel(tc, q_words, q_scales, k_words
                 out=acc[:],
                 lhsT=w_mx[0][:].bitcast(FP8X4),
                 lhsT_scale=w_mx[1][:],
-                rhs=v_mx[0][:, cols].bitcast(FP8X4),
-                rhs_scale=v_mx[1][:, cols],
+                rhs=v_mx[0][:].bitcast(FP8X4),
+                rhs_scale=v_mx[1][:],
                 start=True,
                 stop=True,
             )
@@ -217,51 +218,47 @@ def tile_attend_sigm_kb_segb2q128n512t2048_kernel(tc, q_words, q_scales, k_words
 
         v_turned0 = new_bank("v_turned0", [P, HALVES, 2, P])
         v_turned10 = new_bank("v_turned10", [P, 1, 2, P])
-        round_values(0, 0, first_cols[0])
-        round_values(0, 0, first_cols[1])
-        round_values(1, 0, first_cols[0])
-        round_values(1, 0, first_cols[1])
-        v_listed0 = gather_values("v_listed0", listed_for_all(v_pool[0][:]), B * N)
-        turn_values(v_turned0[:, 0], v_listed0[:, 0:N])
-        turn_values(v_turned10[:, 0], v_listed0[:, N : 2 * N])
-        round_values(0, 1)
-        round_values(1, 1)
-        ks_placed = new_tile("ks_placed", [P, B * N], U8, "v_raw10")
-        nc.vector.tensor_copy(
-            ks_placed[:].rearrange("p (t m) -> p t m", t=PLACES), ks_listed[:].rearrange("p (m t) -> p t m", t=PLACES)
-        )
-        for o in reversed(range(PASSES)):
-            for c in range(4):
-                first = KS_FIRST + 16 * o + 4 * c
-                nc.sync.dma_start(
-                    k_planes[32 * c : 32 * c + 4, o, :].bitcast(I32), ks_placed[first : first + 4, :].bitcast(I32)
-                )
-
-        kb_cols = deal_out("kb_cols", kb_listed)
-        vs_cols = deal_out("vs_cols", vs_listed)
-        part_keys(0, "v_raw01")
+        round_values(first_pool, 0, 0, first_cols[0])
+        round_values(first_pool, 0, 0, first_cols[1])
+        turn_values(v_turned0[:, 0], gather_values(first_pool, 0, 0)[:])
+        round_values(v_pool, 0, 1)
+        round_values(v_pool, 1, 0)
+        turn_values(v_turned0[:, 1], gather_values(v_pool, 0, 1)[:])
+        turn_values(v_turned10[:, 0], gather_values(v_pool, 1, 0)[:])
+        load_keys(1)
+        q_codes = new_tile("q_codes", [P, B * PASSES, NQ], U32)
+        nc.sync.dma_start(q_codes[:].bitcast(I32), q_words.rearrange("b o p q c -> p (b o) (q c)").bitcast(I32))
+        kb_cols = [deal_out("kb_cols%d" % b, kb_listed[ROW:P, N * b : N * (b + 1)]) for b in range(B)]
+        gather_keys(0)
+        vs_listed = new_tile("vs_listed", [P, B * N], F32, "v_raw10")
+        gather_token_scales(0)
+        part_keys(0, 1)
+        gather_token_scales(1)
+        vs_cols = [deal_out("vs_cols%d" % b, vs_listed[ROW:P, N * b : N * (b + 1)]) for b in range(B)]
         gather_keys(1)
-        part_keys(1)
 
-        v_listed01 = gather_values("v_listed01", listed_for(v_pool[1][:], 0), N)
-        turn_values(v_turned0[:, 1], v_listed01[:])
-        v_listed11 = gather_values("v_listed11", listed_for(v_pool[1][:], 1), N)
-        v_grouped0 = new_tile("v_grouped0", [P, DV * PLACES], BF16, "v_pool1")
+        part_keys(1, 2)
+
+        v_grouped0 = new_tile("v_grouped0", [P, DV * PLACES], BF16)
         group_values(v_grouped0[:], v_turned0[:])
-        v_grouped1 = new_tile("v_grouped1", [P, DV * PLACES], BF16, "kw_pool")
+        v_grouped10 = new_tile("v_grouped10", [P, P * PLACES], BF16, "kw_pool")
+        group_values(v_grouped10[:], v_turned10[:], nc.vector.tensor_copy)
+        round_values(v_pool, 1, 1)
+        v_listed11 = gather_values(v_pool, 1, 1)
         accs = [scores(b) for b in range(B)]
-        prob0 = sigmoid(0, accs[0], "v_listed01")
-        v_turned11 = new_bank("v_turned11", [P, 1, 2, P], "scores0")
+        prob0 = sigmoid(0, accs[0])
+        v_turned11 = new_bank("v_turned11", [P, 1, 2, P], "scores01")
         turn_values(v_turned11[:, 0], v_listed11[:])
         prob1 = sigmoid(1, accs[1])
-        group_values(v_grouped1[:, P * PLACES : 2 * P * PLACES], v_turned11[:])
-        group_values(v_grouped1[:, 0 : P * PLACES], v_turned10[:], nc.vector.tensor_copy)
+        v_grouped11 = new_tile("v_grouped11", [P, P * PLACES], BF16, "kb_cols1")
+        group_values(v_grouped11[:], v_turned11[:])
+        v_mx0 = quantize("v0", v_grouped0, DV, "kw_listed1")
         w0 = weigh(0, prob0, vs_cols[0])
-        v_mx0 = quantize("v0", v_grouped0, DV, "vs_listed")
+        v_mx10 = quantize("v10", v_grouped10, P, "v_raw10")
         w_mx0 = quantize("w0", w0, NQ)
         w1 = weigh(1, prob1, vs_cols[1])
-        v_mx1 = quantize("v1", v_grouped1, DV)
+        v_mx11 = quantize("v11", v_grouped11, P)
         w_mx1 = quantize("w1", w1, NQ)
         finish(0, w_mx0, v_mx0, slice(0, DV), "v_turned0")
-        finish(1, w_mx1, v_mx1, slice(0, P), "v_turned10")
-        finish(1, w_mx1, v_mx1, slice(P, DV), None, True)
+        finish(1, w_mx1, v_mx10, slice(0, P), "v_turned10")
+        finish(1, w_mx1, v_mx11, slice(P, DV), "scores00", True)

@@ -54,12 +54,12 @@ def tile_attend_sigm_kb_segb2q128n512t2048_kernel(tc, q_words, q_scales, k_words
         nc.gpsimd.memset(ks_pool[0:KS_FIRST, :].bitcast(I32), 0)
         warm_in = new_tile("warm_in", [P, 1], F32)
         nc.gpsimd.memset(warm_in[:], 0.0)
-        kb_pool = new_tile("kb_pool", [P, T + 1], F32)
+        kb_pool = new_tile("kb_pool", [P, T], F32)
         nc.vector.memset(kb_pool[0:ROW, :].bitcast(I32), 0)
-        vs_pool = new_tile("vs_pool", [P, T], F32)
-        nc.gpsimd.memset(vs_pool[0:ROW, :].bitcast(I32), 0)
         identity = new_tile("identity", [P, P], F32)
         make_identity(nc, identity[:])
+        vs_pool = new_tile("vs_pool", [P, T], F32)
+        nc.gpsimd.memset(vs_pool[0:ROW, :].bitcast(I32), 0)
 
         v_raw = [[new_tile("v_raw%d%d" % (b, h), [P, SEG], F32) for h in range(HALVES)] for b in range(B)]
         first_pool = new_tile("first_pool", [P, SEG], BF16)
@@ -84,7 +84,7 @@ def tile_attend_sigm_kb_segb2q128n512t2048_kernel(tc, q_words, q_scales, k_words
             )
 
         load_values(0, 0, first_cols[1])
-        nc.sync.dma_start(kb_pool[ROW:P, 0:T], kb[0:1, :])
+        nc.sync.dma_start(kb_pool[ROW:P, :], kb[0:1, :])
         scale_rows = new_tile("scale_rows", [P, B * (N + NQ)], U8)
         for b in range(B):
             nc.sync.dma_start(
@@ -109,9 +109,14 @@ def tile_attend_sigm_kb_segb2q128n512t2048_kernel(tc, q_words, q_scales, k_words
             first = KS_FIRST + 8 * c
             nc.sync.dma_start(planes[32 * c : 32 * c + 4, :, :].bitcast(I32), scale_rows[first : first + 8, :].bitcast(I32))
 
-        load_values(1, 1)
+        load_values(1, 1, first_cols[0])
         kb_listed = new_tile("kb_listed", [P, B * N], F32)
-        nc.vector.tensor_copy(kb_listed[:], listed_for_all(kb_pool[:, 0:T]))
+        nc.vector.tensor_copy(kb_listed[:], listed_for_all(kb_pool[:]))
+
+        def load_queries(b):
+            codes = new_tile("q_codes%d" % b, [P, PASSES, NQ], U32)
+            nc.sync.dma_start(codes[:].bitcast(I32), q_words[b].rearrange("o p q c -> p o (q c)").bitcast(I32))
+            return codes
 
         def deal_out(name, listed):
             cols = new_tile(name, [P, PLACES], F32)
@@ -132,8 +137,10 @@ def tile_attend_sigm_kb_segb2q128n512t2048_kernel(tc, q_words, q_scales, k_words
                 places = slice(first, first + PLACES // pieces)
                 nc.vector.tensor_copy(parted[:, :, :, places, :], paired[:, :, :, places, :])
 
-        def gather_token_scales(b):
-            nc.vector.tensor_copy(vs_listed[:, N * b : N * (b + 1)], listed_for(vs_pool[:], b))
+        def gather_token_scales(b, takes_over=None):
+            vs_listed = new_tile("vs_listed%d" % b, [P, N], F32, takes_over)
+            nc.vector.tensor_copy(vs_listed[:], listed_for(vs_pool[:], b))
+            return vs_listed
 
         def round_values(pool, b, h, cols=slice(0, SEG)):
             nc.scalar.activation(pool[:, SEG * b + cols.start : SEG * b + cols.stop], v_raw[b][h][:, cols], ACT.Copy)
@@ -166,7 +173,7 @@ def tile_attend_sigm_kb_segb2q128n512t2048_kernel(tc, q_words, q_scales, k_words
                         out=acc[place],
                         lhsT=k_codes[b][:, place, o, :].bitcast(FP4X4),
                         lhsT_scale=planes[:, o, plane_cols],
-                        rhs=q_codes[:, PASSES * b + o, :].bitcast(FP8X4),
+                        rhs=q_codes[b][:, o, :].bitcast(FP8X4),
                         rhs_scale=planes[:, o, B * N + NQ * b : B * N + NQ * (b + 1)],
                         start=(o == 0),
                         stop=(o == PASSES - 1),
@@ -226,25 +233,27 @@ def tile_attend_sigm_kb_segb2q128n512t2048_kernel(tc, q_words, q_scales, k_words
         turn_values(v_turned0[:, 1], gather_values(v_pool, 0, 1)[:])
         turn_values(v_turned10[:, 0], gather_values(v_pool, 1, 0)[:])
         load_keys(1)
-        q_codes = new_tile("q_codes", [P, B * PASSES, NQ], U32)
-        nc.sync.dma_start(q_codes[:].bitcast(I32), q_words.rearrange("b o p q c -> p (b o) (q c)").bitcast(I32))
+        q_codes = [load_queries(0)]
+        load_values(1, 1, first_cols[1])
+        q_codes.append(load_queries(1))
         kb_cols = [deal_out("kb_cols%d" % b, kb_listed[ROW:P, N * b : N * (b + 1)]) for b in range(B)]
+        vs_listed = [gather_token_scales(0)]
         gather_keys(0)
-        vs_listed = new_tile("vs_listed", [P, B * N], F32, "v_raw10")
-        gather_token_scales(0)
+        vs_listed.append(gather_token_scales(1, "v_raw10"))
         part_keys(0, 1)
-        gather_token_scales(1)
-        vs_cols = [deal_out("vs_cols%d" % b, vs_listed[ROW:P, N * b : N * (b + 1)]) for b in range(B)]
+        vs_cols = [deal_out("vs_cols%d" % b, vs_listed[b][ROW:P, :]) for b in range(B)]
         gather_keys(1)
 
-        part_keys(1, 2)
 
         v_grouped0 = new_tile("v_grouped0", [P, DV * PLACES], BF16)
         group_values(v_grouped0[:], v_turned0[:])
+        round_values(v_pool, 1, 1, first_cols[0])
+        round_values(v_pool, 1, 1, first_cols[1])
+        v_listed11 = gather_values(v_pool, 1, 1)
+        part_keys(1, 2)
         v_grouped10 = new_tile("v_grouped10", [P, P * PLACES], BF16, "kw_pool")
         group_values(v_grouped10[:], v_turned10[:], nc.vector.tensor_copy)
-        round_values(v_pool, 1, 1)
-        v_listed11 = gather_values(v_pool, 1, 1)
+        v_mx0 = quantize("v0", v_grouped0, DV, "kw_listed1")
         accs = [scores(b) for b in range(B)]
         prob0 = sigmoid(0, accs[0])
         v_turned11 = new_bank("v_turned11", [P, 1, 2, P], "scores01")
@@ -252,7 +261,6 @@ def tile_attend_sigm_kb_segb2q128n512t2048_kernel(tc, q_words, q_scales, k_words
         prob1 = sigmoid(1, accs[1])
         v_grouped11 = new_tile("v_grouped11", [P, P * PLACES], BF16, "kb_cols1")
         group_values(v_grouped11[:], v_turned11[:])
-        v_mx0 = quantize("v0", v_grouped0, DV, "kw_listed1")
         w0 = weigh(0, prob0, vs_cols[0])
         v_mx10 = quantize("v10", v_grouped10, P, "v_raw10")
         w_mx0 = quantize("w0", w0, NQ)

@@ -24,6 +24,7 @@ PASSES = D // (P * PLACES)
 HALVES = DV // P
 KS_FIRST = P - PASSES * 16
 ROW = P - 1
+KB_SPLIT = T // 4
 
 
 def tile_attend_sigm_kb_segb2q128n512t2048_kernel(tc, q_words, q_scales, k_words, k_scales, vT, vs, kb, offs, out):
@@ -54,8 +55,9 @@ def tile_attend_sigm_kb_segb2q128n512t2048_kernel(tc, q_words, q_scales, k_words
         nc.gpsimd.memset(ks_pool[0:KS_FIRST, :].bitcast(I32), 0)
         warm_in = new_tile("warm_in", [P, 1], F32)
         nc.gpsimd.memset(warm_in[:], 0.0)
-        kb_pool = new_tile("kb_pool", [P, T], F32)
-        nc.vector.memset(kb_pool[0:ROW, :].bitcast(I32), 0)
+        kb_pool = new_tile("kb_pool", [P, T + 1], F32)
+        nc.vector.memset(kb_pool[0:ROW, KB_SPLIT:].bitcast(I32), 0)
+        nc.gpsimd.memset(kb_pool[0:ROW, 0:KB_SPLIT].bitcast(I32), 0)
         identity = new_tile("identity", [P, P], F32)
         make_identity(nc, identity[:])
         vs_pool = new_tile("vs_pool", [P, T], F32)
@@ -84,7 +86,7 @@ def tile_attend_sigm_kb_segb2q128n512t2048_kernel(tc, q_words, q_scales, k_words
             )
 
         load_values(0, 0, first_cols[1])
-        nc.sync.dma_start(kb_pool[ROW:P, :], kb[0:1, :])
+        nc.sync.dma_start(kb_pool[ROW:P, 0:T], kb[0:1, :])
         scale_rows = new_tile("scale_rows", [P, B * (N + NQ)], U8)
         for b in range(B):
             nc.sync.dma_start(
@@ -111,7 +113,7 @@ def tile_attend_sigm_kb_segb2q128n512t2048_kernel(tc, q_words, q_scales, k_words
 
         load_values(1, 1, first_cols[0])
         kb_listed = new_tile("kb_listed", [P, B * N], F32)
-        nc.vector.tensor_copy(kb_listed[:], listed_for_all(kb_pool[:]))
+        nc.vector.tensor_copy(kb_listed[:], listed_for_all(kb_pool[:, 0:T]))
 
         def load_queries(b):
             codes = new_tile("q_codes%d" % b, [P, PASSES, NQ], U32)

@@ -72,7 +72,8 @@ def tile_attend_sigm_kb_segb2q128n512t2048_kernel(tc, q_words, q_scales, k_words
 
         first_cols = [slice(0, SEG // 2), slice(SEG // 2, SEG)]
         nc.sync.dma_start(ks_pool[KS_FIRST:P, :].bitcast(I32), k_scales.rearrange("o f t -> f o t").bitcast(I32))
-        load_values(0, 0, first_cols[0])
+        quarters = [slice(c, c + SEG // 4) for c in range(0, SEG, SEG // 4)]
+        load_values(0, 0, quarters[0])
 
         warm_out = new_tile("warm_out", [P, 1], F32)
         nc.scalar.activation(warm_out[:], warm_in[:], ACT.Sigmoid)
@@ -85,15 +86,16 @@ def tile_attend_sigm_kb_segb2q128n512t2048_kernel(tc, q_words, q_scales, k_words
                 kw_pool[:, stretch(b)].bitcast(I32), kw_bytes[:, 4 * SEG * b : 4 * SEG * (b + 1)].bitcast(I32)
             )
 
-        load_values(0, 0, first_cols[1])
+        for cols in quarters[1:]:
+            load_values(0, 0, cols)
         nc.sync.dma_start(kb_pool[ROW:P, 0:T], kb[0:1, :])
+        load_values(0, 1)
         scale_rows = new_tile("scale_rows", [P, B * (N + NQ)], U8)
         for b in range(B):
             nc.sync.dma_start(
                 scale_rows[KS_FIRST:P, B * N + NQ * b : B * N + NQ * (b + 1)].bitcast(I32),
                 q_scales[b].rearrange("o f q -> f o q").bitcast(I32),
             )
-        load_values(0, 1)
         nc.sync.dma_start(vs_pool[ROW:P, :], vs[0:1, :])
         load_values(1, 0)
         load_keys(0)
@@ -227,8 +229,8 @@ def tile_attend_sigm_kb_segb2q128n512t2048_kernel(tc, q_words, q_scales, k_words
 
         v_turned0 = new_bank("v_turned0", [P, HALVES, 2, P])
         v_turned10 = new_bank("v_turned10", [P, 1, 2, P])
-        round_values(first_pool, 0, 0, first_cols[0])
-        round_values(first_pool, 0, 0, first_cols[1])
+        for cols in quarters:
+            round_values(first_pool, 0, 0, cols)
         turn_values(v_turned0[:, 0], gather_values(first_pool, 0, 0)[:])
         round_values(v_pool, 0, 1)
         round_values(v_pool, 1, 0)
@@ -256,6 +258,17 @@ def tile_attend_sigm_kb_segb2q128n512t2048_kernel(tc, q_words, q_scales, k_words
         v_grouped10 = new_tile("v_grouped10", [P, P * PLACES], BF16, "kw_pool")
         group_values(v_grouped10[:], v_turned10[:], nc.vector.tensor_copy)
         v_mx0 = quantize("v0", v_grouped0, DV, "kw_listed1")
+        warm_bank = new_bank("warm_bank", [P, PASSES, PASSES * NQ], "v_turned0")
+        for o in range(PASSES):
+            nc.tensor.matmul_mx(
+                out=warm_bank[:, o, :],
+                lhsT=q_codes[0][:, o, :].bitcast(FP8X4),
+                lhsT_scale=planes[:, o, B * N : B * N + NQ],
+                rhs=q_codes[0][:].rearrange("p o q -> p (o q)").bitcast(FP8X4),
+                rhs_scale=planes[:, o, B * N : B * (N + NQ)],
+                start=True,
+                stop=True,
+            )
         accs = [scores(b) for b in range(B)]
         prob0 = sigmoid(0, accs[0])
         v_turned11 = new_bank("v_turned11", [P, 1, 2, P], "scores01")

@@ -43,7 +43,15 @@ def tile_attend_sigm_kb_segb2q128n512t2048_kernel(tc, q_words, q_scales, k_words
             return slice(SEG * b, SEG * (b + 1))
 
         offsets = sbuf.tile([P, B * LIST_COLS], U16, name="offsets")
+        ks_pool = new_tile("ks_pool", [P, T], U8)
+        ks_rows = k_scales.rearrange("o f t -> f o t")
+
+        def load_key_scales(b):
+            nc.sync.dma_start(ks_pool[KS_FIRST:P, stretch(b)].bitcast(I32), ks_rows[:, :, stretch(b)].bitcast(I32))
+
+        load_key_scales(0)
         nc.sync.dma_start(offsets[:], offs)
+        load_key_scales(1)
 
         def listed_for_all(window):
             return window.indirect(offsets[:])
@@ -51,15 +59,14 @@ def tile_attend_sigm_kb_segb2q128n512t2048_kernel(tc, q_words, q_scales, k_words
         def listed_for(window, b):
             return window.indirect(offsets[:, b * LIST_COLS : (b + 1) * LIST_COLS])
 
-        ks_pool = new_tile("ks_pool", [P, T], U8)
-        nc.gpsimd.memset(ks_pool[0:KS_FIRST, :].bitcast(I32), 0)
         warm_in = new_tile("warm_in", [P, 1], F32)
         nc.gpsimd.memset(warm_in[:], 0.0)
+        identity = new_tile("identity", [P, P], F32)
+        make_identity(nc, identity[:])
+        nc.gpsimd.memset(ks_pool[0:KS_FIRST, :].bitcast(I32), 0)
         kb_pool = new_tile("kb_pool", [P, T + 1], F32)
         nc.vector.memset(kb_pool[0:ROW, KB_SPLIT:].bitcast(I32), 0)
         nc.gpsimd.memset(kb_pool[0:ROW, 0:KB_SPLIT].bitcast(I32), 0)
-        identity = new_tile("identity", [P, P], F32)
-        make_identity(nc, identity[:])
         vs_pool = new_tile("vs_pool", [P, T], F32)
         nc.gpsimd.memset(vs_pool[0:ROW, :].bitcast(I32), 0)
 
@@ -71,9 +78,9 @@ def tile_attend_sigm_kb_segb2q128n512t2048_kernel(tc, q_words, q_scales, k_words
             nc.sync.dma_start(v_raw[b][h][:, cols], vT[P * h : P * (h + 1), SEG * b + cols.start : SEG * b + cols.stop])
 
         first_cols = [slice(0, SEG // 2), slice(SEG // 2, SEG)]
-        nc.sync.dma_start(ks_pool[KS_FIRST:P, :].bitcast(I32), k_scales.rearrange("o f t -> f o t").bitcast(I32))
-        quarters = [slice(c, c + SEG // 4) for c in range(0, SEG, SEG // 4)]
-        load_values(0, 0, quarters[0])
+        quarters = [slice(0, 3 * SEG // 8), slice(3 * SEG // 8, 3 * SEG // 4), slice(3 * SEG // 4, SEG)]
+        v_first = new_tile("v_first", [P, 3 * SEG // 8], F32)
+        nc.sync.dma_start(v_first[:], vT[0:P, quarters[0]])
 
         warm_out = new_tile("warm_out", [P, 1], F32)
         nc.scalar.activation(warm_out[:], warm_in[:], ACT.Sigmoid)
@@ -90,30 +97,29 @@ def tile_attend_sigm_kb_segb2q128n512t2048_kernel(tc, q_words, q_scales, k_words
             load_values(0, 0, cols)
         nc.sync.dma_start(kb_pool[ROW:P, 0:T], kb[0:1, :])
         load_values(0, 1)
-        scale_rows = new_tile("scale_rows", [P, B * (N + NQ)], U8)
+        for cols in first_cols:
+            load_values(1, 0, cols)
+        nc.scalar.activation(first_pool[:, quarters[0]], v_first[:], ACT.Copy)
+        scale_rows = new_tile("scale_rows", [P, B * (N + NQ)], U8, "v_first")
         for b in range(B):
             nc.sync.dma_start(
                 scale_rows[KS_FIRST:P, B * N + NQ * b : B * N + NQ * (b + 1)].bitcast(I32),
                 q_scales[b].rearrange("o f q -> f o q").bitcast(I32),
             )
         nc.sync.dma_start(vs_pool[ROW:P, :], vs[0:1, :])
-        load_values(1, 0)
         load_keys(0)
+        load_values(1, 1, first_cols[0])
 
         ks_listed = [new_tile("ks_listed%d" % b, [P, N], U8) for b in range(B)]
         for b in range(B):
-            nc.vector.tensor_copy(ks_listed[b][:], listed_for(ks_pool[:], b))
+            nc.vector.tensor_copy(ks_listed[b][:], listed_for(ks_pool[:, 0 : SEG * (b + 1)], b))
         for b in range(B):
             nc.vector.tensor_copy(
                 scale_rows[:, N * b : N * (b + 1)].rearrange("p (t m) -> p t m", t=PLACES),
                 ks_listed[b][:].rearrange("p (m t) -> p t m", t=PLACES),
             )
         planes = new_tile("planes", [P, PASSES, B * (N + NQ)], U8)
-        for c in range(4):
-            first = KS_FIRST + 8 * c
-            nc.sync.dma_start(planes[32 * c : 32 * c + 4, :, :].bitcast(I32), scale_rows[first : first + 8, :].bitcast(I32))
 
-        load_values(1, 1, first_cols[0])
         kb_listed = new_tile("kb_listed", [P, B * N], F32)
         nc.vector.tensor_copy(kb_listed[:], listed_for_all(kb_pool[:, 0:T]))
 
@@ -229,28 +235,41 @@ def tile_attend_sigm_kb_segb2q128n512t2048_kernel(tc, q_words, q_scales, k_words
 
         v_turned0 = new_bank("v_turned0", [P, HALVES, 2, P])
         v_turned10 = new_bank("v_turned10", [P, 1, 2, P])
-        for cols in quarters:
+        for cols in quarters[1:]:
             round_values(first_pool, 0, 0, cols)
         turn_values(v_turned0[:, 0], gather_values(first_pool, 0, 0)[:])
         round_values(v_pool, 0, 1)
-        round_values(v_pool, 1, 0)
+        for cols in first_cols:
+            round_values(v_pool, 1, 0, cols)
+        v_grouped0 = new_tile("v_grouped0", [P, DV * PLACES], BF16, "v_raw01")
+        group_values(v_grouped0[:, 0 : P * PLACES], v_turned0[:, 0:1])
         turn_values(v_turned0[:, 1], gather_values(v_pool, 0, 1)[:])
         turn_values(v_turned10[:, 0], gather_values(v_pool, 1, 0)[:])
         load_keys(1)
-        q_codes = [load_queries(0)]
         load_values(1, 1, first_cols[1])
+        q_codes = [load_queries(0)]
+        for c in (0, 2, 1, 3):
+            first = KS_FIRST + 8 * c
+            nc.sync.dma_start(planes[32 * c : 32 * c + 4, :, :].bitcast(I32), scale_rows[first : first + 8, :].bitcast(I32))
         q_codes.append(load_queries(1))
         kb_cols = [deal_out("kb_cols%d" % b, kb_listed[ROW:P, N * b : N * (b + 1)]) for b in range(B)]
         vs_listed = [gather_token_scales(0)]
-        gather_keys(0)
-        vs_listed.append(gather_token_scales(1, "v_raw10"))
-        part_keys(0, 1)
+        vs_listed.append(gather_token_scales(1))
+        kw_halves = [new_tile("kw_half%d" % piece, [P, N // 2], U32) for piece in range(2)]
+        for piece in range(2):
+            cols = slice(piece * LIST_COLS // 2, (piece + 1) * LIST_COLS // 2)
+            nc.vector.tensor_copy(kw_halves[piece][:], kw_pool[:, 0:SEG].indirect(offsets[:, cols]))
+        k_codes[0] = new_tile("k_codes0", [P, PLACES, PASSES, P], U16)
+        for piece in range(2):
+            nc.vector.tensor_copy(
+                k_codes[0][:].rearrange("p t o (x y) -> p o x t y", y=4)[:, :, 16 * piece : 16 * (piece + 1), :, :],
+                kw_halves[piece][:].bitcast(U16).rearrange("p (x y t o) -> p o x t y", t=PLACES, y=4, o=PASSES),
+            )
         vs_cols = [deal_out("vs_cols%d" % b, vs_listed[b][ROW:P, :]) for b in range(B)]
         gather_keys(1)
 
 
-        v_grouped0 = new_tile("v_grouped0", [P, DV * PLACES], BF16)
-        group_values(v_grouped0[:], v_turned0[:])
+        group_values(v_grouped0[:, P * PLACES :], v_turned0[:, 1:2])
         round_values(v_pool, 1, 1, first_cols[0])
         round_values(v_pool, 1, 1, first_cols[1])
         v_listed11 = gather_values(v_pool, 1, 1)
@@ -263,9 +282,9 @@ def tile_attend_sigm_kb_segb2q128n512t2048_kernel(tc, q_words, q_scales, k_words
             nc.tensor.matmul_mx(
                 out=warm_bank[:, o, :],
                 lhsT=q_codes[0][:, o, :].bitcast(FP8X4),
-                lhsT_scale=planes[:, o, B * N : B * N + NQ],
+                lhsT_scale=scale_rows[:, 0:NQ],
                 rhs=q_codes[0][:].rearrange("p o q -> p (o q)").bitcast(FP8X4),
-                rhs_scale=planes[:, o, B * N : B * (N + NQ)],
+                rhs_scale=scale_rows[:, 0 : PASSES * NQ],
                 start=True,
                 stop=True,
             )
@@ -277,7 +296,7 @@ def tile_attend_sigm_kb_segb2q128n512t2048_kernel(tc, q_words, q_scales, k_words
         v_grouped11 = new_tile("v_grouped11", [P, P * PLACES], BF16, "kb_cols1")
         group_values(v_grouped11[:], v_turned11[:])
         w0 = weigh(0, prob0, vs_cols[0])
-        v_mx10 = quantize("v10", v_grouped10, P, "v_raw10")
+        v_mx10 = quantize("v10", v_grouped10, P, "vs_listed1")
         w_mx0 = quantize("w0", w0, NQ)
         w1 = weigh(1, prob1, vs_cols[1])
         v_mx11 = quantize("v11", v_grouped11, P)

@@ -129,28 +129,27 @@ def tile_attend_sigm_kb_segb2q128n512t2048_kernel(tc, q_words, q_scales, k_words
             return codes
 
         def deal_out(name, listed):
-            cols = new_tile(name, [P, PLACES], F32)
-            nc.sync.dma_start(cols[:], listed.rearrange("r (m t) -> r m t", t=PLACES))
+            cols = [new_tile("%s%d" % (name, b), [P, PLACES], F32) for b in range(B)]
+            for b in range(B):
+                row = listed[ROW:P, N * b : N * (b + 1)]
+                nc.sync.dma_start(cols[b][:], row.rearrange("r (m t) -> r m t", t=PLACES))
             return cols
 
-        kw_listed = [new_tile("kw_listed%d" % b, [P, N], U32) for b in range(B)]
-        k_codes = [None, None]
+        k_codes = [new_tile("k_codes%d" % b, [P, PLACES, PASSES, P], U16) for b in range(B)]
 
         def gather_keys(b):
-            nc.vector.tensor_copy(kw_listed[b][:], listed_for(kw_pool[:, 0 : SEG * (b + 1)], b))
+            halves = [new_tile("kw_listed%d%d" % (b, half), [P, N // 2], U32) for half in range(2)]
+            for half in range(2):
+                first = b * LIST_COLS + half * LIST_COLS // 2
+                window = kw_pool[:, 0 : SEG * (b + 1)]
+                nc.vector.tensor_copy(halves[half][:], window.indirect(offsets[:, first : first + LIST_COLS // 2]))
+            return halves
 
-        def part_keys(b, pieces):
-            k_codes[b] = new_tile("k_codes%d" % b, [P, PLACES, PASSES, P], U16)
-            parted = k_codes[b][:].rearrange("p t o (x y) -> p o x t y", y=4)
-            paired = kw_listed[b][:].bitcast(U16).rearrange("p (x y t o) -> p o x t y", t=PLACES, y=4, o=PASSES)
-            for first in range(0, PLACES, PLACES // pieces):
-                places = slice(first, first + PLACES // pieces)
-                nc.vector.tensor_copy(parted[:, :, :, places, :], paired[:, :, :, places, :])
-
-        def gather_token_scales(b, takes_over=None):
-            vs_listed = new_tile("vs_listed%d" % b, [P, N], F32, takes_over)
-            nc.vector.tensor_copy(vs_listed[:], listed_for(vs_pool[:], b))
-            return vs_listed
+        def part_keys(b, halves, half, pair):
+            parted = k_codes[b][:].rearrange("p t o (h x y) -> p h o x t y", h=2, y=4)
+            paired = halves[half][:].bitcast(U16).rearrange("p (x y t o) -> p o x t y", t=PLACES, y=4, o=PASSES)
+            places = slice(2 * pair, 2 * pair + 2)
+            nc.vector.tensor_copy(parted[:, half, :, :, places, :], paired[:, :, :, places, :])
 
         def round_values(pool, b, h, cols=slice(0, SEG)):
             nc.scalar.activation(pool[:, SEG * b + cols.start : SEG * b + cols.stop], v_raw[b][h][:, cols], ACT.Copy)
@@ -202,7 +201,7 @@ def tile_attend_sigm_kb_segb2q128n512t2048_kernel(tc, q_words, q_scales, k_words
             nc.vector.tensor_tensor(
                 w[:].rearrange("p (c i t) -> p c t i", i=4, t=PLACES),
                 prob[:].rearrange("p t (c i) -> p c t i", i=4),
-                token_scales[:].unsqueeze(1).unsqueeze(3).to_broadcast([P, NQ // 4, PLACES, 4]),
+                token_scales.unsqueeze(1).unsqueeze(3).to_broadcast([P, NQ // 4, PLACES, 4]),
                 mybir.AluOpType.mult,
             )
             return w
@@ -252,31 +251,27 @@ def tile_attend_sigm_kb_segb2q128n512t2048_kernel(tc, q_words, q_scales, k_words
             first = KS_FIRST + 8 * c
             nc.sync.dma_start(planes[32 * c : 32 * c + 4, :, :].bitcast(I32), scale_rows[first : first + 8, :].bitcast(I32))
         q_codes.append(load_queries(1))
-        kb_cols = [deal_out("kb_cols%d" % b, kb_listed[ROW:P, N * b : N * (b + 1)]) for b in range(B)]
-        vs_listed = [gather_token_scales(0)]
-        vs_listed.append(gather_token_scales(1))
-        kw_halves = [new_tile("kw_half%d" % piece, [P, N // 2], U32) for piece in range(2)]
-        for piece in range(2):
-            cols = slice(piece * LIST_COLS // 2, (piece + 1) * LIST_COLS // 2)
-            nc.vector.tensor_copy(kw_halves[piece][:], kw_pool[:, 0:SEG].indirect(offsets[:, cols]))
-        k_codes[0] = new_tile("k_codes0", [P, PLACES, PASSES, P], U16)
-        for piece in range(2):
-            nc.vector.tensor_copy(
-                k_codes[0][:].rearrange("p t o (x y) -> p o x t y", y=4)[:, :, 16 * piece : 16 * (piece + 1), :, :],
-                kw_halves[piece][:].bitcast(U16).rearrange("p (x y t o) -> p o x t y", t=PLACES, y=4, o=PASSES),
-            )
-        vs_cols = [deal_out("vs_cols%d" % b, vs_listed[b][ROW:P, :]) for b in range(B)]
-        gather_keys(1)
+        kb_cols = deal_out("kb_cols", kb_listed)
+        vs_listed = new_tile("vs_listed", [P, B * N], F32)
+        nc.vector.tensor_copy(vs_listed[:], listed_for_all(vs_pool[:]))
+        kw_halves = gather_keys(0)
+        for half in range(2):
+            for pair in range(2):
+                part_keys(0, kw_halves, half, pair)
+        vs_cols = deal_out("vs_cols", vs_listed)
+        kw_halves = gather_keys(1)
 
 
         group_values(v_grouped0[:, P * PLACES :], v_turned0[:, 1:2])
         round_values(v_pool, 1, 1, first_cols[0])
         round_values(v_pool, 1, 1, first_cols[1])
         v_listed11 = gather_values(v_pool, 1, 1)
-        part_keys(1, 2)
-        v_grouped10 = new_tile("v_grouped10", [P, P * PLACES], BF16, "kw_pool")
+        for pair in range(2):
+            for half in range(2):
+                part_keys(1, kw_halves, half, pair)
+        v_grouped10 = new_tile("v_grouped10", [P, P * PLACES], BF16, "kw_listed10")
         group_values(v_grouped10[:], v_turned10[:], nc.vector.tensor_copy)
-        v_mx0 = quantize("v0", v_grouped0, DV, "kw_listed1")
+        v_mx0 = quantize("v0", v_grouped0, DV, "kw_listed11")
         warm_bank = new_bank("warm_bank", [P, PASSES, PASSES * NQ], "v_turned0")
         for o in range(PASSES):
             nc.tensor.matmul_mx(
@@ -295,10 +290,10 @@ def tile_attend_sigm_kb_segb2q128n512t2048_kernel(tc, q_words, q_scales, k_words
         prob1 = sigmoid(1, accs[1])
         v_grouped11 = new_tile("v_grouped11", [P, P * PLACES], BF16, "kb_cols1")
         group_values(v_grouped11[:], v_turned11[:])
-        w0 = weigh(0, prob0, vs_cols[0])
-        v_mx10 = quantize("v10", v_grouped10, P, "vs_listed1")
+        w0 = weigh(0, prob0, vs_cols[0][:])
+        v_mx10 = quantize("v10", v_grouped10, P, "vs_listed")
         w_mx0 = quantize("w0", w0, NQ)
-        w1 = weigh(1, prob1, vs_cols[1])
+        w1 = weigh(1, prob1, vs_cols[1][:])
         v_mx11 = quantize("v11", v_grouped11, P)
         w_mx1 = quantize("w1", w1, NQ)
         finish(0, w_mx0, v_mx0, slice(0, DV), "v_turned0")

@@ -70,9 +70,11 @@ def tile_attend_sigm_kb_segb2q128n512t2048_kernel(tc, q_words, q_scales, k_words
         vs_pool = new_tile("vs_pool", [P, T], F32)
         nc.gpsimd.memset(vs_pool[0:ROW, :].bitcast(I32), 0)
 
-        v_raw = [[new_tile("v_raw%d%d" % (b, h), [P, SEG], F32) for h in range(HALVES)] for b in range(B)]
+        v_raw = [[new_tile("v_raw%d%d" % (b, h), [P, SEG], F32) for h in range(HALVES - b)] for b in range(B)]
         first_pool = new_tile("first_pool", [P, SEG], BF16)
         v_pool = new_tile("v_pool", [P, T], BF16)
+
+        v_last = [new_tile("v_last%d" % half, [P, SEG // 2], F32) for half in range(2)]
 
         def load_values(b, h, cols=slice(0, SEG)):
             nc.sync.dma_start(v_raw[b][h][:, cols], vT[P * h : P * (h + 1), SEG * b + cols.start : SEG * b + cols.stop])
@@ -108,7 +110,6 @@ def tile_attend_sigm_kb_segb2q128n512t2048_kernel(tc, q_words, q_scales, k_words
             )
         nc.sync.dma_start(vs_pool[ROW:P, :], vs[0:1, :])
         load_keys(0)
-        load_values(1, 1, first_cols[0])
 
         ks_listed = [new_tile("ks_listed%d" % b, [P, N], U8) for b in range(B)]
         for b in range(B):
@@ -128,11 +129,9 @@ def tile_attend_sigm_kb_segb2q128n512t2048_kernel(tc, q_words, q_scales, k_words
             nc.sync.dma_start(codes[:].bitcast(I32), q_words[b].rearrange("o p q c -> p o (q c)").bitcast(I32))
             return codes
 
-        def deal_out(name, listed):
-            cols = [new_tile("%s%d" % (name, b), [P, PLACES], F32) for b in range(B)]
-            for b in range(B):
-                row = listed[ROW:P, N * b : N * (b + 1)]
-                nc.sync.dma_start(cols[b][:], row.rearrange("r (m t) -> r m t", t=PLACES))
+        def deal_out(name, listed, b):
+            cols = new_tile("%s%d" % (name, b), [P, PLACES], F32)
+            nc.sync.dma_start(cols[:], listed[ROW:P, N * b : N * (b + 1)].rearrange("r (m t) -> r m t", t=PLACES))
             return cols
 
         k_codes = [new_tile("k_codes%d" % b, [P, PLACES, PASSES, P], U16) for b in range(B)]
@@ -240,39 +239,45 @@ def tile_attend_sigm_kb_segb2q128n512t2048_kernel(tc, q_words, q_scales, k_words
         round_values(v_pool, 0, 1)
         for cols in first_cols:
             round_values(v_pool, 1, 0, cols)
-        v_grouped0 = new_tile("v_grouped0", [P, DV * PLACES], BF16, "v_raw01")
-        group_values(v_grouped0[:, 0 : P * PLACES], v_turned0[:, 0:1])
+        v_grouped00 = new_tile("v_grouped00", [P, P * PLACES], BF16, "v_raw01")
+        group_values(v_grouped00[:], v_turned0[:, 0:1])
         turn_values(v_turned0[:, 1], gather_values(v_pool, 0, 1)[:])
         turn_values(v_turned10[:, 0], gather_values(v_pool, 1, 0)[:])
+        for half, cols in enumerate(first_cols):
+            nc.sync.dma_start(v_last[half][:], vT[P : 2 * P, SEG + cols.start : SEG + cols.stop])
         load_keys(1)
-        load_values(1, 1, first_cols[1])
         q_codes = [load_queries(0)]
+        kb_cols = [deal_out("kb_cols", kb_listed, 0)]
         for c in (0, 2, 1, 3):
             first = KS_FIRST + 8 * c
             nc.sync.dma_start(planes[32 * c : 32 * c + 4, :, :].bitcast(I32), scale_rows[first : first + 8, :].bitcast(I32))
         q_codes.append(load_queries(1))
-        kb_cols = deal_out("kb_cols", kb_listed)
+        kb_cols.append(deal_out("kb_cols", kb_listed, 1))
         vs_listed = new_tile("vs_listed", [P, B * N], F32)
         nc.vector.tensor_copy(vs_listed[:], listed_for_all(vs_pool[:]))
         kw_halves = gather_keys(0)
         for half in range(2):
             for pair in range(2):
                 part_keys(0, kw_halves, half, pair)
-        vs_cols = deal_out("vs_cols", vs_listed)
+        vs_cols = [deal_out("vs_cols", vs_listed, b) for b in range(B)]
         kw_halves = gather_keys(1)
 
 
-        group_values(v_grouped0[:, P * PLACES :], v_turned0[:, 1:2])
-        round_values(v_pool, 1, 1, first_cols[0])
-        round_values(v_pool, 1, 1, first_cols[1])
-        v_listed11 = gather_values(v_pool, 1, 1)
+        last_pool = new_tile("last_pool", [P, T], BF16, "ks_listed1")
+        nc.gpsimd.memset(last_pool[:, stretch(0)].bitcast(I32), 0)
+        for half, cols in enumerate(first_cols):
+            nc.scalar.activation(last_pool[:, SEG + cols.start : SEG + cols.stop], v_last[half][:], ACT.Copy)
+        v_grouped01 = new_tile("v_grouped01", [P, P * PLACES], BF16, "v_last0")
+        group_values(v_grouped01[:], v_turned0[:, 1:2])
+        v_listed11 = gather_values(last_pool, 1, 1)
         for pair in range(2):
             for half in range(2):
                 part_keys(1, kw_halves, half, pair)
-        v_grouped10 = new_tile("v_grouped10", [P, P * PLACES], BF16, "kw_listed10")
-        group_values(v_grouped10[:], v_turned10[:], nc.vector.tensor_copy)
-        v_mx0 = quantize("v0", v_grouped0, DV, "kw_listed11")
-        warm_bank = new_bank("warm_bank", [P, PASSES, PASSES * NQ], "v_turned0")
+        v_mx0 = new_tile("v0_codes", [P, DV], U32, "kw_listed10"), new_tile("v0_scales", [P, DV], U8)
+        for h, grouped in enumerate((v_grouped00, v_grouped01)):
+            cols = slice(P * h, P * (h + 1))
+            nc.vector.quantize_mx(out=v_mx0[0][:, cols].bitcast(FP8X4), scales=v_mx0[1][:, cols], in_=grouped[:])
+        warm_bank = new_bank("warm_bank", [P, PASSES, PASSES * NQ], "scores13")
         for o in range(PASSES):
             nc.tensor.matmul_mx(
                 out=warm_bank[:, o, :],
@@ -285,6 +290,8 @@ def tile_attend_sigm_kb_segb2q128n512t2048_kernel(tc, q_words, q_scales, k_words
             )
         accs = [scores(b) for b in range(B)]
         prob0 = sigmoid(0, accs[0])
+        v_grouped10 = new_tile("v_grouped10", [P, P * PLACES], BF16, "k_codes0")
+        group_values(v_grouped10[:], v_turned10[:])
         v_turned11 = new_bank("v_turned11", [P, 1, 2, P], "scores01")
         turn_values(v_turned11[:, 0], v_listed11[:])
         prob1 = sigmoid(1, accs[1])
@@ -297,5 +304,5 @@ def tile_attend_sigm_kb_segb2q128n512t2048_kernel(tc, q_words, q_scales, k_words
         v_mx11 = quantize("v11", v_grouped11, P)
         w_mx1 = quantize("w1", w1, NQ)
         finish(0, w_mx0, v_mx0, slice(0, DV), "v_turned0")
-        finish(1, w_mx1, v_mx10, slice(0, P), "v_turned10")
-        finish(1, w_mx1, v_mx11, slice(P, DV), "scores00", True)
+        finish(1, w_mx1, v_mx10, slice(0, P), "v_turned10", True)
+        finish(1, w_mx1, v_mx11, slice(P, DV), "scores00")

@@ -80,8 +80,9 @@ def tile_attend_sigm_kb_segb2q128n512t2048_kernel(tc, q_words, q_scales, k_words
             nc.sync.dma_start(v_raw[b][h][:, cols], vT[P * h : P * (h + 1), SEG * b + cols.start : SEG * b + cols.stop])
 
         first_cols = [slice(0, SEG // 2), slice(SEG // 2, SEG)]
-        quarters = [slice(0, 3 * SEG // 8), slice(3 * SEG // 8, 3 * SEG // 4), slice(3 * SEG // 4, SEG)]
-        v_first = new_tile("v_first", [P, 3 * SEG // 8], F32)
+        quarters = [slice(0, 9 * SEG // 32), slice(9 * SEG // 32, 9 * SEG // 16), slice(9 * SEG // 16, SEG)]
+        second_cols = [slice(0, SEG // 4), slice(SEG // 4, SEG)]
+        v_first = new_tile("v_first", [P, 9 * SEG // 32], F32)
         nc.sync.dma_start(v_first[:], vT[0:P, quarters[0]])
 
         warm_out = new_tile("warm_out", [P, 1], F32)
@@ -97,8 +98,9 @@ def tile_attend_sigm_kb_segb2q128n512t2048_kernel(tc, q_words, q_scales, k_words
 
         for cols in quarters[1:]:
             load_values(0, 0, cols)
+        load_values(0, 1, second_cols[0])
         nc.sync.dma_start(kb_pool[ROW:P, 0:T], kb[0:1, :])
-        load_values(0, 1)
+        load_values(0, 1, second_cols[1])
         for cols in first_cols:
             load_values(1, 0, cols)
         nc.scalar.activation(first_pool[:, quarters[0]], v_first[:], ACT.Copy)
@@ -188,22 +190,24 @@ def tile_attend_sigm_kb_segb2q128n512t2048_kernel(tc, q_words, q_scales, k_words
                     )
             return acc
 
+        query_halves = [slice(0, NQ // 2), slice(NQ // 2, NQ)]
+
         def sigmoid(b, acc, takes_over=None):
             prob = new_tile("prob%d" % b, [P, PLACES, NQ], F32, takes_over)
             for place in range(PLACES):
                 bias = kb_cols[b][:, place : place + 1]
-                nc.scalar.activation(prob[:, place, :], acc[place], ACT.Sigmoid, bias=bias)
+                for queries in query_halves if (b, place) == (B - 1, PLACES - 1) else [slice(0, NQ)]:
+                    nc.scalar.activation(prob[:, place, queries], acc[place][:, queries], ACT.Sigmoid, bias=bias)
             return prob
 
-        def weigh(b, prob, token_scales, takes_over=None):
-            w = new_tile("w%d" % b, [P, NQ * PLACES], BF16, takes_over)
+        def weigh(w, prob, token_scales, queries):
+            count = queries.stop - queries.start
             nc.vector.tensor_tensor(
-                w[:].rearrange("p (c i t) -> p c t i", i=4, t=PLACES),
-                prob[:].rearrange("p t (c i) -> p c t i", i=4),
-                token_scales.unsqueeze(1).unsqueeze(3).to_broadcast([P, NQ // 4, PLACES, 4]),
+                w[:, PLACES * queries.start : PLACES * queries.stop].rearrange("p (c i t) -> p c t i", i=4, t=PLACES),
+                prob[:, :, queries].rearrange("p t (c i) -> p c t i", i=4),
+                token_scales[:].unsqueeze(1).unsqueeze(3).to_broadcast([P, count // 4, PLACES, 4]),
                 mybir.AluOpType.mult,
             )
-            return w
 
         def quantize(name, grouped, width, takes_over=None):
             codes = new_tile(name + "_codes", [P, width], U32, takes_over)
@@ -235,8 +239,9 @@ def tile_attend_sigm_kb_segb2q128n512t2048_kernel(tc, q_words, q_scales, k_words
         v_turned10 = new_bank("v_turned10", [P, 1, 2, P])
         for cols in quarters[1:]:
             round_values(first_pool, 0, 0, cols)
+        round_values(v_pool, 0, 1, second_cols[0])
         turn_values(v_turned0[:, 0], gather_values(first_pool, 0, 0)[:])
-        round_values(v_pool, 0, 1)
+        round_values(v_pool, 0, 1, second_cols[1])
         for cols in first_cols:
             round_values(v_pool, 1, 0, cols)
         v_grouped00 = new_tile("v_grouped00", [P, P * PLACES], BF16, "v_raw01")
@@ -297,12 +302,21 @@ def tile_attend_sigm_kb_segb2q128n512t2048_kernel(tc, q_words, q_scales, k_words
         prob1 = sigmoid(1, accs[1])
         v_grouped11 = new_tile("v_grouped11", [P, P * PLACES], BF16, "kb_cols1")
         group_values(v_grouped11[:], v_turned11[:])
-        w0 = weigh(0, prob0, vs_cols[0][:])
+        w0, w1 = [new_tile("w%d" % b, [P, NQ * PLACES], BF16) for b in range(B)]
+        weigh(w0, prob0, vs_cols[0], slice(0, NQ))
         v_mx10 = quantize("v10", v_grouped10, P, "vs_listed")
         w_mx0 = quantize("w0", w0, NQ)
-        w1 = weigh(1, prob1, vs_cols[1][:])
+        for queries in query_halves:
+            weigh(w1, prob1, vs_cols[1], queries)
+        w_mx1 = new_tile("w1_codes", [P, NQ], U32), new_tile("w1_scales", [P, NQ], U8)
+
+        def quantize_last_weights(cols):
+            grouped = w1[:, PLACES * cols.start : PLACES * cols.stop]
+            nc.vector.quantize_mx(out=w_mx1[0][:, cols].bitcast(FP8X4), scales=w_mx1[1][:, cols], in_=grouped)
+
+        quantize_last_weights(query_halves[0])
         v_mx11 = quantize("v11", v_grouped11, P)
-        w_mx1 = quantize("w1", w1, NQ)
+        quantize_last_weights(query_halves[1])
         finish(0, w_mx0, v_mx0, slice(0, DV), "v_turned0")
         finish(1, w_mx1, v_mx10, slice(0, P), "v_turned10", True)
         finish(1, w_mx1, v_mx11, slice(P, DV), "scores00")

@@ -105,13 +105,13 @@ def tile_attend_sigm_kb_segb2q128n512t2048_kernel(tc, q_words, q_scales, k_words
             load_values(1, 0, cols)
         nc.scalar.activation(first_pool[:, quarters[0]], v_first[:], ACT.Copy)
         scale_rows = new_tile("scale_rows", [P, B * (N + NQ)], U8, "v_first")
+        nc.sync.dma_start(vs_pool[ROW:P, :], vs[0:1, :])
+        load_keys(0)
         for b in range(B):
             nc.sync.dma_start(
                 scale_rows[KS_FIRST:P, B * N + NQ * b : B * N + NQ * (b + 1)].bitcast(I32),
                 q_scales[b].rearrange("o f q -> f o q").bitcast(I32),
             )
-        nc.sync.dma_start(vs_pool[ROW:P, :], vs[0:1, :])
-        load_keys(0)
 
         ks_listed = [new_tile("ks_listed%d" % b, [P, N], U8) for b in range(B)]
         for b in range(B):
@@ -209,11 +209,14 @@ def tile_attend_sigm_kb_segb2q128n512t2048_kernel(tc, q_words, q_scales, k_words
                 mybir.AluOpType.mult,
             )
 
-        def quantize(name, grouped, width, takes_over=None):
-            codes = new_tile(name + "_codes", [P, width], U32, takes_over)
-            scales = new_tile(name + "_scales", [P, width], U8)
-            nc.vector.quantize_mx(out=codes[:].bitcast(FP8X4), scales=scales[:], in_=grouped[:])
-            return codes, scales
+        def mx_tiles(name, width, takes_over=None):
+            return new_tile(name + "_codes", [P, width], U32, takes_over), new_tile(name + "_scales", [P, width], U8)
+
+        def quantize(mx, cols, grouped):
+            nc.vector.quantize_mx(out=mx[0][:, cols].bitcast(FP8X4), scales=mx[1][:, cols], in_=grouped)
+
+        def quantize_weights(mx, w, queries):
+            quantize(mx, queries, w[:, PLACES * queries.start : PLACES * queries.stop])
 
         def finish(b, w_mx, v_mx, cols, bank, on_vector=False):
             width = cols.stop - cols.start
@@ -278,10 +281,9 @@ def tile_attend_sigm_kb_segb2q128n512t2048_kernel(tc, q_words, q_scales, k_words
         for pair in range(2):
             for half in range(2):
                 part_keys(1, kw_halves, half, pair)
-        v_mx0 = new_tile("v0_codes", [P, DV], U32, "kw_listed10"), new_tile("v0_scales", [P, DV], U8)
-        for h, grouped in enumerate((v_grouped00, v_grouped01)):
-            cols = slice(P * h, P * (h + 1))
-            nc.vector.quantize_mx(out=v_mx0[0][:, cols].bitcast(FP8X4), scales=v_mx0[1][:, cols], in_=grouped[:])
+        v_mx0 = mx_tiles("v0", DV, "kw_listed10")
+        quantize(v_mx0, slice(0, P), v_grouped00[:])
+        quantize(v_mx0, slice(P, DV), v_grouped01[:])
         warm_bank = new_bank("warm_bank", [P, PASSES, PASSES * NQ], "scores13")
         for o in range(PASSES):
             nc.tensor.matmul_mx(
@@ -302,21 +304,15 @@ def tile_attend_sigm_kb_segb2q128n512t2048_kernel(tc, q_words, q_scales, k_words
         prob1 = sigmoid(1, accs[1])
         v_grouped11 = new_tile("v_grouped11", [P, P * PLACES], BF16, "kb_cols1")
         group_values(v_grouped11[:], v_turned11[:])
-        w0, w1 = [new_tile("w%d" % b, [P, NQ * PLACES], BF16) for b in range(B)]
-        weigh(w0, prob0, vs_cols[0], slice(0, NQ))
-        v_mx10 = quantize("v10", v_grouped10, P, "vs_listed")
-        w_mx0 = quantize("w0", w0, NQ)
-        for queries in query_halves:
-            weigh(w1, prob1, vs_cols[1], queries)
-        w_mx1 = new_tile("w1_codes", [P, NQ], U32), new_tile("w1_scales", [P, NQ], U8)
-
-        def quantize_last_weights(cols):
-            grouped = w1[:, PLACES * cols.start : PLACES * cols.stop]
-            nc.vector.quantize_mx(out=w_mx1[0][:, cols].bitcast(FP8X4), scales=w_mx1[1][:, cols], in_=grouped)
-
-        quantize_last_weights(query_halves[0])
-        v_mx11 = quantize("v11", v_grouped11, P)
-        quantize_last_weights(query_halves[1])
-        finish(0, w_mx0, v_mx0, slice(0, DV), "v_turned0")
-        finish(1, w_mx1, v_mx10, slice(0, P), "v_turned10", True)
-        finish(1, w_mx1, v_mx11, slice(P, DV), "scores00")
+        w = [new_tile("w%d" % b, [P, NQ * PLACES], BF16) for b in range(B)]
+        w_mx = [mx_tiles("w%d" % b, NQ) for b in range(B)]
+        v_mx1 = [mx_tiles("v10", P, "vs_listed"), mx_tiles("v11", P)]
+        for b, prob, grouped in ((0, prob0, v_grouped10), (1, prob1, v_grouped11)):
+            for queries in query_halves:
+                weigh(w[b], prob, vs_cols[b], queries)
+            quantize_weights(w_mx[b], w[b], query_halves[0])
+            quantize(v_mx1[b], slice(0, P), grouped[:])
+            quantize_weights(w_mx[b], w[b], query_halves[1])
+        finish(0, w_mx[0], v_mx0, slice(0, DV), "v_turned0")
+        finish(1, w_mx[1], v_mx1[0], slice(0, P), "v_turned10", True)
+        finish(1, w_mx[1], v_mx1[1], slice(P, DV), "scores00")

@@ -64,8 +64,9 @@ def tile_attend_sigm_kb_segb2q128n512t2048_kernel(tc, q_words, q_scales, k_words
         identity = new_tile("identity", [P, P], F32)
         make_identity(nc, identity[:])
         nc.gpsimd.memset(ks_pool[0:KS_FIRST, :].bitcast(I32), 0)
-        kb_pool = new_tile("kb_pool", [P, T + 1], F32)
-        nc.vector.memset(kb_pool[0:ROW, KB_SPLIT:].bitcast(I32), 0)
+        kb_pool = new_tile("kb_pool", [P, T], F32)
+        nc.vector.memset(kb_pool[0:ROW, KB_SPLIT : KB_SPLIT + 1].bitcast(I32), 0)
+        nc.vector.memset(kb_pool[0:ROW, KB_SPLIT + 1 :].bitcast(I32), 0)
         nc.gpsimd.memset(kb_pool[0:ROW, 0:KB_SPLIT].bitcast(I32), 0)
         vs_pool = new_tile("vs_pool", [P, T], F32)
         nc.gpsimd.memset(vs_pool[0:ROW, :].bitcast(I32), 0)
@@ -284,17 +285,6 @@ def tile_attend_sigm_kb_segb2q128n512t2048_kernel(tc, q_words, q_scales, k_words
         v_mx0 = mx_tiles("v0", DV, "kw_listed10")
         quantize(v_mx0, slice(0, P), v_grouped00[:])
         quantize(v_mx0, slice(P, DV), v_grouped01[:])
-        warm_bank = new_bank("warm_bank", [P, PASSES, PASSES * NQ], "scores13")
-        for o in range(PASSES):
-            nc.tensor.matmul_mx(
-                out=warm_bank[:, o, :],
-                lhsT=q_codes[0][:, o, :].bitcast(FP8X4),
-                lhsT_scale=scale_rows[:, 0:NQ],
-                rhs=q_codes[0][:].rearrange("p o q -> p (o q)").bitcast(FP8X4),
-                rhs_scale=scale_rows[:, 0 : PASSES * NQ],
-                start=True,
-                stop=True,
-            )
         accs = [scores(b) for b in range(B)]
         prob0 = sigmoid(0, accs[0])
         v_grouped10 = new_tile("v_grouped10", [P, P * PLACES], BF16, "k_codes0")

@@ -21,7 +21,6 @@ PLACES = 4
 SEG = T // B
 LIST_COLS = N // 16
 PASSES = D // (P * PLACES)
-HALVES = DV // P
 KS_FIRST = P - PASSES * 16
 ROW = P - 1
 KB_SPLIT = T // 4
@@ -43,53 +42,15 @@ def tile_attend_sigm_kb_segb2q128n512t2048_kernel(tc, q_words, q_scales, k_words
             return slice(SEG * b, SEG * (b + 1))
 
         offsets = sbuf.tile([P, B * LIST_COLS], U16, name="offsets")
+
+        def listed(window, first, count):
+            return window.indirect(offsets[:, first // 16 : (first + count) // 16])
+
         ks_pool = new_tile("ks_pool", [P, T], U8)
-        ks_rows = k_scales.rearrange("o f t -> f o t")
-
-        def load_key_scales(b):
-            nc.sync.dma_start(ks_pool[KS_FIRST:P, stretch(b)].bitcast(I32), ks_rows[:, :, stretch(b)].bitcast(I32))
-
-        load_key_scales(0)
-        nc.sync.dma_start(offsets[:], offs)
-        load_key_scales(1)
-
-        def listed_for_all(window):
-            return window.indirect(offsets[:])
-
-        def listed_for(window, b):
-            return window.indirect(offsets[:, b * LIST_COLS : (b + 1) * LIST_COLS])
-
-        warm_in = new_tile("warm_in", [P, 1], F32)
-        nc.gpsimd.memset(warm_in[:], 0.0)
-        identity = new_tile("identity", [P, P], F32)
-        make_identity(nc, identity[:])
-        nc.gpsimd.memset(ks_pool[0:KS_FIRST, :].bitcast(I32), 0)
         kb_pool = new_tile("kb_pool", [P, T], F32)
-        nc.vector.memset(kb_pool[0:ROW, KB_SPLIT : KB_SPLIT + 1].bitcast(I32), 0)
-        nc.vector.memset(kb_pool[0:ROW, KB_SPLIT + 1 :].bitcast(I32), 0)
-        nc.gpsimd.memset(kb_pool[0:ROW, 0:KB_SPLIT].bitcast(I32), 0)
         vs_pool = new_tile("vs_pool", [P, T], F32)
-        nc.gpsimd.memset(vs_pool[0:ROW, :].bitcast(I32), 0)
-
-        v_raw = [[new_tile("v_raw%d%d" % (b, h), [P, SEG], F32) for h in range(HALVES - b)] for b in range(B)]
-        first_pool = new_tile("first_pool", [P, SEG], BF16)
-        v_pool = new_tile("v_pool", [P, T], BF16)
-
-        v_last = [new_tile("v_last%d" % half, [P, SEG // 2], F32) for half in range(2)]
-
-        def load_values(b, h, cols=slice(0, SEG)):
-            nc.sync.dma_start(v_raw[b][h][:, cols], vT[P * h : P * (h + 1), SEG * b + cols.start : SEG * b + cols.stop])
-
-        first_cols = [slice(0, SEG // 2), slice(SEG // 2, SEG)]
-        quarters = [slice(0, 9 * SEG // 32), slice(9 * SEG // 32, 9 * SEG // 16), slice(9 * SEG // 16, SEG)]
-        second_cols = [slice(0, SEG // 4), slice(SEG // 4, SEG)]
-        v_first = new_tile("v_first", [P, 9 * SEG // 32], F32)
-        nc.sync.dma_start(v_first[:], vT[0:P, quarters[0]])
-
-        warm_out = new_tile("warm_out", [P, 1], F32)
-        nc.scalar.activation(warm_out[:], warm_in[:], ACT.Sigmoid)
-
         kw_pool = new_tile("kw_pool", [P, T], U32)
+        v_pool = [[new_tile("v_pool%d%d" % (b, h), [P, SEG * (b + 1)], F32) for h in range(2)] for b in range(B)]
         kw_bytes = k_words[0].rearrange("p t c -> p (t c)")
 
         def load_keys(b):
@@ -97,54 +58,81 @@ def tile_attend_sigm_kb_segb2q128n512t2048_kernel(tc, q_words, q_scales, k_words
                 kw_pool[:, stretch(b)].bitcast(I32), kw_bytes[:, 4 * SEG * b : 4 * SEG * (b + 1)].bitcast(I32)
             )
 
-        for cols in quarters[1:]:
-            load_values(0, 0, cols)
-        load_values(0, 1, second_cols[0])
-        nc.sync.dma_start(kb_pool[ROW:P, 0:T], kb[0:1, :])
-        load_values(0, 1, second_cols[1])
-        for cols in first_cols:
-            load_values(1, 0, cols)
-        nc.scalar.activation(first_pool[:, quarters[0]], v_first[:], ACT.Copy)
-        scale_rows = new_tile("scale_rows", [P, B * (N + NQ)], U8, "v_first")
+        def load_values(b, h):
+            nc.sync.dma_start(v_pool[b][h][:, stretch(b)], vT[P * h : P * (h + 1), stretch(b)])
+
+        nc.sync.dma_start(ks_pool[KS_FIRST:P, :].bitcast(I32), k_scales.rearrange("o f t -> f o t").bitcast(I32))
+        nc.scalar.dma_start(kb_pool[ROW:P, :], kb[0:1, :])
+        nc.sync.dma_start(offsets[:], offs)
         nc.sync.dma_start(vs_pool[ROW:P, :], vs[0:1, :])
         load_keys(0)
-        for b in range(B):
-            nc.sync.dma_start(
-                scale_rows[KS_FIRST:P, B * N + NQ * b : B * N + NQ * (b + 1)].bitcast(I32),
-                q_scales[b].rearrange("o f q -> f o q").bitcast(I32),
-            )
+        load_values(0, 0)
+        q_planes = new_tile("q_planes", [P, B * PASSES, NQ], U8)
+        q_rows = q_scales.rearrange("b o f q -> f (b o) q")
+        for c in range(4):
+            nc.sync.dma_start(q_planes[32 * c : 32 * c + 4, :, :].bitcast(I32), q_rows[4 * c : 4 * c + 4].bitcast(I32))
+        load_keys(1)
+        q_codes = new_tile("q_codes", [P, B * PASSES, NQ], U32)
+        nc.sync.dma_start(q_codes[:].bitcast(I32), q_words.rearrange("b o p q c -> p (b o) (q c)").bitcast(I32))
 
-        ks_listed = [new_tile("ks_listed%d" % b, [P, N], U8) for b in range(B)]
-        for b in range(B):
-            nc.vector.tensor_copy(ks_listed[b][:], listed_for(ks_pool[:, 0 : SEG * (b + 1)], b))
+        warm_in = new_tile("warm_in", [P, 1], F32)
+        nc.gpsimd.memset(warm_in[:], 0.0)
+        warm_out = new_tile("warm_out", [P, 1], F32)
+        nc.scalar.activation(warm_out[:], warm_in[:], ACT.Sigmoid)
+        nc.gpsimd.memset(ks_pool[0:KS_FIRST, :].bitcast(I32), 0)
+        nc.vector.memset(kb_pool[0:ROW, KB_SPLIT : KB_SPLIT + 1].bitcast(I32), 0)
+        nc.vector.memset(kb_pool[0:ROW, KB_SPLIT + 1 :].bitcast(I32), 0)
+        nc.gpsimd.memset(kb_pool[0:ROW, 0:KB_SPLIT].bitcast(I32), 0)
+        identity = new_tile("identity", [P, P], F32)
+        make_identity(nc, identity[:])
+        nc.gpsimd.memset(vs_pool[0:ROW, :].bitcast(I32), 0)
+        for h in range(2):
+            nc.gpsimd.memset(v_pool[1][h][:, stretch(0)].bitcast(I32), 0)
+
+        ks_listed = new_tile("ks_listed", [P, B * N], U8)
         for b in range(B):
             nc.vector.tensor_copy(
-                scale_rows[:, N * b : N * (b + 1)].rearrange("p (t m) -> p t m", t=PLACES),
-                ks_listed[b][:].rearrange("p (m t) -> p t m", t=PLACES),
+                ks_listed[:, N * b : N * (b + 1)].rearrange("p (t m) -> p m t", t=PLACES), listed(ks_pool[:], N * b, N)
             )
-        planes = new_tile("planes", [P, PASSES, B * (N + NQ)], U8)
+        planes = new_tile("planes", [P, PASSES, B * N], U8)
+        for c in (0, 2, 1, 3):
+            first = KS_FIRST + 8 * c
+            nc.sync.dma_start(planes[32 * c : 32 * c + 4, :, :].bitcast(I32), ks_listed[first : first + 8, :].bitcast(I32))
 
-        kb_listed = new_tile("kb_listed", [P, B * N], F32)
-        nc.vector.tensor_copy(kb_listed[:], listed_for_all(kb_pool[:, 0:T]))
+        def gather_row(name, pool, first, count, takes_over=None):
+            row = new_tile(name, [P, count], F32, takes_over)
+            nc.scalar.activation(row[:], listed(pool[:], first, count), ACT.Copy)
+            return row
 
-        def load_queries(b):
-            codes = new_tile("q_codes%d" % b, [P, PASSES, NQ], U32)
-            nc.sync.dma_start(codes[:].bitcast(I32), q_words[b].rearrange("o p q c -> p o (q c)").bitcast(I32))
-            return codes
-
-        def deal_out(name, listed, b):
-            cols = new_tile("%s%d" % (name, b), [P, PLACES], F32)
-            nc.sync.dma_start(cols[:], listed[ROW:P, N * b : N * (b + 1)].rearrange("r (m t) -> r m t", t=PLACES))
+        def deal_out(name, row):
+            cols = new_tile(name, [P, PLACES], F32)
+            nc.sync.dma_start(cols[:], row[ROW:P, :].rearrange("r (m t) -> r m t", t=PLACES))
             return cols
+
+        def gather_values(engine, v_listed, b, h, first=0, count=N):
+            window = listed(v_pool[b][h][:], N * b + first, count)
+            if engine is nc.scalar:
+                nc.scalar.activation(v_listed[:, first : first + count], window, ACT.Copy)
+            else:
+                nc.vector.tensor_copy(v_listed[:, first : first + count], window)
+
+        def turn_values(name, v_listed, takes_over=None):
+            bank = new_bank(name, [P, 2, P], takes_over)
+            words = v_listed[:].bitcast(F32)
+            for u in range(2):
+                nc.tensor.transpose(bank[:, u, :], words[:, u : N // 2 : 2], identity[:])
+            return bank
+
+        def group_values(grouped, bank):
+            nc.scalar.copy(grouped.bitcast(F32).rearrange("p (f u) -> p f u", u=2), bank[:].rearrange("p u f -> p f u"))
 
         k_codes = [new_tile("k_codes%d" % b, [P, PLACES, PASSES, P], U16) for b in range(B)]
 
         def gather_keys(b):
             halves = [new_tile("kw_listed%d%d" % (b, half), [P, N // 2], U32) for half in range(2)]
             for half in range(2):
-                first = b * LIST_COLS + half * LIST_COLS // 2
                 window = kw_pool[:, 0 : SEG * (b + 1)]
-                nc.vector.tensor_copy(halves[half][:], window.indirect(offsets[:, first : first + LIST_COLS // 2]))
+                nc.vector.tensor_copy(halves[half][:], listed(window, N * b + half * N // 2, N // 2))
             return halves
 
         def part_keys(b, halves, half, pair):
@@ -152,24 +140,6 @@ def tile_attend_sigm_kb_segb2q128n512t2048_kernel(tc, q_words, q_scales, k_words
             paired = halves[half][:].bitcast(U16).rearrange("p (x y t o) -> p o x t y", t=PLACES, y=4, o=PASSES)
             places = slice(2 * pair, 2 * pair + 2)
             nc.vector.tensor_copy(parted[:, half, :, :, places, :], paired[:, :, :, places, :])
-
-        def round_values(pool, b, h, cols=slice(0, SEG)):
-            nc.scalar.activation(pool[:, SEG * b + cols.start : SEG * b + cols.stop], v_raw[b][h][:, cols], ACT.Copy)
-
-        def gather_values(pool, b, h, takes_over=None):
-            v_listed = new_tile("v_listed%d%d" % (b, h), [P, N], BF16, takes_over)
-            nc.scalar.activation(v_listed[:], listed_for(pool[:], b), ACT.Copy)
-            return v_listed
-
-        def turn_values(bank, v_listed):
-            words = v_listed.bitcast(F32)
-            for u in range(2):
-                nc.tensor.transpose(bank[:, u, :], words[:, u : N // 2 : 2], identity[:])
-
-        def group_values(grouped, bank, copy=nc.scalar.copy):
-            copy(
-                grouped.bitcast(F32).rearrange("p (h f u) -> p h f u", f=P, u=2), bank.rearrange("p h u f -> p h f u")
-            )
 
         def scores(b):
             if b == 0:
@@ -184,40 +154,38 @@ def tile_attend_sigm_kb_segb2q128n512t2048_kernel(tc, q_words, q_scales, k_words
                         out=acc[place],
                         lhsT=k_codes[b][:, place, o, :].bitcast(FP4X4),
                         lhsT_scale=planes[:, o, plane_cols],
-                        rhs=q_codes[b][:, o, :].bitcast(FP8X4),
-                        rhs_scale=planes[:, o, B * N + NQ * b : B * N + NQ * (b + 1)],
+                        rhs=q_codes[:, PASSES * b + o, :].bitcast(FP8X4),
+                        rhs_scale=q_planes[:, PASSES * b + o, :],
                         start=(o == 0),
                         stop=(o == PASSES - 1),
                     )
             return acc
 
-        query_halves = [slice(0, NQ // 2), slice(NQ // 2, NQ)]
-
         def sigmoid(b, acc, takes_over=None):
             prob = new_tile("prob%d" % b, [P, PLACES, NQ], F32, takes_over)
             for place in range(PLACES):
-                bias = kb_cols[b][:, place : place + 1]
-                for queries in query_halves if (b, place) == (B - 1, PLACES - 1) else [slice(0, NQ)]:
-                    nc.scalar.activation(prob[:, place, queries], acc[place][:, queries], ACT.Sigmoid, bias=bias)
+                nc.scalar.activation(prob[:, place, :], acc[place], ACT.Sigmoid, bias=kb_cols[b][:, place : place + 1])
             return prob
 
-        def weigh(w, prob, token_scales, queries):
-            count = queries.stop - queries.start
-            nc.vector.tensor_tensor(
-                w[:, PLACES * queries.start : PLACES * queries.stop].rearrange("p (c i t) -> p c t i", i=4, t=PLACES),
-                prob[:, :, queries].rearrange("p t (c i) -> p c t i", i=4),
-                token_scales[:].unsqueeze(1).unsqueeze(3).to_broadcast([P, count // 4, PLACES, 4]),
-                mybir.AluOpType.mult,
-            )
+        query_halves = [slice(0, NQ // 2), slice(NQ // 2, NQ)]
+
+        def weigh(b, token_scales):
+            for queries in query_halves:
+                nc.vector.tensor_tensor(
+                    w[b][:, PLACES * queries.start : PLACES * queries.stop].rearrange("p (c i t) -> p c t i", i=4, t=PLACES),
+                    prob[b][:, :, queries].rearrange("p t (c i) -> p c t i", i=4),
+                    token_scales[:].unsqueeze(1).unsqueeze(3).to_broadcast([P, NQ // 8, PLACES, 4]),
+                    mybir.AluOpType.mult,
+                )
+
+        def quantize_weights(b, queries):
+            quantize(w_mx[b], queries, w[b][:, PLACES * queries.start : PLACES * queries.stop])
 
         def mx_tiles(name, width, takes_over=None):
             return new_tile(name + "_codes", [P, width], U32, takes_over), new_tile(name + "_scales", [P, width], U8)
 
         def quantize(mx, cols, grouped):
             nc.vector.quantize_mx(out=mx[0][:, cols].bitcast(FP8X4), scales=mx[1][:, cols], in_=grouped)
-
-        def quantize_weights(mx, w, queries):
-            quantize(mx, queries, w[:, PLACES * queries.start : PLACES * queries.stop])
 
         def finish(b, w_mx, v_mx, cols, bank, on_vector=False):
             width = cols.stop - cols.start
@@ -239,70 +207,55 @@ def tile_attend_sigm_kb_segb2q128n512t2048_kernel(tc, q_words, q_scales, k_words
                 nc.scalar.activation(y[:], acc[:], ACT.Copy, scale=1.0 / 16.0)
                 (nc.scalar if b else nc.sync).dma_start(out[b][:, cols], y[:])
 
-        v_turned0 = new_bank("v_turned0", [P, HALVES, 2, P])
-        v_turned10 = new_bank("v_turned10", [P, 1, 2, P])
-        for cols in quarters[1:]:
-            round_values(first_pool, 0, 0, cols)
-        round_values(v_pool, 0, 1, second_cols[0])
-        turn_values(v_turned0[:, 0], gather_values(first_pool, 0, 0)[:])
-        round_values(v_pool, 0, 1, second_cols[1])
-        for cols in first_cols:
-            round_values(v_pool, 1, 0, cols)
-        v_grouped00 = new_tile("v_grouped00", [P, P * PLACES], BF16, "v_raw01")
-        group_values(v_grouped00[:], v_turned0[:, 0:1])
-        turn_values(v_turned0[:, 1], gather_values(v_pool, 0, 1)[:])
-        turn_values(v_turned10[:, 0], gather_values(v_pool, 1, 0)[:])
-        for half, cols in enumerate(first_cols):
-            nc.sync.dma_start(v_last[half][:], vT[P : 2 * P, SEG + cols.start : SEG + cols.stop])
-        load_keys(1)
-        q_codes = [load_queries(0)]
-        kb_cols = [deal_out("kb_cols", kb_listed, 0)]
-        for c in (0, 2, 1, 3):
-            first = KS_FIRST + 8 * c
-            nc.sync.dma_start(planes[32 * c : 32 * c + 4, :, :].bitcast(I32), scale_rows[first : first + 8, :].bitcast(I32))
-        q_codes.append(load_queries(1))
-        kb_cols.append(deal_out("kb_cols", kb_listed, 1))
-        vs_listed = new_tile("vs_listed", [P, B * N], F32)
-        nc.vector.tensor_copy(vs_listed[:], listed_for_all(vs_pool[:]))
-        kw_halves = gather_keys(0)
-        for half in range(2):
-            for pair in range(2):
-                part_keys(0, kw_halves, half, pair)
-        vs_cols = [deal_out("vs_cols", vs_listed, b) for b in range(B)]
-        kw_halves = gather_keys(1)
+        v_listed = [[new_tile("v_listed%d%d" % (b, h), [P, N], BF16) for h in range(2)] for b in range(B)]
 
+        kb_listed = gather_row("kb_listed", kb_pool, 0, B * N)
+        kb_cols = [deal_out("kb_cols%d" % b, kb_listed[:, N * b : N * (b + 1)]) for b in range(B)]
+        load_values(0, 1)
+        load_values(1, 0)
+        vs_cols0 = deal_out("vs_cols0", gather_row("vs_listed0", vs_pool, 0, N))
+        load_values(1, 1)
+        gather_values(nc.scalar, v_listed[0][0], 0, 0)
+        vs_cols1 = deal_out("vs_cols1", gather_row("vs_listed1", vs_pool, N, N, "v_pool00"))
+        turned00 = turn_values("turned00", v_listed[0][0])
+        grouped00 = new_tile("grouped00", [P, P * PLACES], BF16, "vs_pool")
+        group_values(grouped00[:], turned00)
 
-        last_pool = new_tile("last_pool", [P, T], BF16, "ks_listed1")
-        nc.gpsimd.memset(last_pool[:, stretch(0)].bitcast(I32), 0)
-        for half, cols in enumerate(first_cols):
-            nc.scalar.activation(last_pool[:, SEG + cols.start : SEG + cols.stop], v_last[half][:], ACT.Copy)
-        v_grouped01 = new_tile("v_grouped01", [P, P * PLACES], BF16, "v_last0")
-        group_values(v_grouped01[:], v_turned0[:, 1:2])
-        v_listed11 = gather_values(last_pool, 1, 1)
-        for pair in range(2):
+        for b in range(B):
+            kw_halves = gather_keys(b)
             for half in range(2):
-                part_keys(1, kw_halves, half, pair)
-        v_mx0 = mx_tiles("v0", DV, "kw_listed10")
-        quantize(v_mx0, slice(0, P), v_grouped00[:])
-        quantize(v_mx0, slice(P, DV), v_grouped01[:])
+                for pair in range(2):
+                    part_keys(b, kw_halves, half, pair)
         accs = [scores(b) for b in range(B)]
-        prob0 = sigmoid(0, accs[0])
-        v_grouped10 = new_tile("v_grouped10", [P, P * PLACES], BF16, "k_codes0")
-        group_values(v_grouped10[:], v_turned10[:])
-        v_turned11 = new_bank("v_turned11", [P, 1, 2, P], "scores01")
-        turn_values(v_turned11[:, 0], v_listed11[:])
-        prob1 = sigmoid(1, accs[1])
-        v_grouped11 = new_tile("v_grouped11", [P, P * PLACES], BF16, "kb_cols1")
-        group_values(v_grouped11[:], v_turned11[:])
+        prob = [sigmoid(b, accs[b]) for b in range(B)]
         w = [new_tile("w%d" % b, [P, NQ * PLACES], BF16) for b in range(B)]
         w_mx = [mx_tiles("w%d" % b, NQ) for b in range(B)]
-        v_mx1 = [mx_tiles("v10", P, "vs_listed"), mx_tiles("v11", P)]
-        for b, prob, grouped in ((0, prob0, v_grouped10), (1, prob1, v_grouped11)):
-            for queries in query_halves:
-                weigh(w[b], prob, vs_cols[b], queries)
-            quantize_weights(w_mx[b], w[b], query_halves[0])
-            quantize(v_mx1[b], slice(0, P), grouped[:])
-            quantize_weights(w_mx[b], w[b], query_halves[1])
-        finish(0, w_mx[0], v_mx0, slice(0, DV), "v_turned0")
-        finish(1, w_mx[1], v_mx1[0], slice(0, P), "v_turned10", True)
-        finish(1, w_mx[1], v_mx1[1], slice(P, DV), "scores00")
+        v_mx0 = mx_tiles("v0", DV, "v_pool01")
+        v_mx1 = [mx_tiles("v1%d" % h, P) for h in range(2)]
+        gather_values(nc.vector, v_listed[0][1], 0, 1)
+        quantize(v_mx0, slice(0, P), grouped00[:])
+        turned01 = turn_values("turned01", v_listed[0][1], "scores00")
+        gather_values(nc.vector, v_listed[1][0], 1, 0, 0, N // 2)
+        gather_values(nc.scalar, v_listed[1][0], 1, 0, N // 2, N // 2)
+        turned10 = turn_values("turned10", v_listed[1][0], "scores01")
+        weigh(0, vs_cols0)
+        for queries in query_halves:
+            quantize_weights(0, queries)
+        gather_values(nc.vector, v_listed[1][1], 1, 1, 0, N // 2)
+        gather_values(nc.scalar, v_listed[1][1], 1, 1, N // 2, N // 2)
+        turned11 = turn_values("turned11", v_listed[1][1])
+        grouped_late = new_tile("grouped_late", [P, 2 * P * PLACES], BF16, "v_pool11")
+        grouped01, grouped10 = grouped_late[:, 0 : P * PLACES], grouped_late[:, P * PLACES :]
+        group_values(grouped01, turned01)
+        group_values(grouped10, turned10)
+        grouped11 = new_tile("grouped11", [P, P * PLACES], BF16)
+        group_values(grouped11[:], turned11)
+        weigh(1, vs_cols1)
+        quantize(v_mx0, slice(P, DV), grouped01)
+        quantize_weights(1, query_halves[0])
+        quantize(v_mx1[0], slice(0, P), grouped10)
+        quantize_weights(1, query_halves[1])
+        quantize(v_mx1[1], slice(0, P), grouped11[:])
+        finish(0, w_mx[0], v_mx0, slice(0, DV), "turned00")
+        finish(1, w_mx[1], v_mx1[0], slice(0, P), "scores10", True)
+        finish(1, w_mx[1], v_mx1[1], slice(P, DV), "scores11")

@@ -30,6 +30,7 @@ def tile_attend_sigm_kb_segb2q128n512t2048_kernel(tc, q_words, q_scales, k_words
     nc = tc.nc
     with ExitStack() as ctx:
         sbuf = ctx.enter_context(tc.tile_pool(name="sbuf", bufs=1))
+        placed = ctx.enter_context(tc.tile_pool(name="placed", bufs=1))
         psum = ctx.enter_context(tc.psum_pool(name="psum", bufs=1))
 
         def new_tile(name, shape, dtype, takes_over=None):
@@ -50,13 +51,11 @@ def tile_attend_sigm_kb_segb2q128n512t2048_kernel(tc, q_words, q_scales, k_words
         kb_pool = new_tile("kb_pool", [P, T], F32)
         vs_pool = new_tile("vs_pool", [P, T], F32)
         kw_pool = new_tile("kw_pool", [P, T], U32)
-        v_pool = [[new_tile("v_pool%d%d" % (b, h), [P, SEG * (b + 1)], F32) for h in range(2)] for b in range(B)]
+        v_pool = [
+            [new_tile("v_pool00", [P, SEG], F32), placed.tile([P, SEG], F32, name="v_pool01", align_bytes=64, offset=0)],
+            [new_tile("v_pool10", [P, T], F32), placed.tile([P, T], F32, name="v_pool11", align_bytes=64, offset=4 * SEG)],
+        ]
         kw_bytes = k_words[0].rearrange("p t c -> p (t c)")
-
-        def load_keys(b):
-            nc.sync.dma_start(
-                kw_pool[:, stretch(b)].bitcast(I32), kw_bytes[:, 4 * SEG * b : 4 * SEG * (b + 1)].bitcast(I32)
-            )
 
         def load_values(b, h):
             nc.sync.dma_start(v_pool[b][h][:, stretch(b)], vT[P * h : P * (h + 1), stretch(b)])
@@ -65,13 +64,12 @@ def tile_attend_sigm_kb_segb2q128n512t2048_kernel(tc, q_words, q_scales, k_words
         nc.scalar.dma_start(kb_pool[ROW:P, :], kb[0:1, :])
         nc.sync.dma_start(offsets[:], offs)
         nc.sync.dma_start(vs_pool[ROW:P, :], vs[0:1, :])
-        load_keys(0)
-        load_values(0, 0)
+        nc.sync.dma_start(kw_pool[:].bitcast(I32), kw_bytes.bitcast(I32))
         q_planes = new_tile("q_planes", [P, B * PASSES, NQ], U8)
         q_rows = q_scales.rearrange("b o f q -> f (b o) q")
         for c in range(4):
             nc.sync.dma_start(q_planes[32 * c : 32 * c + 4, :, :].bitcast(I32), q_rows[4 * c : 4 * c + 4].bitcast(I32))
-        load_keys(1)
+        load_values(0, 0)
         q_codes = new_tile("q_codes", [P, B * PASSES, NQ], U32)
         nc.sync.dma_start(q_codes[:].bitcast(I32), q_words.rearrange("b o p q c -> p (b o) (q c)").bitcast(I32))
 
@@ -79,12 +77,12 @@ def tile_attend_sigm_kb_segb2q128n512t2048_kernel(tc, q_words, q_scales, k_words
         nc.gpsimd.memset(warm_in[:], 0.0)
         warm_out = new_tile("warm_out", [P, 1], F32)
         nc.scalar.activation(warm_out[:], warm_in[:], ACT.Sigmoid)
+        identity = new_tile("identity", [P, P], F32)
+        make_identity(nc, identity[:])
         nc.gpsimd.memset(ks_pool[0:KS_FIRST, :].bitcast(I32), 0)
         nc.vector.memset(kb_pool[0:ROW, KB_SPLIT : KB_SPLIT + 1].bitcast(I32), 0)
         nc.vector.memset(kb_pool[0:ROW, KB_SPLIT + 1 :].bitcast(I32), 0)
         nc.gpsimd.memset(kb_pool[0:ROW, 0:KB_SPLIT].bitcast(I32), 0)
-        identity = new_tile("identity", [P, P], F32)
-        make_identity(nc, identity[:])
         nc.gpsimd.memset(vs_pool[0:ROW, :].bitcast(I32), 0)
         for h in range(2):
             nc.gpsimd.memset(v_pool[1][h][:, stretch(0)].bitcast(I32), 0)
@@ -99,15 +97,10 @@ def tile_attend_sigm_kb_segb2q128n512t2048_kernel(tc, q_words, q_scales, k_words
             first = KS_FIRST + 8 * c
             nc.sync.dma_start(planes[32 * c : 32 * c + 4, :, :].bitcast(I32), ks_listed[first : first + 8, :].bitcast(I32))
 
-        def gather_row(name, pool, first, count, takes_over=None):
-            row = new_tile(name, [P, count], F32, takes_over)
-            nc.scalar.activation(row[:], listed(pool[:], first, count), ACT.Copy)
+        def gather_row(name, pool, b):
+            row = new_tile(name, [P, N], F32)
+            nc.scalar.activation(row[:], listed(pool[:], N * b, N), ACT.Copy)
             return row
-
-        def deal_out(name, row):
-            cols = new_tile(name, [P, PLACES], F32)
-            nc.sync.dma_start(cols[:], row[ROW:P, :].rearrange("r (m t) -> r m t", t=PLACES))
-            return cols
 
         def gather_values(engine, v_listed, b, h, first=0, count=N):
             window = listed(v_pool[b][h][:], N * b + first, count)
@@ -123,6 +116,12 @@ def tile_attend_sigm_kb_segb2q128n512t2048_kernel(tc, q_words, q_scales, k_words
                 nc.tensor.transpose(bank[:, u, :], words[:, u : N // 2 : 2], identity[:])
             return bank
 
+        def turn_row(name, row):
+            bank = new_bank(name, [P, PLACES, P])
+            for place in range(PLACES):
+                nc.tensor.transpose(bank[:, place, :], row[:, place:N:PLACES], identity[:])
+            return bank[:, :, ROW:P]
+
         def group_values(grouped, bank):
             nc.scalar.copy(grouped.bitcast(F32).rearrange("p (f u) -> p f u", u=2), bank[:].rearrange("p u f -> p f u"))
 
@@ -131,8 +130,7 @@ def tile_attend_sigm_kb_segb2q128n512t2048_kernel(tc, q_words, q_scales, k_words
         def gather_keys(b):
             halves = [new_tile("kw_listed%d%d" % (b, half), [P, N // 2], U32) for half in range(2)]
             for half in range(2):
-                window = kw_pool[:, 0 : SEG * (b + 1)]
-                nc.vector.tensor_copy(halves[half][:], listed(window, N * b + half * N // 2, N // 2))
+                nc.vector.tensor_copy(halves[half][:], listed(kw_pool[:], N * b + half * N // 2, N // 2))
             return halves
 
         def part_keys(b, halves, half, pair):
@@ -146,7 +144,7 @@ def tile_attend_sigm_kb_segb2q128n512t2048_kernel(tc, q_words, q_scales, k_words
                 banks = [new_bank("scores0%d" % pair, [P, 2, NQ]) for pair in range(PLACES // 2)]
                 acc = [banks[place // 2][:, place % 2, :] for place in range(PLACES)]
             else:
-                acc = [new_bank("scores1%d" % place, [P, NQ])[:] for place in range(PLACES)]
+                acc = [new_bank("scores1%d" % place, [P, NQ], row_banks[place])[:] for place in range(PLACES)]
             for place in range(PLACES):
                 plane_cols = slice(N * b + place * P, N * b + (place + 1) * P)
                 for o in range(PASSES):
@@ -161,20 +159,18 @@ def tile_attend_sigm_kb_segb2q128n512t2048_kernel(tc, q_words, q_scales, k_words
                     )
             return acc
 
-        def sigmoid(b, acc, takes_over=None):
-            prob = new_tile("prob%d" % b, [P, PLACES, NQ], F32, takes_over)
+        def sigmoid(b):
             for place in range(PLACES):
-                nc.scalar.activation(prob[:, place, :], acc[place], ACT.Sigmoid, bias=kb_cols[b][:, place : place + 1])
-            return prob
+                nc.scalar.activation(prob[b][:, place, :], accs[b][place], ACT.Sigmoid, bias=cols[:, b, place : place + 1])
 
         query_halves = [slice(0, NQ // 2), slice(NQ // 2, NQ)]
 
-        def weigh(b, token_scales):
+        def weigh(b):
             for queries in query_halves:
                 nc.vector.tensor_tensor(
                     w[b][:, PLACES * queries.start : PLACES * queries.stop].rearrange("p (c i t) -> p c t i", i=4, t=PLACES),
                     prob[b][:, :, queries].rearrange("p t (c i) -> p c t i", i=4),
-                    token_scales[:].unsqueeze(1).unsqueeze(3).to_broadcast([P, NQ // 8, PLACES, 4]),
+                    cols[:, B + b, :].unsqueeze(1).unsqueeze(3).to_broadcast([P, NQ // 8, PLACES, 4]),
                     mybir.AluOpType.mult,
                 )
 
@@ -209,16 +205,18 @@ def tile_attend_sigm_kb_segb2q128n512t2048_kernel(tc, q_words, q_scales, k_words
 
         v_listed = [[new_tile("v_listed%d%d" % (b, h), [P, N], BF16) for h in range(2)] for b in range(B)]
 
-        kb_listed = gather_row("kb_listed", kb_pool, 0, B * N)
-        kb_cols = [deal_out("kb_cols%d" % b, kb_listed[:, N * b : N * (b + 1)]) for b in range(B)]
         load_values(0, 1)
         load_values(1, 0)
-        vs_cols0 = deal_out("vs_cols0", gather_row("vs_listed0", vs_pool, 0, N))
         load_values(1, 1)
+        row_banks = ["kb_turned0", "kb_turned1", "vs_turned0", "vs_turned1"]
+        rows = [gather_row("%s_listed%d" % (name, b), pool, b) for name, pool in (("kb", kb_pool), ("vs", vs_pool)) for b in range(B)]
+        turned_rows = [turn_row(name, row) for name, row in zip(row_banks, rows)]
         gather_values(nc.scalar, v_listed[0][0], 0, 0)
-        vs_cols1 = deal_out("vs_cols1", gather_row("vs_listed1", vs_pool, N, N, "v_pool00"))
+        cols = new_tile("cols", [P, 2 * B, PLACES], F32, "v_pool00")
+        for j, turned in enumerate(turned_rows):
+            nc.scalar.copy(cols[:, j, :].unsqueeze(2), turned)
         turned00 = turn_values("turned00", v_listed[0][0])
-        grouped00 = new_tile("grouped00", [P, P * PLACES], BF16, "vs_pool")
+        grouped00 = new_tile("grouped00", [P, P * PLACES], BF16)
         group_values(grouped00[:], turned00)
 
         for b in range(B):
@@ -227,35 +225,38 @@ def tile_attend_sigm_kb_segb2q128n512t2048_kernel(tc, q_words, q_scales, k_words
                 for pair in range(2):
                     part_keys(b, kw_halves, half, pair)
         accs = [scores(b) for b in range(B)]
-        prob = [sigmoid(b, accs[b]) for b in range(B)]
-        w = [new_tile("w%d" % b, [P, NQ * PLACES], BF16) for b in range(B)]
         w_mx = [mx_tiles("w%d" % b, NQ) for b in range(B)]
-        v_mx0 = mx_tiles("v0", DV, "v_pool01")
         v_mx1 = [mx_tiles("v1%d" % h, P) for h in range(2)]
+        prob = [new_tile("prob%d" % b, [P, PLACES, NQ], F32) for b in range(B)]
+        for b in range(B):
+            sigmoid(b)
         gather_values(nc.vector, v_listed[0][1], 0, 1)
+        v_mx0 = (placed.tile([P, DV], U32, name="v0_codes", align_bytes=64, offset=0), new_tile("v0_scales", [P, DV], U8))
+        w = [placed.tile([P, NQ * PLACES], BF16, name="w0", align_bytes=64, offset=4 * DV)]
         quantize(v_mx0, slice(0, P), grouped00[:])
         turned01 = turn_values("turned01", v_listed[0][1], "scores00")
+        weigh(0)
+        for queries in query_halves:
+            quantize_weights(0, queries)
         gather_values(nc.vector, v_listed[1][0], 1, 0, 0, N // 2)
         gather_values(nc.scalar, v_listed[1][0], 1, 0, N // 2, N // 2)
         turned10 = turn_values("turned10", v_listed[1][0], "scores01")
-        weigh(0, vs_cols0)
-        for queries in query_halves:
-            quantize_weights(0, queries)
         gather_values(nc.vector, v_listed[1][1], 1, 1, 0, N // 2)
         gather_values(nc.scalar, v_listed[1][1], 1, 1, N // 2, N // 2)
         turned11 = turn_values("turned11", v_listed[1][1])
-        grouped_late = new_tile("grouped_late", [P, 2 * P * PLACES], BF16, "v_pool11")
+        grouped_late = placed.tile([P, 2 * P * PLACES], BF16, name="grouped_late", align_bytes=64, offset=4 * SEG)
+        w.append(placed.tile([P, NQ * PLACES], BF16, name="w1", align_bytes=64, offset=4 * T))
         grouped01, grouped10 = grouped_late[:, 0 : P * PLACES], grouped_late[:, P * PLACES :]
         group_values(grouped01, turned01)
         group_values(grouped10, turned10)
         grouped11 = new_tile("grouped11", [P, P * PLACES], BF16)
         group_values(grouped11[:], turned11)
-        weigh(1, vs_cols1)
+        weigh(1)
         quantize(v_mx0, slice(P, DV), grouped01)
         quantize_weights(1, query_halves[0])
         quantize(v_mx1[0], slice(0, P), grouped10)
         quantize_weights(1, query_halves[1])
         quantize(v_mx1[1], slice(0, P), grouped11[:])
         finish(0, w_mx[0], v_mx0, slice(0, DV), "turned00")
-        finish(1, w_mx[1], v_mx1[0], slice(0, P), "scores10", True)
-        finish(1, w_mx[1], v_mx1[1], slice(P, DV), "scores11")
+        finish(1, w_mx[1], v_mx1[0], slice(0, P), row_banks[0], True)
+        finish(1, w_mx[1], v_mx1[1], slice(P, DV), row_banks[1])

@@ -51,14 +51,10 @@ def tile_attend_sigm_kb_segb2q128n512t2048_kernel(tc, q_words, q_scales, k_words
         kb_pool = new_tile("kb_pool", [P, T], F32)
         vs_pool = new_tile("vs_pool", [P, T], F32)
         kw_pool = new_tile("kw_pool", [P, T], U32)
-        v_pool = [
-            [new_tile("v_pool00", [P, SEG], F32), placed.tile([P, SEG], F32, name="v_pool01", align_bytes=64, offset=0)],
-            [new_tile("v_pool10", [P, T], F32), placed.tile([P, T], F32, name="v_pool11", align_bytes=64, offset=4 * SEG)],
-        ]
+        v_low = new_tile("v_low", [P, T], F32)
+        v_high = [new_tile("v_high0", [P, SEG], F32), placed.tile([P, T], F32, name="v_high1", align_bytes=64, offset=0)]
+        v_pool = [[v_low, v_high[b]] for b in range(B)]
         kw_bytes = k_words[0].rearrange("p t c -> p (t c)")
-
-        def load_values(b, h):
-            nc.sync.dma_start(v_pool[b][h][:, stretch(b)], vT[P * h : P * (h + 1), stretch(b)])
 
         nc.sync.dma_start(ks_pool[KS_FIRST:P, :].bitcast(I32), k_scales.rearrange("o f t -> f o t").bitcast(I32))
         nc.scalar.dma_start(kb_pool[ROW:P, :], kb[0:1, :])
@@ -69,7 +65,7 @@ def tile_attend_sigm_kb_segb2q128n512t2048_kernel(tc, q_words, q_scales, k_words
         q_rows = q_scales.rearrange("b o f q -> f (b o) q")
         for c in range(4):
             nc.sync.dma_start(q_planes[32 * c : 32 * c + 4, :, :].bitcast(I32), q_rows[4 * c : 4 * c + 4].bitcast(I32))
-        load_values(0, 0)
+        nc.sync.dma_start(v_low[:], vT[0:P, :])
         q_codes = new_tile("q_codes", [P, B * PASSES, NQ], U32)
         nc.sync.dma_start(q_codes[:].bitcast(I32), q_words.rearrange("b o p q c -> p (b o) (q c)").bitcast(I32))
 
@@ -84,8 +80,7 @@ def tile_attend_sigm_kb_segb2q128n512t2048_kernel(tc, q_words, q_scales, k_words
         nc.vector.memset(kb_pool[0:ROW, KB_SPLIT + 1 :].bitcast(I32), 0)
         nc.gpsimd.memset(kb_pool[0:ROW, 0:KB_SPLIT].bitcast(I32), 0)
         nc.gpsimd.memset(vs_pool[0:ROW, :].bitcast(I32), 0)
-        for h in range(2):
-            nc.gpsimd.memset(v_pool[1][h][:, stretch(0)].bitcast(I32), 0)
+        nc.gpsimd.memset(v_high[1][:, stretch(0)].bitcast(I32), 0)
 
         ks_listed = new_tile("ks_listed", [P, B * N], U8)
         for b in range(B):
@@ -140,11 +135,8 @@ def tile_attend_sigm_kb_segb2q128n512t2048_kernel(tc, q_words, q_scales, k_words
             nc.vector.tensor_copy(parted[:, half, :, :, places, :], paired[:, :, :, places, :])
 
         def scores(b):
-            if b == 0:
-                banks = [new_bank("scores0%d" % pair, [P, 2, NQ]) for pair in range(PLACES // 2)]
-                acc = [banks[place // 2][:, place % 2, :] for place in range(PLACES)]
-            else:
-                acc = [new_bank("scores1%d" % place, [P, NQ], row_banks[place])[:] for place in range(PLACES)]
+            banks = [new_bank("scores%d%d" % (b, pair), [P, 2, NQ]) for pair in range(PLACES // 2)]
+            acc = [banks[place // 2][:, place % 2, :] for place in range(PLACES)]
             for place in range(PLACES):
                 plane_cols = slice(N * b + place * P, N * b + (place + 1) * P)
                 for o in range(PASSES):
@@ -163,22 +155,20 @@ def tile_attend_sigm_kb_segb2q128n512t2048_kernel(tc, q_words, q_scales, k_words
             for place in range(PLACES):
                 nc.scalar.activation(prob[b][:, place, :], accs[b][place], ACT.Sigmoid, bias=cols[:, b, place : place + 1])
 
-        query_halves = [slice(0, NQ // 2), slice(NQ // 2, NQ)]
-
         def weigh(b):
-            for queries in query_halves:
-                nc.vector.tensor_tensor(
-                    w[b][:, PLACES * queries.start : PLACES * queries.stop].rearrange("p (c i t) -> p c t i", i=4, t=PLACES),
-                    prob[b][:, :, queries].rearrange("p t (c i) -> p c t i", i=4),
-                    cols[:, B + b, :].unsqueeze(1).unsqueeze(3).to_broadcast([P, NQ // 8, PLACES, 4]),
-                    mybir.AluOpType.mult,
-                )
+            nc.vector.tensor_tensor(
+                w[b][:].rearrange("p (c i t) -> p c t i", i=4, t=PLACES),
+                prob[b][:].rearrange("p t (c i) -> p c t i", i=4),
+                turned_rows[B + b].unsqueeze(1).to_broadcast([P, NQ // 4, PLACES, 4]),
+                mybir.AluOpType.mult,
+            )
 
-        def quantize_weights(b, queries):
-            quantize(w_mx[b], queries, w[b][:, PLACES * queries.start : PLACES * queries.stop])
+        def late_tile(name, shape, dtype, slot):
+            return placed.tile(shape, dtype, name=name, align_bytes=64, offset=slot * 4 * DV)
 
-        def mx_tiles(name, width, takes_over=None):
-            return new_tile(name + "_codes", [P, width], U32, takes_over), new_tile(name + "_scales", [P, width], U8)
+        def mx_tiles(name, width, slot=None):
+            codes = new_tile(name + "_codes", [P, width], U32) if slot is None else late_tile(name + "_codes", [P, width], U32, slot)
+            return codes, new_tile(name + "_scales", [P, width], U8)
 
         def quantize(mx, cols, grouped):
             nc.vector.quantize_mx(out=mx[0][:, cols].bitcast(FP8X4), scales=mx[1][:, cols], in_=grouped)
@@ -205,19 +195,16 @@ def tile_attend_sigm_kb_segb2q128n512t2048_kernel(tc, q_words, q_scales, k_words
 
         v_listed = [[new_tile("v_listed%d%d" % (b, h), [P, N], BF16) for h in range(2)] for b in range(B)]
 
-        load_values(0, 1)
-        load_values(1, 0)
-        load_values(1, 1)
+        for b in range(B):
+            nc.sync.dma_start(v_high[b][:, stretch(b)], vT[P:DV, stretch(b)])
         row_banks = ["kb_turned0", "kb_turned1", "vs_turned0", "vs_turned1"]
         rows = [gather_row("%s_listed%d" % (name, b), pool, b) for name, pool in (("kb", kb_pool), ("vs", vs_pool)) for b in range(B)]
         turned_rows = [turn_row(name, row) for name, row in zip(row_banks, rows)]
-        gather_values(nc.scalar, v_listed[0][0], 0, 0)
-        cols = new_tile("cols", [P, 2 * B, PLACES], F32, "v_pool00")
-        for j, turned in enumerate(turned_rows):
-            nc.scalar.copy(cols[:, j, :].unsqueeze(2), turned)
-        turned00 = turn_values("turned00", v_listed[0][0])
-        grouped00 = new_tile("grouped00", [P, P * PLACES], BF16)
-        group_values(grouped00[:], turned00)
+        for b in range(B):
+            gather_values(nc.scalar, v_listed[b][0], b, 0)
+        cols = new_tile("cols", [P, B, PLACES], F32, "v_low")
+        for b in range(B):
+            nc.scalar.copy(cols[:, b, :].unsqueeze(2), turned_rows[b])
 
         for b in range(B):
             kw_halves = gather_keys(b)
@@ -225,38 +212,27 @@ def tile_attend_sigm_kb_segb2q128n512t2048_kernel(tc, q_words, q_scales, k_words
                 for pair in range(2):
                     part_keys(b, kw_halves, half, pair)
         accs = [scores(b) for b in range(B)]
-        w_mx = [mx_tiles("w%d" % b, NQ) for b in range(B)]
-        v_mx1 = [mx_tiles("v1%d" % h, P) for h in range(2)]
         prob = [new_tile("prob%d" % b, [P, PLACES, NQ], F32) for b in range(B)]
         for b in range(B):
             sigmoid(b)
-        gather_values(nc.vector, v_listed[0][1], 0, 1)
-        v_mx0 = (placed.tile([P, DV], U32, name="v0_codes", align_bytes=64, offset=0), new_tile("v0_scales", [P, DV], U8))
-        w = [placed.tile([P, NQ * PLACES], BF16, name="w0", align_bytes=64, offset=4 * DV)]
-        quantize(v_mx0, slice(0, P), grouped00[:])
-        turned01 = turn_values("turned01", v_listed[0][1], "scores00")
-        weigh(0)
-        for queries in query_halves:
-            quantize_weights(0, queries)
-        gather_values(nc.vector, v_listed[1][0], 1, 0, 0, N // 2)
-        gather_values(nc.scalar, v_listed[1][0], 1, 0, N // 2, N // 2)
-        turned10 = turn_values("turned10", v_listed[1][0], "scores01")
-        gather_values(nc.vector, v_listed[1][1], 1, 1, 0, N // 2)
-        gather_values(nc.scalar, v_listed[1][1], 1, 1, N // 2, N // 2)
-        turned11 = turn_values("turned11", v_listed[1][1])
-        grouped_late = placed.tile([P, 2 * P * PLACES], BF16, name="grouped_late", align_bytes=64, offset=4 * SEG)
-        w.append(placed.tile([P, NQ * PLACES], BF16, name="w1", align_bytes=64, offset=4 * T))
-        grouped01, grouped10 = grouped_late[:, 0 : P * PLACES], grouped_late[:, P * PLACES :]
-        group_values(grouped01, turned01)
-        group_values(grouped10, turned10)
-        grouped11 = new_tile("grouped11", [P, P * PLACES], BF16)
-        group_values(grouped11[:], turned11)
-        weigh(1)
-        quantize(v_mx0, slice(P, DV), grouped01)
-        quantize_weights(1, query_halves[0])
-        quantize(v_mx1[0], slice(0, P), grouped10)
-        quantize_weights(1, query_halves[1])
-        quantize(v_mx1[1], slice(0, P), grouped11[:])
-        finish(0, w_mx[0], v_mx0, slice(0, DV), "turned00")
-        finish(1, w_mx[1], v_mx1[0], slice(0, P), row_banks[0], True)
-        finish(1, w_mx[1], v_mx1[1], slice(P, DV), row_banks[1])
+        for b in range(B):
+            gather_values(nc.vector, v_listed[b][1], b, 1)
+        grouped = [new_tile("grouped%d" % b, [P, 2, P * PLACES], BF16) for b in range(B)]
+        for b in range(B):
+            for h in range(2):
+                turned = turn_values("turned%d%d" % (b, h), v_listed[b][h], "scores%d%d" % (b, h))
+                group_values(grouped[b][:, h, :], turned)
+        w = [late_tile("w%d" % b, [P, NQ * PLACES], BF16, b) for b in range(B)]
+        w_mx = [mx_tiles("w%d" % b, NQ) for b in range(B)]
+        v_mx0 = mx_tiles("v0", DV, 2)
+        v_mx1 = [mx_tiles("v1%d" % h, P, 3 + h) for h in range(2)]
+        for b in range(B):
+            weigh(b)
+        quantize(w_mx[0], slice(0, NQ), w[0][:])
+        quantize(v_mx0, slice(0, DV), grouped[0][:].rearrange("p h x -> p (h x)"))
+        quantize(w_mx[1], slice(0, NQ), w[1][:])
+        for h in range(2):
+            quantize(v_mx1[h], slice(0, P), grouped[1][:, h, :])
+        finish(0, w_mx[0], v_mx0, slice(0, DV), row_banks[0])
+        finish(1, w_mx[1], v_mx1[0], slice(0, P), row_banks[1], True)
+        finish(1, w_mx[1], v_mx1[1], slice(P, DV), row_banks[2])

@@ -23,6 +23,7 @@ LIST_COLS = N // 16
 PASSES = D // (P * PLACES)
 KS_FIRST = P - PASSES * 16
 ROW = P - 1
+SCALAR_SHARE = N // 4
 KB_SPLIT = T // 4
 
 
@@ -52,7 +53,7 @@ def tile_attend_sigm_kb_segb2q128n512t2048_kernel(tc, q_words, q_scales, k_words
         vs_pool = new_tile("vs_pool", [P, T], F32)
         kw_pool = new_tile("kw_pool", [P, T], U32)
         v_low = new_tile("v_low", [P, T], F32)
-        v_high = [new_tile("v_high0", [P, SEG], F32), placed.tile([P, T], F32, name="v_high1", align_bytes=64, offset=0)]
+        v_high = [new_tile("v_high0", [P, SEG], F32), new_tile("v_high1", [P, T], F32)]
         v_pool = [[v_low, v_high[b]] for b in range(B)]
         kw_bytes = k_words[0].rearrange("p t c -> p (t c)")
 
@@ -159,15 +160,15 @@ def tile_attend_sigm_kb_segb2q128n512t2048_kernel(tc, q_words, q_scales, k_words
             nc.vector.tensor_tensor(
                 w[b][:].rearrange("p (c i t) -> p c t i", i=4, t=PLACES),
                 prob[b][:].rearrange("p t (c i) -> p c t i", i=4),
-                turned_rows[B + b].unsqueeze(1).to_broadcast([P, NQ // 4, PLACES, 4]),
+                vs_cols[b][:].unsqueeze(1).unsqueeze(3).to_broadcast([P, NQ // 4, PLACES, 4]),
                 mybir.AluOpType.mult,
             )
 
-        def late_tile(name, shape, dtype, slot):
-            return placed.tile(shape, dtype, name=name, align_bytes=64, offset=slot * 4 * DV)
-
-        def mx_tiles(name, width, slot=None):
-            codes = new_tile(name + "_codes", [P, width], U32) if slot is None else late_tile(name + "_codes", [P, width], U32, slot)
+        def mx_tiles(name, width, first=None):
+            if first is None:
+                codes = new_tile(name + "_codes", [P, width], U32)
+            else:
+                codes = placed.tile([P, width], U32, name=name + "_codes", align_bytes=64, offset=4 * first)
             return codes, new_tile(name + "_scales", [P, width], U8)
 
         def quantize(mx, cols, grouped):
@@ -197,37 +198,43 @@ def tile_attend_sigm_kb_segb2q128n512t2048_kernel(tc, q_words, q_scales, k_words
 
         for b in range(B):
             nc.sync.dma_start(v_high[b][:, stretch(b)], vT[P:DV, stretch(b)])
-        row_banks = ["kb_turned0", "kb_turned1", "vs_turned0", "vs_turned1"]
-        rows = [gather_row("%s_listed%d" % (name, b), pool, b) for name, pool in (("kb", kb_pool), ("vs", vs_pool)) for b in range(B)]
-        turned_rows = [turn_row(name, row) for name, row in zip(row_banks, rows)]
+        row_banks = ["kb_turned0", "kb_turned1"]
+        turned_rows = [turn_row(row_banks[b], gather_row("kb_listed%d" % b, kb_pool, b)) for b in range(B)]
+        vs_listed = new_tile("vs_listed", [P, B * N], F32)
+        nc.scalar.activation(vs_listed[:], listed(vs_pool[:], 0, B * N), ACT.Copy)
+        vs_cols = [new_tile("vs_cols%d" % b, [P, PLACES], F32) for b in range(B)]
+        for b in range(B):
+            nc.sync.dma_start(vs_cols[b][:], vs_listed[ROW:P, N * b : N * (b + 1)].rearrange("r (m t) -> r m t", t=PLACES))
         for b in range(B):
             gather_values(nc.scalar, v_listed[b][0], b, 0)
-        cols = new_tile("cols", [P, B, PLACES], F32, "v_low")
-        for b in range(B):
-            nc.scalar.copy(cols[:, b, :].unsqueeze(2), turned_rows[b])
 
         for b in range(B):
             kw_halves = gather_keys(b)
             for half in range(2):
                 for pair in range(2):
                     part_keys(b, kw_halves, half, pair)
+            if b == 0:
+                cols = new_tile("cols", [P, B, PLACES], F32, "kw_listed00")
+                for turned in range(B):
+                    nc.vector.tensor_copy(cols[:, turned, :].unsqueeze(2), turned_rows[turned])
         accs = [scores(b) for b in range(B)]
-        prob = [new_tile("prob%d" % b, [P, PLACES, NQ], F32) for b in range(B)]
-        for b in range(B):
-            sigmoid(b)
-        for b in range(B):
-            gather_values(nc.vector, v_listed[b][1], b, 1)
+        prob = [new_tile("prob0", [P, PLACES, NQ], F32), placed.tile([P, PLACES, NQ], F32, name="prob1", align_bytes=64, offset=0)]
+        sigmoid(0)
+        gather_values(nc.scalar, v_listed[0][1], 0, 1, N - SCALAR_SHARE, SCALAR_SHARE)
+        sigmoid(1)
+        gather_values(nc.vector, v_listed[0][1], 0, 1, 0, N - SCALAR_SHARE)
+        gather_values(nc.vector, v_listed[1][1], 1, 1)
         grouped = [new_tile("grouped%d" % b, [P, 2, P * PLACES], BF16) for b in range(B)]
         for b in range(B):
             for h in range(2):
                 turned = turn_values("turned%d%d" % (b, h), v_listed[b][h], "scores%d%d" % (b, h))
                 group_values(grouped[b][:, h, :], turned)
-        w = [late_tile("w%d" % b, [P, NQ * PLACES], BF16, b) for b in range(B)]
+        w = [new_tile("w%d" % b, [P, NQ * PLACES], BF16) for b in range(B)]
         w_mx = [mx_tiles("w%d" % b, NQ) for b in range(B)]
-        v_mx0 = mx_tiles("v0", DV, 2)
-        v_mx1 = [mx_tiles("v1%d" % h, P, 3 + h) for h in range(2)]
         for b in range(B):
             weigh(b)
+        v_mx0 = mx_tiles("v0", DV, 0)
+        v_mx1 = [mx_tiles("v1%d" % h, P, DV + P * h) for h in range(2)]
         quantize(w_mx[0], slice(0, NQ), w[0][:])
         quantize(v_mx0, slice(0, DV), grouped[0][:].rearrange("p h x -> p (h x)"))
         quantize(w_mx[1], slice(0, NQ), w[1][:])
@@ -235,4 +242,4 @@ def tile_attend_sigm_kb_segb2q128n512t2048_kernel(tc, q_words, q_scales, k_words
             quantize(v_mx1[h], slice(0, P), grouped[1][:, h, :])
         finish(0, w_mx[0], v_mx0, slice(0, DV), row_banks[0])
         finish(1, w_mx[1], v_mx1[0], slice(0, P), row_banks[1], True)
-        finish(1, w_mx[1], v_mx1[1], slice(P, DV), row_banks[2])
+        finish(1, w_mx[1], v_mx1[1], slice(P, DV), None)

@@ -23,8 +23,8 @@ LIST_COLS = N // 16
 PASSES = D // (P * PLACES)
 KS_FIRST = P - PASSES * 16
 ROW = P - 1
-SCALAR_SHARE = N // 4
 KB_SPLIT = T // 4
+SCALAR_SHARE = N // 4
 
 
 def tile_attend_sigm_kb_segb2q128n512t2048_kernel(tc, q_words, q_scales, k_words, k_scales, vT, vs, kb, offs, out):
@@ -53,22 +53,21 @@ def tile_attend_sigm_kb_segb2q128n512t2048_kernel(tc, q_words, q_scales, k_words
         vs_pool = new_tile("vs_pool", [P, T], F32)
         kw_pool = new_tile("kw_pool", [P, T], U32)
         v_low = new_tile("v_low", [P, T], F32)
-        v_high = [new_tile("v_high0", [P, SEG], F32), new_tile("v_high1", [P, T], F32)]
-        v_pool = [[v_low, v_high[b]] for b in range(B)]
         kw_bytes = k_words[0].rearrange("p t c -> p (t c)")
 
         nc.sync.dma_start(ks_pool[KS_FIRST:P, :].bitcast(I32), k_scales.rearrange("o f t -> f o t").bitcast(I32))
         nc.scalar.dma_start(kb_pool[ROW:P, :], kb[0:1, :])
         nc.sync.dma_start(offsets[:], offs)
+        scale_rows = new_tile("scale_rows", [P, B * N + PASSES * NQ], U8)
+        nc.sync.dma_start(
+            scale_rows[KS_FIRST:P, B * N :].rearrange("p (o q) -> p o q", o=PASSES).bitcast(I32),
+            q_scales.rearrange("b o f q -> f (b o) q").bitcast(I32),
+        )
         nc.sync.dma_start(vs_pool[ROW:P, :], vs[0:1, :])
         nc.sync.dma_start(kw_pool[:].bitcast(I32), kw_bytes.bitcast(I32))
-        q_planes = new_tile("q_planes", [P, B * PASSES, NQ], U8)
-        q_rows = q_scales.rearrange("b o f q -> f (b o) q")
-        for c in range(4):
-            nc.sync.dma_start(q_planes[32 * c : 32 * c + 4, :, :].bitcast(I32), q_rows[4 * c : 4 * c + 4].bitcast(I32))
-        nc.sync.dma_start(v_low[:], vT[0:P, :])
         q_codes = new_tile("q_codes", [P, B * PASSES, NQ], U32)
         nc.sync.dma_start(q_codes[:].bitcast(I32), q_words.rearrange("b o p q c -> p (b o) (q c)").bitcast(I32))
+        nc.sync.dma_start(v_low[:], vT[0:P, :])
 
         warm_in = new_tile("warm_in", [P, 1], F32)
         nc.gpsimd.memset(warm_in[:], 0.0)
@@ -81,17 +80,22 @@ def tile_attend_sigm_kb_segb2q128n512t2048_kernel(tc, q_words, q_scales, k_words
         nc.vector.memset(kb_pool[0:ROW, KB_SPLIT + 1 :].bitcast(I32), 0)
         nc.gpsimd.memset(kb_pool[0:ROW, 0:KB_SPLIT].bitcast(I32), 0)
         nc.gpsimd.memset(vs_pool[0:ROW, :].bitcast(I32), 0)
-        nc.gpsimd.memset(v_high[1][:, stretch(0)].bitcast(I32), 0)
 
-        ks_listed = new_tile("ks_listed", [P, B * N], U8)
+        ks_listed = [new_tile("ks_listed%d" % b, [P, N], U8) for b in range(B)]
+        for b in range(B):
+            nc.vector.tensor_copy(ks_listed[b][:], listed(ks_pool[:], N * b, N))
         for b in range(B):
             nc.vector.tensor_copy(
-                ks_listed[:, N * b : N * (b + 1)].rearrange("p (t m) -> p m t", t=PLACES), listed(ks_pool[:], N * b, N)
+                scale_rows[:, N * b : N * (b + 1)].rearrange("p (t m) -> p t m", t=PLACES),
+                ks_listed[b][:].rearrange("p (m t) -> p t m", t=PLACES),
             )
-        planes = new_tile("planes", [P, PASSES, B * N], U8)
+        v_high = [new_tile("v_high0", [P, SEG], F32), new_tile("v_high1", [P, T], F32, "ks_listed0")]
+        v_pool = [[v_low, v_high[b]] for b in range(B)]
+        nc.gpsimd.memset(v_high[1][:, stretch(0)].bitcast(I32), 0)
+        planes = new_tile("planes", [P, PASSES, B * N + PASSES * NQ], U8)
         for c in (0, 2, 1, 3):
             first = KS_FIRST + 8 * c
-            nc.sync.dma_start(planes[32 * c : 32 * c + 4, :, :].bitcast(I32), ks_listed[first : first + 8, :].bitcast(I32))
+            nc.sync.dma_start(planes[32 * c : 32 * c + 4, :, :].bitcast(I32), scale_rows[first : first + 8, :].bitcast(I32))
 
         def gather_row(name, pool, b):
             row = new_tile(name, [P, N], F32)
@@ -146,7 +150,7 @@ def tile_attend_sigm_kb_segb2q128n512t2048_kernel(tc, q_words, q_scales, k_words
                         lhsT=k_codes[b][:, place, o, :].bitcast(FP4X4),
                         lhsT_scale=planes[:, o, plane_cols],
                         rhs=q_codes[:, PASSES * b + o, :].bitcast(FP8X4),
-                        rhs_scale=q_planes[:, PASSES * b + o, :],
+                        rhs_scale=planes[:, b, B * N + NQ * o : B * N + NQ * (o + 1)],
                         start=(o == 0),
                         stop=(o == PASSES - 1),
                     )

@@ -24,7 +24,7 @@ PASSES = D // (P * PLACES)
 KS_FIRST = P - PASSES * 16
 ROW = P - 1
 KB_SPLIT = T // 4
-SCALAR_SHARE = N // 4
+SCALAR_SHARE = N // 2
 
 
 def tile_attend_sigm_kb_segb2q128n512t2048_kernel(tc, q_words, q_scales, k_words, k_scales, vT, vs, kb, offs, out):
@@ -127,17 +127,16 @@ def tile_attend_sigm_kb_segb2q128n512t2048_kernel(tc, q_words, q_scales, k_words
 
         k_codes = [new_tile("k_codes%d" % b, [P, PLACES, PASSES, P], U16) for b in range(B)]
 
-        def gather_keys(b):
-            halves = [new_tile("kw_listed%d%d" % (b, half), [P, N // 2], U32) for half in range(2)]
-            for half in range(2):
-                nc.vector.tensor_copy(halves[half][:], listed(kw_pool[:], N * b + half * N // 2, N // 2))
-            return halves
+        def gather_keys(b, half):
+            words = new_tile("kw_listed%d%d" % (b, half), [P, N // 2], U32)
+            nc.vector.tensor_copy(words[:], listed(kw_pool[:], N * b + half * N // 2, N // 2))
+            return words
 
-        def part_keys(b, halves, half, pair):
+        def part_keys(b, half, words):
             parted = k_codes[b][:].rearrange("p t o (h x y) -> p h o x t y", h=2, y=4)
-            paired = halves[half][:].bitcast(U16).rearrange("p (x y t o) -> p o x t y", t=PLACES, y=4, o=PASSES)
-            places = slice(2 * pair, 2 * pair + 2)
-            nc.vector.tensor_copy(parted[:, half, :, :, places, :], paired[:, :, :, places, :])
+            paired = words[:].bitcast(U16).rearrange("p (x y t o) -> p o x t y", t=PLACES, y=4, o=PASSES)
+            for places in (slice(0, 2), slice(2, 4)):
+                nc.vector.tensor_copy(parted[:, half, :, :, places, :], paired[:, :, :, places, :])
 
         def scores(b):
             banks = [new_bank("scores%d%d" % (b, pair), [P, 2, NQ]) for pair in range(PLACES // 2)]
@@ -212,15 +211,15 @@ def tile_attend_sigm_kb_segb2q128n512t2048_kernel(tc, q_words, q_scales, k_words
         for b in range(B):
             gather_values(nc.scalar, v_listed[b][0], b, 0)
 
+        kw_listed = [gather_keys(0, 0), gather_keys(0, 1), gather_keys(1, 0)]
+        for half in range(2):
+            part_keys(0, half, kw_listed[half])
+        cols = new_tile("cols", [P, B, PLACES], F32, "kw_listed00")
         for b in range(B):
-            kw_halves = gather_keys(b)
-            for half in range(2):
-                for pair in range(2):
-                    part_keys(b, kw_halves, half, pair)
-            if b == 0:
-                cols = new_tile("cols", [P, B, PLACES], F32, "kw_listed00")
-                for turned in range(B):
-                    nc.vector.tensor_copy(cols[:, turned, :].unsqueeze(2), turned_rows[turned])
+            nc.vector.tensor_copy(cols[:, b, :].unsqueeze(2), turned_rows[b])
+        kw_listed.append(gather_keys(1, 1))
+        for half in range(2):
+            part_keys(1, half, kw_listed[2 + half])
         accs = [scores(b) for b in range(B)]
         prob = [new_tile("prob0", [P, PLACES, NQ], F32), placed.tile([P, PLACES, NQ], F32, name="prob1", align_bytes=64, offset=0)]
         sigmoid(0)

from contextlib import ExitStack

import concourse.mybir as mybir
from concourse.masks import make_identity

B, N, T, D, DV, NQ = 2, 512, 2048, 1024, 256, 128
FLOPS = 2 * B * NQ * N * (D + DV)

F32 = mybir.dt.float32
BF16 = mybir.dt.bfloat16
I32 = mybir.dt.int32
U32 = mybir.dt.uint32
U16 = mybir.dt.uint16
U8 = mybir.dt.uint8
FP8X4 = mybir.dt.float8_e4m3fn_x4
FP4X4 = mybir.dt.float4_e2m1fn_x4
ACT = mybir.ActivationFunctionType

P = 128
PLACES = 4
SEG = T // B
LIST_COLS = N // 16
PASSES = D // (P * PLACES)
KS_FIRST = P - PASSES * 16
ROW = P - 1
KB_SPLIT = T // 4
SCALAR_SHARE = N // 2


def tile_attend_sigm_kb_segb2q128n512t2048_kernel(tc, q_words, q_scales, k_words, k_scales, vT, vs, kb, offs, out):
    nc = tc.nc
    with ExitStack() as ctx:
        sbuf = ctx.enter_context(tc.tile_pool(name="sbuf", bufs=1))
        placed = ctx.enter_context(tc.tile_pool(name="placed", bufs=1))
        psum = ctx.enter_context(tc.psum_pool(name="psum", bufs=1))

        def new_tile(name, shape, dtype, takes_over=None):
            return sbuf.tile(shape, dtype, name=name, tag=takes_over or name, align_bytes=64)

        def new_bank(name, shape, takes_over=None):
            return psum.tile(shape, F32, name=name, tag=takes_over or name)

        def stretch(b):
            return slice(SEG * b, SEG * (b + 1))

        offsets = sbuf.tile([P, B * LIST_COLS], U16, name="offsets")

        def listed(window, first, count):
            return window.indirect(offsets[:, first // 16 : (first + count) // 16])

        ks_pool = new_tile("ks_pool", [P, T], U8)
        kb_pool = new_tile("kb_pool", [P, T], F32)
        vs_pool = new_tile("vs_pool", [P, T], F32)
        kw_pool = new_tile("kw_pool", [P, T], U32)
        v_low = new_tile("v_low", [P, T], F32)
        kw_bytes = k_words[0].rearrange("p t c -> p (t c)")

        nc.sync.dma_start(ks_pool[KS_FIRST:P, :].bitcast(I32), k_scales.rearrange("o f t -> f o t").bitcast(I32))
        nc.scalar.dma_start(kb_pool[ROW:P, :], kb[0:1, :])
        nc.sync.dma_start(offsets[:], offs)
        scale_rows = new_tile("scale_rows", [P, B * N + PASSES * NQ], U8)
        nc.sync.dma_start(
            scale_rows[KS_FIRST:P, B * N :].rearrange("p (o q) -> p o q", o=PASSES).bitcast(I32),
            q_scales.rearrange("b o f q -> f (b o) q").bitcast(I32),
        )
        nc.sync.dma_start(vs_pool[ROW:P, :], vs[0:1, :])
        nc.sync.dma_start(kw_pool[:].bitcast(I32), kw_bytes.bitcast(I32))
        q_codes = new_tile("q_codes", [P, B * PASSES, NQ], U32)
        nc.sync.dma_start(q_codes[:].bitcast(I32), q_words.rearrange("b o p q c -> p (b o) (q c)").bitcast(I32))
        nc.sync.dma_start(v_low[:], vT[0:P, :])

        warm_in = new_tile("warm_in", [P, 1], F32)
        nc.gpsimd.memset(warm_in[:], 0.0)
        warm_out = new_tile("warm_out", [P, 1], F32)
        nc.scalar.activation(warm_out[:], warm_in[:], ACT.Sigmoid)
        identity = new_tile("identity", [P, P], F32)
        make_identity(nc, identity[:])
        nc.gpsimd.memset(ks_pool[0:KS_FIRST, :].bitcast(I32), 0)
        nc.vector.memset(kb_pool[0:ROW, KB_SPLIT : KB_SPLIT + 1].bitcast(I32), 0)
        nc.vector.memset(kb_pool[0:ROW, KB_SPLIT + 1 :].bitcast(I32), 0)
        nc.gpsimd.memset(kb_pool[0:ROW, 0:KB_SPLIT].bitcast(I32), 0)
        nc.gpsimd.memset(vs_pool[0:ROW, :].bitcast(I32), 0)

        ks_listed = [new_tile("ks_listed%d" % b, [P, N], U8) for b in range(B)]
        for b in range(B):
            nc.vector.tensor_copy(ks_listed[b][:], listed(ks_pool[:], N * b, N))
        for b in range(B):
            nc.vector.tensor_copy(
                scale_rows[:, N * b : N * (b + 1)].rearrange("p (t m) -> p t m", t=PLACES),
                ks_listed[b][:].rearrange("p (m t) -> p t m", t=PLACES),
            )
        v_high = [new_tile("v_high0", [P, SEG], F32), new_tile("v_high1", [P, T], F32, "ks_listed0")]
        v_pool = [[v_low, v_high[b]] for b in range(B)]
        nc.gpsimd.memset(v_high[1][:, stretch(0)].bitcast(I32), 0)
        planes = new_tile("planes", [P, PASSES, B * N + PASSES * NQ], U8)
        for c in (0, 2, 1, 3):
            first = KS_FIRST + 8 * c
            nc.sync.dma_start(planes[32 * c : 32 * c + 4, :, :].bitcast(I32), scale_rows[first : first + 8, :].bitcast(I32))

        def gather_row(name, pool, b):
            row = new_tile(name, [P, N], F32)
            nc.scalar.activation(row[:], listed(pool[:], N * b, N), ACT.Copy)
            return row

        def gather_values(engine, v_listed, b, h, first=0, count=N):
            window = listed(v_pool[b][h][:], N * b + first, count)
            if engine is nc.scalar:
                nc.scalar.activation(v_listed[:, first : first + count], window, ACT.Copy)
            else:
                nc.vector.tensor_copy(v_listed[:, first : first + count], window)

        def turn_values(name, v_listed, takes_over=None):
            bank = new_bank(name, [P, 2, P], takes_over)
            words = v_listed[:].bitcast(F32)
            for u in range(2):
                nc.tensor.transpose(bank[:, u, :], words[:, u : N // 2 : 2], identity[:])
            return bank

        def turn_row(name, row):
            bank = new_bank(name, [P, PLACES, P])
            for place in range(PLACES):
                nc.tensor.transpose(bank[:, place, :], row[:, place:N:PLACES], identity[:])
            return bank[:, :, ROW:P]

        def group_values(grouped, bank):
            nc.scalar.copy(grouped.bitcast(F32).rearrange("p (f u) -> p f u", u=2), bank[:].rearrange("p u f -> p f u"))

        k_codes = [new_tile("k_codes%d" % b, [P, PLACES, PASSES, P], U16) for b in range(B)]

        def gather_keys(b, half):
            words = new_tile("kw_listed%d%d" % (b, half), [P, N // 2], U32)
            nc.vector.tensor_copy(words[:], listed(kw_pool[:], N * b + half * N // 2, N // 2))
            return words

        def part_keys(b, half, words):
            parted = k_codes[b][:].rearrange("p t o (h x y) -> p h o x t y", h=2, y=4)
            paired = words[:].bitcast(U16).rearrange("p (x y t o) -> p o x t y", t=PLACES, y=4, o=PASSES)
            for places in (slice(0, 2), slice(2, 4)):
                nc.vector.tensor_copy(parted[:, half, :, :, places, :], paired[:, :, :, places, :])

        def scores(b):
            banks = [new_bank("scores%d%d" % (b, pair), [P, 2, NQ]) for pair in range(PLACES // 2)]
            acc = [banks[place // 2][:, place % 2, :] for place in range(PLACES)]
            for place in range(PLACES):
                plane_cols = slice(N * b + place * P, N * b + (place + 1) * P)
                for o in range(PASSES):
                    nc.tensor.matmul_mx(
                        out=acc[place],
                        lhsT=k_codes[b][:, place, o, :].bitcast(FP4X4),
                        lhsT_scale=planes[:, o, plane_cols],
                        rhs=q_codes[:, PASSES * b + o, :].bitcast(FP8X4),
                        rhs_scale=planes[:, b, B * N + NQ * o : B * N + NQ * (o + 1)],
                        start=(o == 0),
                        stop=(o == PASSES - 1),
                    )
            return acc

        def sigmoid(b):
            for place in range(PLACES):
                nc.scalar.activation(prob[b][:, place, :], accs[b][place], ACT.Sigmoid, bias=cols[:, b, place : place + 1])

        def weigh(b):
            nc.vector.tensor_tensor(
                w[b][:].rearrange("p (c i t) -> p c t i", i=4, t=PLACES),
                prob[b][:].rearrange("p t (c i) -> p c t i", i=4),
                vs_cols[b][:].unsqueeze(1).unsqueeze(3).to_broadcast([P, NQ // 4, PLACES, 4]),
                mybir.AluOpType.mult,
            )

        def mx_tiles(name, width, first=None):
            if first is None:
                codes = new_tile(name + "_codes", [P, width], U32)
            else:
                codes = placed.tile([P, width], U32, name=name + "_codes", align_bytes=64, offset=4 * first)
            return codes, new_tile(name + "_scales", [P, width], U8)

        def quantize(mx, cols, grouped):
            nc.vector.quantize_mx(out=mx[0][:, cols].bitcast(FP8X4), scales=mx[1][:, cols], in_=grouped)

        def finish(b, w_mx, v_mx, cols, bank, on_vector=False):
            width = cols.stop - cols.start
            acc = new_bank("y_acc%d_%d" % (b, cols.start), [P, width], bank)
            nc.tensor.matmul_mx(
                out=acc[:],
                lhsT=w_mx[0][:].bitcast(FP8X4),
                lhsT_scale=w_mx[1][:],
                rhs=v_mx[0][:].bitcast(FP8X4),
                rhs_scale=v_mx[1][:],
                start=True,
                stop=True,
            )
            y = new_tile("y%d_%d" % (b, cols.start), [P, width], F32)
            if on_vector:
                nc.vector.tensor_scalar_mul(y[:], acc[:], 1.0 / 16.0)
                nc.sync.dma_start(out[b][:, cols], y[:])
            else:
                nc.scalar.activation(y[:], acc[:], ACT.Copy, scale=1.0 / 16.0)
                (nc.scalar if b else nc.sync).dma_start(out[b][:, cols], y[:])

        v_listed = [[new_tile("v_listed%d%d" % (b, h), [P, N], BF16) for h in range(2)] for b in range(B)]

        for b in range(B):
            nc.sync.dma_start(v_high[b][:, stretch(b)], vT[P:DV, stretch(b)])
        row_banks = ["kb_turned0", "kb_turned1"]
        turned_rows = [turn_row(row_banks[b], gather_row("kb_listed%d" % b, kb_pool, b)) for b in range(B)]
        vs_listed = new_tile("vs_listed", [P, B * N], F32)
        nc.scalar.activation(vs_listed[:], listed(vs_pool[:], 0, B * N), ACT.Copy)
        vs_cols = [new_tile("vs_cols%d" % b, [P, PLACES], F32) for b in range(B)]
        for b in range(B):
            nc.sync.dma_start(vs_cols[b][:], vs_listed[ROW:P, N * b : N * (b + 1)].rearrange("r (m t) -> r m t", t=PLACES))
        for b in range(B):
            gather_values(nc.scalar, v_listed[b][0], b, 0)

        kw_listed = [gather_keys(0, 0), gather_keys(0, 1), gather_keys(1, 0)]
        for half in range(2):
            part_keys(0, half, kw_listed[half])
        cols = new_tile("cols", [P, B, PLACES], F32, "kw_listed00")
        for b in range(B):
            nc.vector.tensor_copy(cols[:, b, :].unsqueeze(2), turned_rows[b])
        kw_listed.append(gather_keys(1, 1))
        for half in range(2):
            part_keys(1, half, kw_listed[2 + half])
        accs = [scores(b) for b in range(B)]
        prob = [new_tile("prob0", [P, PLACES, NQ], F32), placed.tile([P, PLACES, NQ], F32, name="prob1", align_bytes=64, offset=0)]
        sigmoid(0)
        gather_values(nc.scalar, v_listed[0][1], 0, 1, N - SCALAR_SHARE, SCALAR_SHARE)
        sigmoid(1)
        gather_values(nc.vector, v_listed[0][1], 0, 1, 0, N - SCALAR_SHARE)
        gather_values(nc.vector, v_listed[1][1], 1, 1)
        grouped = [new_tile("grouped%d" % b, [P, 2, P * PLACES], BF16) for b in range(B)]
        for b in range(B):
            for h in range(2):
                turned = turn_values("turned%d%d" % (b, h), v_listed[b][h], "scores%d%d" % (b, h))
                group_values(grouped[b][:, h, :], turned)
        w = [new_tile("w%d" % b, [P, NQ * PLACES], BF16) for b in range(B)]
        w_mx = [mx_tiles("w%d" % b, NQ) for b in range(B)]
        for b in range(B):
            weigh(b)
        v_mx0 = mx_tiles("v0", DV, 0)
        v_mx1 = [mx_tiles("v1%d" % h, P, DV + P * h) for h in range(2)]
        quantize(w_mx[0], slice(0, NQ), w[0][:])
        quantize(v_mx0, slice(0, DV), grouped[0][:].rearrange("p h x -> p (h x)"))
        quantize(w_mx[1], slice(0, NQ), w[1][:])
        for h in range(2):
            quantize(v_mx1[h], slice(0, P), grouped[1][:, h, :])
        finish(0, w_mx[0], v_mx0, slice(0, DV), row_banks[0])
        finish(1, w_mx[1], v_mx1[0], slice(0, P), row_banks[1], True)
        finish(1, w_mx[1], v_mx1[1], slice(P, DV), None)
